import numpy as np, ml_dtypes
CORES = [5,29,101,125,133,157,229,253]
N = 8
BF = ml_dtypes.bfloat16
def f(rng, *shape):
    return (rng.standard_normal(shape, dtype=np.float32) * np.exp2(rng.integers(-2, 3, shape[:-1] + (1,)))).astype(BF)
def wide(rng, *shape):
    v = f(rng, *shape).astype(np.float32); k = shape[:-2] + (1, shape[-1])
    return (v * np.exp2(rng.integers(-6, 7, k)) * (rng.random(k) > 0.0625)).astype(BF)
def gentries(a):
    return np.ascontiguousarray(a.reshape(8, 16, -1).transpose(0, 2, 1)).reshape(8, -1)
def gtable(e):
    e = np.asarray(e); return np.ascontiguousarray(e.reshape(8, -1, 16).transpose(0, 2, 1)).reshape(128, -1).astype(np.int32)
B, PI, C, F, NEED, R = 128, 16, 8, 3072, 10, 3
def faces(rng):
    v = rng.standard_normal((N, 8, 16, F), dtype=np.float32) + rng.standard_normal((N, 8, 1, F), dtype=np.float32)
    return (v * np.exp2(rng.integers(-2, 3, (N, 8, 16, 1)))).astype(BF).reshape(N, 128, F)
def parts(rng):
    return rng.integers(0, C + 1, (N, 8, PI, B)), rng.integers(0, F, (N, 8, C, PI, B)), rng.integers(0, PI, (N, 8, B))
def pack(x, c, kinds, p):
    s = np.where(np.arange(C)[:, None, None] < c[:, :, None], kinds, F)
    return {"x": x, "sd": np.stack([gtable(a.reshape(8, -1)) for a in s]), "act": np.stack([gtable(a) for a in p])}
def setup_inputs(rng):
    c, kinds, p = parts(rng)
    return pack(faces(rng), c, kinds, p)
def setup_inputs_full(rng):
    c, kinds, p = parts(rng)
    c = C - rng.choice(np.array([0, 0, 0, 1, 1, 2]), (N, 8, PI, B))
    c[:, 1:3] = C - 1; p[:, 1] = rng.integers(0, PI); p[:, 2] = rng.integers(0, PI, (N, 1)); kinds[:, 2] = rng.integers(0, F)
    n = np.take_along_axis(c, p[:, :, None, :], 2); n[..., ::2] = C; n[:, 1:3] = C
    np.put_along_axis(c, p[:, :, None, :], n, 2); c[0, 0] = C
    return pack(faces(rng), c, kinds, p)
def setup_inputs_ties(rng):
    c, kinds, p = parts(rng)
    cl = rng.choice(np.array([-1] * 7 + [0, 16 - NEED, 17 - NEED, NEED - 1, NEED, NEED + 1, 16]), (N, 8, 1, F))
    o = np.argsort(rng.random((N, 8, 16)), axis=2)[..., None]
    v = np.where(cl < 0, 1.0, np.where(o < cl, 2.0, 0.0))
    z = v[:, 1::4] - 1.0
    v[:, 1::4] = np.where(z == 0, rng.choice(np.array([0.0, -0.0]), (N, 2, 1, F)), z)
    e = rng.integers(-3, 4, (N, 8, 16, 1)); e[:, 3] = 59
    v = v * np.exp2(e)
    v[:, 2::4] = v[:, 2::4] * np.exp2(rng.choice(np.array([-57.0, 50.0]), (N, 2, 1, F)))
    c = 2 * rng.integers(0, C // 2 + 1, (N, 8, PI, B))
    return pack(v.astype(BF).reshape(N, 128, F), c, kinds, p)
def setup_inputs_sparse(rng):
    c, kinds, p = parts(rng)
    c = np.where(rng.random((N, 8, PI, B)) < 0.2, rng.integers(1, C + 1, (N, 8, PI, B)), 0)
    n = np.where(rng.random((N, 8, 1, B)) < 0.5, rng.integers(1, C + 1, (N, 8, 1, B)), 0)
    q = rng.permutation(N); n[q[0]] = 0; n[q[1]] = 1
    h = rng.permutation(8); n[:, h[1]] = 0
    np.put_along_axis(c, p[:, :, None, :], n, 2); c[:, h[0]] = 0
    return pack(faces(rng), c, kinds, p)
def setup_inputs_ends(rng):
    c, kinds, p = parts(rng); few = np.array([0, F - 1, 1, F - 2, F // 2])
    p = (PI - 1) * rng.integers(0, 2, (N, 8, B))
    kinds[:, ::2] = rng.choice(few, (N, 4, C, PI, B)); kinds[:, 0] = rng.choice(few, (1, 1, 1, B))
    return pack(faces(rng), c, kinds, p)
def setup_inputs_spread(rng):
    c, kinds, p = parts(rng)
    c = np.minimum(((C + 1) * rng.random((N, 8, PI, B)) ** np.exp2(rng.integers(-2, 3, (N, 8, 1, B)))).astype(np.int64), C)
    kinds = np.minimum((F * rng.random((N, 8, C, PI, B)) ** 3).astype(np.int64), F - 1)
    v = wide(rng, N, 128, F).astype(np.float32).reshape(N, 8, 16, F); v[:, 1::2] *= np.float32(2.0 ** 44)
    return pack(v.reshape(N, 128, F).astype(BF), c, kinds, p)
def check_inputs(d):
    bad = []
    v = np.abs(np.asarray(d["x"]).astype(np.float32))
    if not np.all((v == 0) | ((v >= 2.0 ** -60) & (v <= 2.0 ** 60))): bad.append("size of x")
    if np.min(d["sd"]) < 0 or np.max(d["sd"]) > F: bad.append("range of sd")
    if np.min(d["act"]) < 0 or np.max(d["act"]) > PI - 1: bad.append("range of act")
    s = np.stack([gentries(a) for a in d["sd"]]).reshape(N, 8, C, PI, B)
    if np.any((s[:, :, :-1] == F) & (s[:, :, 1:] != F)): bad.append("a seed above an empty slot")
    return bad
def reference(x, sd, act):
    s = np.stack([gentries(a) for a in sd]).astype(np.int64).reshape(N, 8, C, PI, B)
    p = np.stack([gentries(a) for a in act]).astype(np.int64)
    xf = np.concatenate([x.astype(np.float32).reshape(N, 8, 16, F), np.zeros((N, 8, 16, 1), np.float32)], axis=3)
    pits = np.arange(PI)[:, None]; slots = np.arange(C)[:, None, None]; score = np.zeros((N, 8, B), np.int64)
    for rnd in range(R):
        c = np.add.reduce((s != F).astype(np.int64), axis=2)
        up = np.take_along_axis(s, p[:, :, None, None, :], 3)[:, :, :, 0]
        n = np.take_along_axis(c, p[:, :, None, :], 2)[:, :, 0]
        own = pits == p[:, :, None, :]
        s = np.where(own[:, :, None], F, s); c = np.where(own, 0, c)
        up, p, n = np.roll(up, 1, axis=0), np.roll(p, 1, axis=0), np.roll(n, 1, axis=0)
        k = (pits - p[:, :, None, :] - 1) & (PI - 1)
        here = k < n[:, :, None, :]
        a = np.where(here, np.take_along_axis(up, np.minimum(k, C - 1), 2), F)
        w = np.zeros((N, 8, PI, B), np.int64)
        for r in range(N):
            fa = np.take_along_axis(xf[r], a[r].reshape(8, 1, PI * B), 2)
            for j in range(C):
                fs = np.take_along_axis(xf[r], s[r, :, j].reshape(8, 1, PI * B), 2)
                beat = np.add.reduce((fa > fs).astype(np.int64), axis=1) >= NEED
                w[r] += beat.reshape(8, PI, B) & (s[r, :, j] != F)
        cap = here & ((2 * w > c) | (c == C))
        score = score + np.add.reduce(np.where(cap, c, 0), axis=2)
        at = np.where(cap, 0, c)
        s = np.where(cap[:, :, None], F, s)
        s = np.where(here[:, :, None] & (slots == at[:, :, None]), a[:, :, None], s)
        last = (p + n) & (PI - 1)
        p = np.where(np.take_along_axis(cap, last[:, :, None, :], 2)[:, :, 0], PI - 1 - last, last)
    return {"ys": np.stack([gtable(v.reshape(8, -1)) for v in s]).astype(np.float32),
            "yp": np.stack([gtable(v) for v in p]).astype(np.float32), "yc": np.stack([gtable(v) for v in score]).astype(np.float32)}

@@ -1,0 +1,691 @@
+import numpy as np
+from concourse.mybir import AluOpType, ActivationFunctionType
+
+A = AluOpType
+AF = ActivationFunctionType
+F, E8 = 3072, 8192
+MW = 80
+NENG = 8
+WAKE, TRIP, GC, PE = 80.0, 5000.0, (1.25, 1.9), 0.52
+MOVES, TEMP, SEED = 30000, 60.0, 1
+
+LISTS = [("ROT", 64), ("ZB", 8), ("YZ", 8), ("SB", 8), ("LO", 32), ("HI", 32), ("BB", 32), ("DUP", 32),
+         ("YL", 16), ("CB", 6), ("PS", 8), ("NAT", 8), ("NATD", 8), ("FB", 32), ("UN", 64)]
+LOFF = {}
+_o = 0
+for _n, _k in LISTS:
+    LOFF[_n] = _o
+    _o += _k
+LTOT = _o
+COLS = ["ib", "il", "i", "h", "z", "gb", "il128", "il904", "il8p", "il8", "il64", "il960", "il1920", "sgb", "ib15",
+        "sw", "i15", "sgz", "z71", "bp", "gb128", "ngb128"]
+SCALED = [("nib", -1.0), ("ih", 0.5), ("n75", -7.5), ("n8", -8.0), ("i16b", 16.0), ("i8k", 8192.0), ("n32k", -32768.0)]
+
+f32, bf, i32, u16 = "float32", "bfloat16", "int32", "uint16"
+SB_ = {
+    "xw": (3088, bf), "sdi": (1024, i32), "acti": (8, i32), "S": (1024, f32), "S1": (1024, f32), "SC": (1024, f32), "TT": (2048, f32),
+    "lf": (LTOT, f32), "lu": (LTOT, u16), "pi": (8, i32), "ibits": (8, i32), "col": (32, f32),
+    "c64": (8, f32), "c4": (32, f32), "c8": (64, f32), "s8": (64, f32), "s4": (32, f32), "au": (64, f32), "az": (64, f32),
+    "dd": (144, f32), "qt": (64, f32), "t8": (64, f32), "ti": (64, i32), "ti2": (64, i32), "tj": (32, i32), "tj2": (32, i32),
+    "tf": (64, f32), "tf2": (64, f32), "tf3": (64, f32), "tf4": (64, f32), "idf": (8, f32),
+    "idm": (128 * 9, bf), "mwl": (512, f32), "if32": (128, f32), "nf32": (128, f32), "psw": (128, f32), "bm": (144, bf), "bm3": (144, bf),
+    "ct2": (128, f32), "ckey": (128, f32), "cr": (192, bf), "crn": (64, bf), "cm": (64, bf), "c10": (64, bf), "cpit": (128, f32),
+    "ones": (240, f32), "one": (512, bf), "rst8": (240, f32),
+    "pp": (16, f32), "uu": (8, f32), "zm": (128, f32), "oft": (8, u16), "xg": (128, f32), "yb": (160, f32), "ym": (128, f32),
+    "mf": (MW, f32), "t2": (128, i32), "hl8": (128, i32), "hlb": (128, bf), "fs": (512, f32), "w8": (512, f32), "off": (448, u16),
+    "hi1": (512, f32), "lo1": (512, f32), "fa": (1024, bf), "gb0": (1024, bf), "gb1": (1024, bf),
+    "cmp": (7168, bf), "sig": (384, bf), "val": (512, bf),
+    "nh": (64, bf), "sl": (8, bf), "ct": (64, bf), "cabs": (64, f32), "st": (64, bf), "key": (128, f32),
+    "om": (128, f32), "code_": (192, f32), "pa": (240, f32), "cs3": (240, f32), "ea": (240, f32),
+    "app": (240, f32), "ed": (160, f32), "tl": (64, f32), "cap": (64, f32), "prod": (128, f32), "cs2": (128, f32),
+    "r1": (MW, f32), "r2": (MW, f32), "r3": (MW, f32), "r4": (MW, f32),
+    "vw1": (64, f32), "vw": (64, f32), "vq": (128, f32), "ncl": (128, f32), "vq2": (128, f32), "kq": (128, f32), "ce0": (128, bf),
+    "cape": (128, f32), "sct": (64, f32), "sc": (64, f32), "scs": (64, f32),
+    "hn1": (128, f32), "hn3": (128, f32), "aq": (128, f32), "ins": (1024, f32), "yo": (1024, f32), "rr": (128, f32),
+    "o8": (16, f32), "w8s": (16, f32),
+    "msg0": (MW, u16), "msg1": (MW, u16), "msg2": (MW, u16), "in0": (MW, u16), "in1": (MW, u16), "in2": (MW, u16),
+}
+ALIAS = {"ib16": ("idm", 0), "i3k": ("idm", 128), "m00": ("mwl", 0), "m01": ("mwl", 128), "m10": ("mwl", 256), "m11": ("mwl", 384)}
+for _k, (_n, _v) in enumerate(SCALED):
+    ALIAS[_n] = ("idm", 128 * (_k + 2))
+PS_ = {"pd": 1024, "pa_": 512, "pb_": 512, "pc_": 512, "pt_": 512, "pl_": 512, "pm_": 512}
+SCRATCH = {}
+for _n, (_k, _d) in SB_.items():
+    SCRATCH[_n] = ("sbuf", [128, _k], _d)
+for _n, _k in PS_.items():
+    SCRATCH[_n] = ("psum", [128, _k], "float32")
+SEMAPHORES = ["ev", "es", "et", "eg", "sent", "arr0", "arr1", "arr2"] + ["dm%d" % k for k in range(8)]
+_PLAN = {}
+
+
+def _relay(src, dst, topo):
+    if topo.may_write(src, dst):
+        return None
+    ok = [c for c in topo.cores_of(src) if c != src and topo.may_write(c, dst)]
+    near = [c for c in ok if topo.die(c) == topo.die(src)]
+    return (near or ok)[0]
+
+
+def _mask(src, dst, topo):
+    m = 0
+    for e in topo.engines(src, dst)[:NENG]:
+        m |= 1 << e
+    return m
+
+
+def _conflict(ra, rb):
+    for (n, lo, hi, st) in ra:
+        for (n2, lo2, hi2, st2) in rb:
+            if n == n2 and lo < hi2 and lo2 < hi and not (st == st2 and (lo - lo2) % st):
+                return True
+    return False
+
+
+def _order(ops, deps):
+    n = len(ops)
+    reach = []
+    red = []
+    for k in range(n):
+        m = 0
+        keep = []
+        for j in sorted(set(deps[k]), reverse=True):
+            if not m >> j & 1:
+                keep.append(j)
+                m |= reach[j] | 1 << j
+        reach.append(m)
+        red.append(keep)
+    succ = [[] for _ in range(n)]
+    for k in range(n):
+        for j in red[k]:
+            succ[j].append(k)
+    qi = ["vstgyx".index(o["q"]) for o in ops]
+    c0 = [o["c"][0] for o in ops]
+    c1 = [o["c"][1] for o in ops]
+    lat = [o["lat"] + WAKE for o in ops]
+
+    def span(order):
+        f0 = [0.0] * 6
+        f1 = [0.0] * 6
+        d0 = [0.0] * n
+        d1 = [0.0] * n
+        for k in order:
+            q = qi[k]
+            a = f0[q]
+            b = f1[q]
+            for j in red[k]:
+                if d0[j] > a:
+                    a = d0[j]
+                if d1[j] > b:
+                    b = d1[j]
+            a += c0[k]
+            b += c1[k]
+            f0[q] = a
+            f1[q] = b
+            d0[k] = a + lat[k]
+            d1[k] = b + lat[k]
+        return max(d0) + max(d1) + 1e-4 * (sum(d0) + sum(d1))
+
+    rng = np.random.default_rng(SEED)
+    order = list(range(n))
+    cur = best = span(order)
+    keep = list(order)
+    for it in range(MOVES):
+        i = int(rng.integers(n))
+        k = order[i]
+        step = int(rng.integers(1, 40))
+        j = i
+        if rng.random() < 0.5:
+            pre = set(red[k])
+            while j > 0 and i - j < step and order[j - 1] not in pre:
+                j -= 1
+            if not any(qi[x] == qi[k] for x in order[j:i]):
+                continue
+        else:
+            post = set(succ[k])
+            while j < n - 1 and j - i < step and order[j + 1] not in post:
+                j += 1
+            if not any(qi[x] == qi[k] for x in order[i + 1:j + 1]):
+                continue
+        order.insert(j, order.pop(i))
+        s = span(order)
+        if s <= cur + TEMP * (1.0 - it / MOVES) * rng.exponential():
+            cur = s
+            if s < best:
+                best = s
+                keep = list(order)
+        else:
+            order.insert(i, order.pop(j))
+    return keep
+
+
+def _emit(g, T, ops):
+    Q = {"v": g.vector, "s": g.scalar, "t": g.tensor, "g": g, "y": g.sync}
+    if "deps" not in _PLAN:
+        deps = []
+        for k, o in enumerate(ops):
+            d = list(o["after"])
+            for j in range(k):
+                p = ops[j]
+                c = _conflict(p["w"], o["r"]) or _conflict(p["w"], o["w"]) or _conflict(p["r"], o["w"])
+                if not c and (p["q"] != o["q"] or p["open"] or o["open"]):
+                    c = _conflict(p["b"], o["b"])
+                if c:
+                    d.append(j)
+            deps.append(d)
+        _PLAN["deps"] = deps
+        _PLAN["order"] = _order(ops, deps)
+    deps, order = _PLAN["deps"], _PLAN["order"]
+    cnt = {"v": 0, "s": 0, "t": 0, "g": 0}
+    tok = {}
+    for k in order:
+        o = ops[k]
+        if o["sem"] is not None:
+            tok[k] = (o["sem"], o["n"])
+        else:
+            cnt[o["q"]] += 1
+            tok[k] = ("e" + o["q"], cnt[o["q"]])
+    known = {q: {} for q in Q}
+    clock = {}
+    last = {}
+    for k in order:
+        o = ops[k]
+        q = o["q"]
+        if q == "x":
+            clock[k] = {tok[k][0]: tok[k][1]}
+            continue
+        want = {}
+        src = {}
+        for j in deps[k]:
+            if q == "t" and ops[j]["q"] == "t":
+                continue
+            s, n = tok[j]
+            if n > want.get(s, 0):
+                want[s] = n
+                src[s] = j
+        for s in sorted(want, key=lambda s: -len(clock[src[s]])):
+            if known[q].get(s, 0) < want[s]:
+                Q[q].wait_ge(T.sem[s], want[s])
+                for s2, n2 in clock[src[s]].items():
+                    if known[q].get(s2, 0) < n2:
+                        known[q][s2] = n2
+        ins = o["f"](Q[q])
+        c = dict(known[q])
+        if not o["own"]:
+            ins.then_inc(T.sem[tok[k][0]], 16 if o["sem"] is not None else 1)
+        c[tok[k][0]] = tok[k][1]
+        last[tok[k][0]] = max(last.get(tok[k][0], 0), tok[k][1])
+        clock[k] = c
+    for s, n in last.items():
+        if max(known[q].get(s, 0) for q in Q) < n:
+            g.wait_ge(T.sem[s], n)
+
+
+def rank_program(g, core, T, topo):
+    cores = list(T.cores)
+    N = len(cores)
+    rank = T.rank_of(core)
+    if rank is None:
+        for r in range(N):
+            src, dst = cores[r], cores[(r + 1) % N]
+            if _relay(src, dst, topo) == core:
+                rid, pid = topo.addr(dst, core)
+                for t in range(3):
+                    g.wait_ge(T.sem["arr%d" % t], NENG)
+                    g.remote_dma(T["in%d" % t][:], T["in%d" % t][:], T.sem["arr%d" % t], T.sem.sent, pid, rid, _mask(core, dst, topo))
+                g.wait_ge(T.sem.sent, 3 * NENG)
+        return
+    nxt = cores[(rank + 1) % N]
+    hop = _relay(core, nxt, topo)
+    hop = nxt if hop is None else hop
+    rid, pid = topo.addr(hop, core)
+    hmask = _mask(core, hop, topo)
+
+    ops = []
+    ndma = [0]
+    sends = {}
+
+    def ap(name, lo=0, hi=None, step=1):
+        if name in ALIAS:
+            name, lo = ALIAS[name]
+            hi = lo + 128
+        w = SB_[name][0] if name in SB_ else PS_[name]
+        hi = w if hi is None else hi
+        real = T[name][:, lo:hi] if step == 1 else T[name][:, lo:hi:step]
+        banks = [(name, b, b + 1, 1) for b in range(lo // 512, (hi - 1) // 512 + 1)] if name in PS_ else []
+        return (real, [(name, lo, hi, step)], banks, len(range(lo, hi, step)), "p" if name in PS_ else SB_[name][1])
+
+    def ind(win, offs):
+        return (win[0].indirect(offs[0]), win[1] + offs[1], [], 16 * offs[3], "ind")
+
+    def lst(name, k0=0, k1=None):
+        k1 = dict(LISTS)[name] if k1 is None else k1
+        return ap("lu", LOFF[name] + k0, LOFF[name] + k1)
+
+    def lfl(name, k0=0, k1=None):
+        k1 = dict(LISTS)[name] if k1 is None else k1
+        return ap("lf", LOFF[name] + k0, LOFF[name] + k1)
+
+    def col(name):
+        k = COLS.index(name)
+        return ap("col", k, k + 1)
+
+    def rec(q, f, outs, ins, sem=None, n=0, own=False, after=(), c=None, lat=0.0, two=False, open_=False):
+        r, w, b = [], [], []
+        for a in ins:
+            if isinstance(a, tuple):
+                r += a[1]
+                b += a[2]
+        for a in outs:
+            w += a[1]
+            b += a[2]
+        if c is None:
+            a = ins[0] if ins else outs[0]
+            per = 2.0 if (two and "p" not in (a[4], ins[1][4])) or q == "g" else 1.0
+            c = [{"v": 50.0, "s": 65.0, "g": 130.0}[q] + max(64.0, a[3] * (x if a[4] == "ind" else per)) * 1.04 for x in GC]
+        else:
+            c = [c, c]
+        ops.append({"q": q, "f": f, "r": r, "w": w, "b": b, "sem": sem, "n": n, "own": own, "after": list(after), "c": c, "lat": lat,
+                    "open": open_})
+        return len(ops) - 1
+
+    def raw(a):
+        return a[0] if isinstance(a, tuple) else a
+
+    def tt(o, a, b, op):
+        return rec("v", lambda e: e.tensor_tensor(o[0], a[0], b[0], op), [o], [a, b], two=True)
+
+    def ts(o, a, s1, op0, s2=None, op1=None):
+        if op1 is None:
+            return rec("v", lambda e: e.tensor_scalar(o[0], a[0], raw(s1), None, op0), [o], [a, s1])
+        return rec("v", lambda e: e.tensor_scalar(o[0], a[0], raw(s1), raw(s2), op0, op1), [o], [a, s1, s2])
+
+    def cp(o, a):
+        return rec("v", lambda e: e.tensor_copy(o[0], a[0]), [o], [a])
+
+    def ms(o, c):
+        return rec("v", lambda e: e.memset(o[0], c), [o], [])
+
+    def scan(o, d0, d1):
+        return rec("v", lambda e: e.tensor_tensor_scan(o[0], d0[0], d1[0], 0.0, A.mult, A.add), [o], [d0, d1])
+
+    def tr(o, a):
+        return rec("v", lambda e: e.transpose(o[0], a[0]), [o], [a])
+
+    def act(o, a, fn=AF.Identity, scale=1.0, bias=0.0):
+        return rec("s", lambda e: e.activation(o[0], a[0], fn, bias=raw(bias), scale=raw(scale)), [o], [a, scale, bias])
+
+    def mms(items):
+        def f(e):
+            for (o, l, r, start, stop) in items:
+                ins = e.matmul(o[0], l[0], r[0], start, stop)
+            return ins
+        c = sum(max(64, r[3]) * (4 if r[4] == f32 else 1) * PE for (o, l, r, start, stop) in items)
+        return rec("t", f, [x[0] for x in items], [x[1] for x in items] + [x[2] for x in items], c=c,
+                   open_=not (items[0][3] and items[-1][4]))
+
+    def mm(o, l, r, start, stop):
+        return mms([(o, l, r, start, stop)])
+
+    def group(o, terms, start=True, stop=True):
+        return mms([(o, l, r, start and k == 0, stop and k == len(terms) - 1) for k, (l, r) in enumerate(terms)])
+
+    def iota(o, pat, base, ch=0):
+        if SB_[o[1][0][0]][1] == i32:
+            return rec("g", lambda e: e.iota(o[0], pat, base, ch), [o], [])
+        return rec("g", lambda e: e.iota(o[0], pat, base, ch, allow_small_or_imprecise_dtypes=True), [o], [])
+
+    def dma(q, o, a, after=()):
+        s = "dm%d" % ndma[0]
+        ndma[0] += 1
+        return rec(q, lambda e: e.dma_start(o[0], a[0]), [o], [a], sem=s, n=16, after=after, c=100.0,
+                   lat=2000.0 + 2.56 * max(o[3], a[3]))
+
+    def hbm(t):
+        return (t, [], [], 0, "hbm")
+
+    def send(t):
+        m = ap("msg%d" % t)
+        sends[t] = rec("g", lambda e: e.remote_dma(T["in%d" % t][:], m[0], T.sem["arr%d" % t], T.sem.sent, pid, rid, hmask), [], [m],
+                       sem="sent", n=NENG * (t + 1), own=True, c=300.0, lat=TRIP)
+
+    def arrive(t):
+        rec("x", None, [ap("in%d" % t)], [], sem="arr%d" % t, n=NENG, c=0.0, after=[sends[t]])
+
+    dma("s", ap("acti"), hbm(T.act[:]))
+    d_sd = dma("y", ap("sdi"), hbm(T.sd[:]))
+    dma("y", ap("xw", 0, F), hbm(T.x[:]), after=[d_sd])
+
+    iota(ap("pi", 0, 1), [[0, 1]], 0, 1)
+    iota(ap("s8"), [[1, 8], [0, 8]], 0)
+    iota(ap("c8"), [[0, 8], [1, 8]], 0)
+    iota(ap("c4"), [[0, 8], [1, 4]], 0)
+    iota(ap("dd"), [[1, 144]], 0, -1)
+    iota(ap("c64"), [[1, 8]], 0)
+    iota(ap("s4"), [[1, 8], [0, 4]], 1)
+    iota(ap("cpit", 0, 128, 2), [[-1, 8], [0, 8]], 15)
+    iota(ap("cpit", 1, 128, 2), [[1, 8], [0, 8]], 0)
+    iota(ap("au"), [[1, 8], [2, 8]], 1)
+    iota(ap("az"), [[0, 8], [8, 2], [0, 4]], 0)
+    iota(ap("ct2"), [[-8, 2], [0, 8], [1, 8]], 8)
+    iota(ap("ckey", 0, 64), [[0, 8], [-1, 8]], 7)
+    iota(ap("ckey", 64, 128), [[0, 8], [1, 8]], 0)
+    iota(ap("ones"), [[0, 240]], 1)
+    rec("g", lambda e: e.affine_select(T["rst8"][:], T["ones"][:], [[0, 30], [1, 8]], A.is_gt, 0.0, 0, 0), [ap("rst8")], [ap("ones")])
+    p = ap("pi", 0, 1)
+    for k, (sh, m) in enumerate([(3, 1), (0, 7), (0, 15), (1, 7), (0, 1), (4, 1)]):
+        ts(ap("ibits", k, k + 1), p, sh, A.logical_shift_right, m, A.bitwise_and)
+    cp(ap("col", 0, 6), ap("ibits", 0, 6))
+    ts(col("il1920"), col("il"), 128.0, A.mult, 1920.0, A.add)
+    ts(col("gb128"), col("gb"), 128.0, A.mult)
+    ts(col("ngb128"), col("gb"), -128.0, A.mult, 128.0, A.add)
+    act(col("sgb"), col("ib"), scale=-2.0, bias=1.0)
+    act(col("ib15"), col("ib"), scale=15.0)
+    act(col("il8p"), col("il"), bias=8.0)
+    act(ap("qt"), ap("s8"), scale=col("sgb"), bias=col("ib15"))
+    act(lfl("BB"), ap("c4"), scale=2.0, bias=col("ib"))
+    act(ap("tf"), ap("qt"), scale=8.0)
+    act(lfl("ZB", 0, 4), lfl("BB", 0, 4))
+    act(lfl("ZB", 4, 8), lfl("BB", 0, 4), bias=8.0)
+    act(lfl("YZ", 0, 4), lfl("BB", 0, 4), scale=16.0, bias=col("il"))
+    act(lfl("YZ", 4, 8), lfl("BB", 0, 4), scale=16.0, bias=col("il8p"))
+    act(ap("idf"), ap("c64"), scale=16.0, bias=col("i"))
+    act(lfl("SB"), ap("c64"), scale=0.0, bias=col("h"))
+    ts(ap("ib16"), ap("dd", 0, 128), 0.0, A.is_equal)
+    act(ap("if32"), ap("ib16"))
+    ts(ap("ti"), ap("qt"), -128.0, A.mult, col("il1920"), A.add)
+    ts(ap("m00"), ap("dd", 0, 128), 0.0, A.is_equal, col("ngb128"), A.mult)
+    ts(ap("ti2"), ap("ti"), 896, A.bitwise_and)
+    tt(ap("tf2"), ap("tf"), ap("c8"), A.add)
+    ts(ap("m01"), ap("dd", 0, 128), 16.0, A.is_equal, col("ngb128"), A.mult)
+    tt(lfl("ROT"), ap("tf2"), ap("ti2"), A.add)
+    ts(ap("m10"), ap("dd", 0, 128), -16.0, A.is_equal, col("gb128"), A.mult)
+    ts(ap("m11"), ap("dd", 0, 128), 0.0, A.is_equal, col("gb128"), A.mult)
+    cp(ap("lu", 0, LOFF["LO"]), ap("lf", 0, LOFF["LO"]))
+    act(ap("i3k"), ap("ib16"), scale=float(F))
+    act(ap("nf32"), ap("ib16"), scale=-1.0)
+    for n, s, sc_, b in [("il128", "il", 128.0, 0.0), ("il904", "il", -128.0, 904.0), ("sw", "ib", -16.0, 8.0), ("i15", "i", -1.0, 15.0),
+                         ("il8", "il", 8.0, 0.0), ("il64", "il", 8.0, 64.0), ("il960", "il", 16.0, 960.0),
+                         ("sgz", "z", -2.0, 1.0), ("z71", "z", 71.0, 0.0)]:
+        act(col(n), col(s), scale=sc_, bias=b)
+    act(lfl("LO"), lfl("BB"), scale=16.0, bias=col("il128"))
+    act(lfl("HI"), lfl("BB"), scale=16.0, bias=col("il904"))
+
+    def wl_offsets(nm, lo):
+        for gp in range(2):
+            group(ap("pm_", gp, 8, 2), [(ap("m%d0" % gp), ap(nm, lo, lo + 8, 2)), (ap("m%d1" % gp), ap(nm, lo + 1, lo + 8, 2)),
+                                        (ap("if32"), ap("idf", gp, 8, 2))])
+
+    def preload(plus):
+        for h in range(2):
+            mm(ap("pd", 512 * h, 512 * h + 512), ap("if32"), ap("S", 512 * h, 512 * h + 512), True, False)
+            if plus:
+                mm(ap("pd", 512 * h, 512 * h + 512), ap("i3k"), ap("one"), False, False)
+
+    def clear():
+        for h in range(2):
+            mms([(ap("pd", 512 * h + pos, 512 * h + 512, 8), ap("i3k"), ap("ce0", 64 * h, 64 * h + 64), False, pos == 7)
+                 for pos in range(8)])
+
+    def refresh(last):
+        act(ap("lo1"), ind(ap("S"), lst("LO")))
+        if last:
+            ts(ap("SC"), ap("S"), float(F), A.min)
+        else:
+            tr(ap("TT", 0, 1024), ap("S"))
+        mm(ap("pl_"), ap("if32"), ap("lo1"), True, False)
+        act(ap("hi1"), ind(ap("S"), lst("HI")))
+        if not last:
+            for u in range(8):
+                mm(ap("pd", 128 * (7 - u), 128 * (8 - u)), ap("psw"), ap("TT", 128 * u, 128 * u + 128), True, True)
+
+    cp(ap("pp", 0, 8), ap("acti"))
+    ts(ap("pp", 8, 16), ap("acti"), -1.0, A.mult, 15.0, A.add)
+    ms(ap("msg0"), 0)
+    tt(ap("uu"), ap("pp", 0, 8), ap("pp", 8, 16), A.min)
+    ts(ap("zm"), ind(ap("pp"), lst("ZB")), 8.0, A.is_ge, float(F), A.mult)
+    wl_offsets("uu", 0)
+    cp(ap("msg0", 64, 72), ap("pp", 8, 16))
+    tt(ap("ce0"), ind(ap("pp", 8, 16), lst("SB")), ap("cpit"), A.is_equal)
+    cp(ap("oft"), ap("pm_", 0, 8))
+    cp(ap("S"), ind(ap("sdi"), lst("ROT")))
+    preload(False)
+    clear()
+    tr(ap("TT", 0, 1024), ap("S"))
+    cp(ap("xg"), ind(ap("TT", 0, 1024), ap("oft")))
+    ts(ap("tj"), ap("s4"), col("il"), A.add)
+    tr(ap("yb", 0, 128), ap("xg"))
+    ts(ap("tj2"), ap("tj"), 7, A.bitwise_and)
+    tt(ap("ym"), ind(ap("yb", 0, 128), lst("YZ")), ap("zm"), A.max)
+    tt(lfl("LO"), lfl("LO"), ap("tj2"), A.add)
+    tt(ap("r2", 0, 64), ap("ym", 0, 64), ap("ym", 64, 128), A.min)
+    tt(lfl("HI"), lfl("HI"), ap("tj2"), A.add)
+    cp(ap("msg0", 0, 64), ap("r2", 0, 64))
+    send(0)
+    iota(ap("cm"), [[0, 8], [1, 8]], 0)
+    iota(ap("c10"), [[0, 64]], 10)
+    iota(ap("cr", 0, 64), [[0, 8], [E8, 8]], -2 * E8)
+    iota(ap("cr", 64, 128), [[0, 8], [E8, 8]], 2 * E8)
+    iota(ap("cr", 71, 128, 8), [[0, 8]], E8)
+    iota(ap("cr", 128, 192), [[0, 64]], -4 * E8)
+    iota(ap("cr", 135, 192, 8), [[0, 8]], 4 * E8)
+    iota(ap("yb", 144, 160), [[0, 16]], F)
+    iota(ap("pa"), [[0, 240]], 0)
+    iota(ap("crn"), [[0, 64]], E8)
+    iota(ap("one"), [[0, 512]], 1)
+
+    act(lfl("DUP"), lfl("BB"), scale=8.0, bias=col("il"))
+    act(lfl("YL", 0, 4), lfl("BB", 0, 4), scale=0.0, bias=144.0)
+    act(lfl("YL", 4, 5), col("il"), bias=136.0)
+    act(lfl("YL", 5, 9), lfl("YZ", 4, 8))
+    act(lfl("YL", 9, 10), col("il"), bias=136.0)
+    act(lfl("YL", 10, 14), lfl("YZ", 0, 4))
+    act(lfl("YL", 14, 15), col("il"), bias=128.0)
+    act(lfl("YL", 15, 16), col("il"), bias=128.0)
+    act(lfl("CB", 0, 4), lfl("BB", 0, 4), scale=8.0, bias=7.0)
+    act(lfl("CB", 4, 5), col("il"), scale=8.0, bias=7.0)
+    act(lfl("CB", 5, 6), col("il"), scale=8.0, bias=7.0)
+    act(col("bp"), col("h"), scale=8.0, bias=col("z71"))
+    act(lfl("NAT", 0, 4), lfl("BB", 0, 4), bias=col("il8"))
+    act(lfl("NAT", 4, 8), lfl("BB", 0, 4), bias=col("il64"))
+    act(lfl("PS"), ap("c64"), scale=col("sgz"), bias=col("bp"))
+    act(lfl("NATD"), lfl("BB", 0, 8), bias=col("il8"))
+    act(ap("t8"), ap("c8"), scale=2.0, bias=col("ib"))
+    act(lfl("FB"), ap("c8", 0, 32), scale=16.0, bias=col("i"))
+    act(ap("tf3"), ap("t8"), AF.Abs, scale=128.0, bias=-960.0)
+    for n, v in SCALED[:2]:
+        act(ap(n), ap("ib16"), scale=v)
+    act(ap("tf4"), ap("tf3"), scale=-1.0, bias=col("il960"))
+    for n, v in SCALED[2:]:
+        act(ap(n), ap("ib16"), scale=v)
+
+    cp(ap("lu", LOFF["LO"], LOFF["BB"]), ap("lf", LOFF["LO"], LOFF["BB"]))
+    cp(ap("S"), ap("pd"))
+    ts(ap("psw"), ap("dd", 0, 128), col("sw"), A.is_equal)
+    refresh(False)
+    ts(ap("ti"), ap("au"), col("ib"), A.add)
+    tt(ap("tf2"), ap("tf4"), ap("az"), A.add)
+    ts(ap("ti2"), ap("ti"), 7, A.bitwise_and)
+    ms(ap("xw", F, F + 16), 2.0 ** 61)
+    tt(lfl("UN"), ap("tf2"), ap("ti2"), A.add)
+    ts(ap("bm"), ap("dd"), col("i15"), A.is_equal)
+    cp(ap("lu", LOFF["BB"], LTOT), ap("lf", LOFF["BB"], LTOT))
+    ts(ap("bm3"), ap("dd"), col("i15"), A.is_equal, 3.0, A.mult)
+
+    xw = ap("xw")
+
+    def slot_a(s):
+        tt(ap("cmp", 1024 * s, 1024 * s + 1024), ind(xw, ap("off", 64 * s, 64 * s + 64)), ap("fa"), A.is_lt)
+
+    def gath_b(k):
+        act(ap("gb%d" % k), ind(xw, ap("off", 64 * (5 + k), 64 * (6 + k))))
+
+    def diff_b(k, h):
+        group(ap("pd", 512 * h, 512 * h + 512), [(ap("ib16"), ap("fa", 512 * h, 512 * h + 512)),
+                                                 (ap("nib"), ap("gb%d" % k, 512 * h, 512 * h + 512))])
+
+    def sign_b(k, h):
+        lo = 1024 * (5 + k) + 512 * h
+        act(ap("cmp", lo, lo + 512), ap("pd", 512 * h, 512 * h + 512), AF.Sign, bias=-2.0 ** -70)
+
+    def rows(out, lo, hi, b):
+        group(out, [(ap(b, 15 - i, 143 - i), ap("cmp", lo + i, hi, 16)) for i in range(16)])
+
+    def thr(k0, n, src):
+        act(ap("sig", 64 * k0, 64 * (k0 + n)), src, AF.Sign, bias=-9.5)
+
+    def acc(k0, n, stop=False):
+        for k in range(k0, k0 + n):
+            mm(ap("pt_", 0, 64), ap("nib"), ap("sig", 64 * k, 64 * k + 64), False, stop)
+
+    for t in range(3):
+        last = t == 2
+        m = "in%d" % t
+        arrive(t)
+        act(ap("fa"), ind(xw, ap(m, 0, 64)))
+        cp(ap("mf"), ap(m))
+        tt(ap("t2"), ind(ap("mf", 64, 72), lst("BB", 0, 8)), ap("ct2"), A.add)
+        ts(ap("hl8"), ap("t2"), 8, A.bitwise_and)
+        ts(ap("hlb"), ap("hl8"), 512.0, A.mult)
+        mms([(ap("pl_", 64 * s, 64 * s + 64), ap("ib16"), ap("hlb", 64, 128), False, s == 7) for s in range(8)])
+        tt(ap("fs"), ind(ap("hlb", 0, 64), lst("DUP")), ap("hi1"), A.add)
+        tt(ap("w8"), ap("fs"), ap("pl_"), A.min)
+        ts(ap("off"), ap("w8", 0, 448), float(F), A.min)
+        act(ap("nh"), ap("mf", 0, 64), AF.Sign, bias=0.5 - F)
+        lsum = [(ap("if32"), ap("mf", 64, 72))] + [(ap("ih"), ap("nh", k, 64, 8)) for k in range(8)]
+        group(ap("pc_", 128, 136), lsum)
+        if not last:
+            act(ap("TT", 1024, 1536), ap("pd", 0, 512))
+        act(ap("sl"), ap("pc_", 128, 136), AF.Sign, bias=-3.5)
+        group(ap("pc_", 136, 144), lsum + [(ap("n8"), ap("sl"))])
+        if not last:
+            act(ap("TT", 1536, 2048), ap("pd", 512, 1024))
+        act(ap("val"), ap("w8"), AF.Sign, scale=-1.0, bias=F - 0.5)
+        cnt = [(ap("ih" if s < 7 else "n75"), ap("val", 64 * s, 64 * s + 64)) for s in range(8)]
+        group(ap("pb_", 256, 320), cnt)
+        if not last:
+            group(ap("pb_", 320, 384), cnt + [(ap("ib16"), ap("cm"))])
+        act(ap("yb", 136, 144), ap("pc_", 136, 144), scale=-1.0, bias=11.0)
+        act(ap("yb", 128, 136), ap("pc_", 136, 144), bias=4.0)
+        if not last:
+            wl_offsets("yb", 136)
+        slot_a(0)
+        act(ap("ct"), ap("pb_", 256, 320), bias=-4.0)
+        if not last:
+            act(ap("st"), ap("pb_", 320, 384), AF.Sign, bias=-10.5)
+            tail = [(ap("i8k"), ap("ct")), (ap("n32k"), ap("st"))]
+            group(ap("pa_", 256, 320), [(ap("ib16"), ap("cr", 0, 64)), (ap("if32"), ap("mf", 0, 64))] + tail)
+            group(ap("pa_", 320, 384), [(ap("ib16"), ap("cr", 64, 128)), (ap("if32"), ap("mf", 0, 64))])
+            group(ap("pa_", 384, 448), [(ap("ib16"), ap("cr", 128, 192))] + tail)
+        else:
+            group(ap("pa_", 256, 320), [(ap("ib16"), ap("crn")), (ap("if32"), ap("mf", 0, 64)), (ap("i8k"), ap("ct"))])
+        act(ap("cabs"), ap("pb_", 256, 320), AF.Abs, bias=-4.0)
+        gath_b(0)
+        group(ap("pt_", 0, 64), [(ap("ib16"), ap("ct")), (ap("i16b"), ap("nh")), (ap("ib16"), ap("c10"))], stop=False)
+        diff_b(0, 0)
+        diff_b(0, 1)
+        tt(ap("key"), ap("hl8"), ap("ckey"), A.add)
+        if not last:
+            act(ap("code_"), ap("pa_", 256, 448))
+            cp(ap("oft"), ap("pm_", 0, 8))
+            tt(ap("om"), ind(ap("yb", 128, 136), lst("BB", 0, 8)), ap("key"), A.is_equal)
+            act(ap("xg"), ind(ap("TT"), ap("oft")))
+        else:
+            act(ap("code_", 0, 64), ap("pa_", 256, 320))
+            ts(ap("hn1"), ind(ap("hl8"), lst("NAT")), 0.125, A.mult)
+            tt(ap("om", 0, 64), ind(ap("yb", 128, 136), lst("BB", 0, 4)), ap("key", 0, 64), A.is_equal)
+        gath_b(1)
+        slot_a(1)
+        if last:
+            tt(ap("vq"), ind(ap("code_", 0, 64), lst("NATD")), ap("hn1"), A.mult)
+        sign_b(0, 0)
+        sign_b(0, 1)
+        diff_b(1, 0)
+        diff_b(1, 1)
+        rows(ap("pa_", 0, 128), 0, 2048, "bm")
+        if not last:
+            tt(ap("pa", 0, 64), ap("code_", 64, 128), ap("om", 64, 128), A.mult)
+            tt(ap("pa", 80, 144), ap("code_", 0, 64), ap("om", 64, 128), A.mult)
+            tt(ap("pa", 160, 224), ap("code_", 0, 64), ap("om", 0, 64), A.mult)
+            tr(ap("yb", 0, 128), ap("xg"))
+            scan(ap("cs3"), ap("rst8"), ap("pa"))
+        else:
+            for s in range(8):
+                act(ap("ins", 128 * s, 128 * s + 128), ap("vq"), AF.Abs, bias=-float(E8 * (s + 1)))
+        sign_b(1, 0)
+        sign_b(1, 1)
+        thr(0, 2, ap("pa_", 0, 128))
+        slot_a(2)
+        if last:
+            tt(ap("S1"), ind(ap("SC"), lst("UN")), ap("ins"), A.min)
+        rows(ap("pb_", 0, 128), 5120, 7168, "bm3")
+        acc(0, 2)
+        if not last:
+            for pos in range(8):
+                act(ap("ea", pos, 240, 8), ap("cs3", 7, 240, 8), AF.Abs, bias=-float(E8 * (pos + 1)))
+        rows(ap("pa_", 128, 192), 2048, 3072, "bm")
+        thr(4, 2, ap("pb_", 0, 128))
+        thr(2, 1, ap("pa_", 128, 192))
+        slot_a(3)
+        acc(4, 2)
+        acc(2, 1)
+        rows(ap("pb_", 128, 192), 3072, 4096, "bm")
+        thr(3, 1, ap("pb_", 128, 192))
+        slot_a(4)
+        rows(ap("pc_", 0, 64), 4096, 5120, "bm")
+        acc(3, 1, True)
+        if not last:
+            tt(ap("app"), ind(ap("yb"), lst("YL", 0, 15)), ap("ea"), A.min)
+            group(ap("pm_", 256, 416), [(ap("if32"), ap("app", 0, 160)), (ap("nf32"), ap("app", 80, 240))])
+            act(ap("ed"), ap("pm_", 256, 416))
+            preload(True)
+        else:
+            ts(ap("aq"), ind(ap("mf", 0, 64), lst("NATD")), float(F), A.add)
+            ts(ap("hn3"), ap("hn1"), float(F), A.mult)
+            tt(ap("w8s", 0, 8), ap("yb", 128, 136), ap("yb", 136, 144), A.subtract)
+        ts(ap("tl"), ap("pc_", 0, 64), 9.5, A.is_ge, 2.0, A.mult)
+        tt(ap("cap"), ap("tl"), ap("pt_", 0, 64), A.is_gt)
+        if not last:
+            tt(ap("prod"), ind(ap("cap"), lst("DUP", 0, 8)), ap("om"), A.mult)
+            scan(ap("cs2"), ap("rst8", 0, 128), ap("prod"))
+            tt(ap("r1"), ind(ap("cs2", 64, 128), lst("CB", 0, 5)), ap("ed", 0, 80), A.mult)
+            tt(ap("r2"), ap("r1"), ap("ed", 80, 160), A.add)
+            tt(ap("r3"), ind(ap("cs2", 0, 64), lst("CB", 0, 5)), ap("r2"), A.mult)
+            tt(ap("r4"), ap("r3"), ap("app", 160, 240), A.add)
+            ts(ap("msg%d" % (t + 1)), ap("r4"), float(F), A.min)
+            send(t + 1)
+            tt(ap("vw1"), ap("cap"), ap("code_", 128, 192), A.mult)
+            tt(ap("ncl"), ind(ap("r4", 64, 72), lst("SB")), ap("cpit"), A.not_equal)
+            tt(ap("vw"), ap("code_", 0, 64), ap("vw1"), A.subtract)
+            tt(ap("kq"), ind(ap("cap"), lst("DUP", 0, 8)), ap("hl8"), A.mult)
+            tt(ap("vq"), ind(ap("vw"), lst("DUP", 0, 8)), ap("hl8"), A.mult)
+            tt(ap("vq2"), ind(ap("vq"), lst("PS")), ap("ncl"), A.mult)
+            tt(ap("ce0"), ind(ap("kq"), lst("PS")), ap("ncl"), A.subtract)
+            for pos in range(8):
+                act(ap("ins", pos, 1024, 8), ap("vq2"), AF.Abs, scale=0.125, bias=-float(E8 * (pos + 1)))
+            clear()
+            if t == 0:
+                tt(ap("sc"), ap("cap"), ap("cabs"), A.mult)
+            else:
+                tt(ap("sct"), ap("cap"), ap("cabs"), A.mult)
+                tt(ap("sc"), ap("sc"), ap("sct"), A.add)
+            tt(ap("S"), ap("ins"), ap("pd"), A.min)
+            refresh(t == 1)
+        else:
+            tt(ap("cape"), ind(ap("cap"), lst("NATD")), ap("hn3"), A.mult)
+            tt(ap("yo", 512, 1024), ind(ap("cape"), lst("FB")), ap("S1", 512, 1024), A.max)
+            dma("y", hbm(T.ys[:, 512:1024]), ap("yo", 512, 1024))
+            tt(ap("rr"), ap("aq"), ap("cape"), A.subtract)
+            tt(ap("yo", 0, 512), ind(ap("cape"), lst("FB")), ap("S1", 0, 512), A.max)
+            tt(ap("prod", 0, 64), ap("cap"), ap("om", 0, 64), A.mult)
+            tt(ap("yo", 0, 128), ap("yo", 0, 128), ap("rr"), A.min)
+            dma("s", hbm(T.ys[:, 0:512]), ap("yo", 0, 512))
+            tt(ap("sct"), ap("cap"), ap("cabs"), A.mult)
+            scan(ap("cs2", 0, 64), ap("rst8", 0, 64), ap("prod", 0, 64))
+            tt(ap("sc"), ap("sc"), ap("sct"), A.add)
+            tt(ap("w8s", 8, 16), ap("w8s", 0, 8), ap("cs2", 7, 64, 8), A.mult)
+            scan(ap("scs"), ap("rst8", 0, 64), ap("sc"))
+            tt(ap("o8", 0, 8), ap("w8s", 8, 16), ap("yb", 136, 144), A.add)
+            dma("s", hbm(T.yp[:]), ap("o8", 0, 8))
+            cp(ap("o8", 8, 16), ap("scs", 7, 64, 8))
+            dma("y", hbm(T.yc[:]), ap("o8", 8, 16))
+    _emit(g, T, ops)

@@ -5,45 +5,47 @@ A = AluOpType
 AF = ActivationFunctionType
 F, E8 = 3072, 8192
 MW = 80
-NENG = 8
-WAKE, TRIP, GC, PE = 80.0, 5000.0, (1.25, 1.9), 0.52
-MOVES, TEMP, SEED = 30000, 60.0, 1
+MSGS = [("p", "0", 64, MW), ("0", "0", 0, 64), ("q", "1", 64, MW), ("1", "1", 0, 64), ("r", "2", 64, MW), ("2", "2", 0, 64)]
+WAKE, TRIP, PE = 110.0, 6000.0, 0.5
+GC = ((1.3, 0.9), (1.85, 1.15))
+MOVES, TEMP, SEED = 130000, 200.0, 4
 
-LISTS = [("ROT", 64), ("ZB", 8), ("YZ", 8), ("SB", 8), ("LO", 32), ("HI", 32), ("BB", 32), ("DUP", 32),
-         ("YL", 16), ("CB", 6), ("PS", 8), ("NAT", 8), ("NATD", 8), ("FB", 32), ("UN", 64)]
+LISTS = [("ROT", 64), ("ZB", 8), ("YZ", 8), ("SBB", 8), ("LO", 32), ("HI", 32), ("RT", 64), ("BB", 32), ("DUP", 32),
+         ("YL", 16), ("CB", 6), ("NAT", 8), ("NATD", 8), ("UN", 64)]
 LOFF = {}
 _o = 0
 for _n, _k in LISTS:
     LOFF[_n] = _o
     _o += _k
 LTOT = _o
-COLS = ["ib", "il", "i", "h", "z", "gb", "il128", "il904", "il8p", "il8", "il64", "il960", "il1920", "sgb", "ib15",
-        "sw", "i15", "sgz", "z71", "bp", "gb128", "ngb128"]
-SCALED = [("nib", -1.0), ("ih", 0.5), ("n75", -7.5), ("n8", -8.0), ("i16b", 16.0), ("i8k", 8192.0), ("n32k", -32768.0)]
+COLS = ["ib", "il", "i", "gb", "il128", "il904", "il8p", "il8", "il64", "il1920", "sgb", "ib15",
+        "sw", "i15", "ib504", "bn", "il32", "gb128", "ngb128"]
+SCALED = [("nib", -1.0), ("ih", 0.5), ("n75", -7.5), ("n8", -8.0), ("i8b", 8.0), ("i64b", 64.0), ("n128", -128.0),
+          ("i8k", 8192.0), ("n32k", -32768.0)]
 
 f32, bf, i32, u16 = "float32", "bfloat16", "int32", "uint16"
 SB_ = {
     "xw": (3088, bf), "sdi": (1024, i32), "acti": (8, i32), "S": (1024, f32), "S1": (1024, f32), "SC": (1024, f32), "TT": (2048, f32),
     "lf": (LTOT, f32), "lu": (LTOT, u16), "pi": (8, i32), "ibits": (8, i32), "col": (32, f32),
-    "c64": (8, f32), "c4": (32, f32), "c8": (64, f32), "s8": (64, f32), "s4": (32, f32), "au": (64, f32), "az": (64, f32),
+    "c4": (32, f32), "c8": (64, f32), "s8": (64, f32), "s4": (32, f32), "au": (64, f32),
     "dd": (144, f32), "qt": (64, f32), "t8": (64, f32), "ti": (64, i32), "ti2": (64, i32), "tj": (32, i32), "tj2": (32, i32),
     "tf": (64, f32), "tf2": (64, f32), "tf3": (64, f32), "tf4": (64, f32), "idf": (8, f32),
-    "idm": (128 * 9, bf), "mwl": (512, f32), "if32": (128, f32), "nf32": (128, f32), "psw": (128, f32), "bm": (144, bf), "bm3": (144, bf),
-    "ct2": (128, f32), "ckey": (128, f32), "cr": (192, bf), "crn": (64, bf), "cm": (64, bf), "c10": (64, bf), "cpit": (128, f32),
+    "idm": (128 * 11, bf), "mwl": (512, f32), "if32": (128, f32), "nf32": (128, f32), "psw": (128, f32), "bm": (144, bf), "bm3": (144, bf),
+    "ct2": (128, f32), "ckey": (128, f32), "cr": (128, bf), "crn": (64, bf), "cm": (64, bf), "cpit": (128, f32),
     "ones": (240, f32), "one": (512, bf), "rst8": (240, f32),
-    "pp": (16, f32), "uu": (8, f32), "zm": (128, f32), "oft": (8, u16), "xg": (128, f32), "yb": (160, f32), "ym": (128, f32),
-    "mf": (MW, f32), "t2": (128, i32), "hl8": (128, i32), "hlb": (128, bf), "fs": (512, f32), "w8": (512, f32), "off": (448, u16),
-    "hi1": (512, f32), "lo1": (512, f32), "fa": (1024, bf), "gb0": (1024, bf), "gb1": (1024, bf),
+    "pp": (16, f32), "uu": (8, f32), "zm": (128, f32), "oft": (8, u16), "xg": (128, f32), "yb": (176, f32), "ym": (128, f32),
+    "mf": (64, f32), "offa": (64, u16), "t2": (128, i32), "hl8": (128, i32), "hlb": (64, bf), "fs": (512, f32), "w8": (512, f32),
+    "off": (448, u16), "fa": (1024, bf), "gb0": (1024, bf), "gb1": (1024, bf),
     "cmp": (7168, bf), "sig": (384, bf), "val": (512, bf),
     "nh": (64, bf), "sl": (8, bf), "ct": (64, bf), "cabs": (64, f32), "st": (64, bf), "key": (128, f32),
     "om": (128, f32), "code_": (192, f32), "pa": (240, f32), "cs3": (240, f32), "ea": (240, f32),
-    "app": (240, f32), "ed": (160, f32), "tl": (64, f32), "cap": (64, f32), "prod": (128, f32), "cs2": (128, f32),
-    "r1": (MW, f32), "r2": (MW, f32), "r3": (MW, f32), "r4": (MW, f32),
+    "app": (240, f32), "ed": (160, f32), "dc": (64, f32), "cap": (64, f32), "prod": (128, f32), "cs2": (128, f32),
+    "r1": (MW, f32), "r2": (MW, f32), "r3": (MW, f32),
     "vw1": (64, f32), "vw": (64, f32), "vq": (128, f32), "ncl": (128, f32), "vq2": (128, f32), "kq": (128, f32), "ce0": (128, bf),
-    "cape": (128, f32), "sct": (64, f32), "sc": (64, f32), "scs": (64, f32),
+    "cape": (128, bf), "sct": (64, f32), "sc": (64, f32), "scs": (64, f32),
     "hn1": (128, f32), "hn3": (128, f32), "aq": (128, f32), "ins": (1024, f32), "yo": (1024, f32), "rr": (128, f32),
     "o8": (16, f32), "w8s": (16, f32),
-    "msg0": (MW, u16), "msg1": (MW, u16), "msg2": (MW, u16), "in0": (MW, u16), "in1": (MW, u16), "in2": (MW, u16),
+    "msg0": (MW, f32), "msg1": (MW, f32), "msg2": (MW, f32), "in0": (MW, f32), "in1": (MW, f32), "in2": (MW, f32),
 }
 ALIAS = {"ib16": ("idm", 0), "i3k": ("idm", 128), "m00": ("mwl", 0), "m01": ("mwl", 128), "m10": ("mwl", 256), "m11": ("mwl", 384)}
 for _k, (_n, _v) in enumerate(SCALED):
@@ -54,7 +56,7 @@ for _n, (_k, _d) in SB_.items():
     SCRATCH[_n] = ("sbuf", [128, _k], _d)
 for _n, _k in PS_.items():
     SCRATCH[_n] = ("psum", [128, _k], "float32")
-SEMAPHORES = ["ev", "es", "et", "eg", "sent", "arr0", "arr1", "arr2"] + ["dm%d" % k for k in range(8)]
+SEMAPHORES = ["ev", "es", "et", "eg", "sent", "arrp", "arrq", "arrr", "arr0", "arr1", "arr2"] + ["dm%d" % k for k in range(8)]
 _PLAN = {}
 
 
@@ -64,13 +66,6 @@ def _relay(src, dst, topo):
     ok = [c for c in topo.cores_of(src) if c != src and topo.may_write(c, dst)]
     near = [c for c in ok if topo.die(c) == topo.die(src)]
     return (near or ok)[0]
-
-
-def _mask(src, dst, topo):
-    m = 0
-    for e in topo.engines(src, dst)[:NENG]:
-        m |= 1 << e
-    return m
 
 
 def _conflict(ra, rb):
@@ -123,38 +118,69 @@ def _order(ops, deps):
             f1[q] = b
             d0[k] = a + lat[k]
             d1[k] = b + lat[k]
-        return max(d0) + max(d1) + 1e-4 * (sum(d0) + sum(d1))
+        return max(d0) * 1.3 + max(d1) + 1e-4 * (sum(d0) + sum(d1)), d0, d1
+
+    def held(order, d, c):
+        before = {}
+        prev = [-1] * n
+        for k in order:
+            prev[k] = before.get(qi[k], -1)
+            before[qi[k]] = k
+        k = max(range(n), key=lambda x: d[x])
+        out = []
+        while True:
+            start = d[k] - lat[k] - c[k]
+            j = max(red[k], key=lambda x: d[x]) if red[k] else -1
+            if j >= 0 and d[j] >= start - 1e-6:
+                k = j
+            elif prev[k] >= 0:
+                if not reach[k] >> prev[k] & 1:
+                    out.append((prev[k], k))
+                k = prev[k]
+            else:
+                return out
 
     rng = np.random.default_rng(SEED)
     order = list(range(n))
-    cur = best = span(order)
+    cur, d0, d1 = span(order)
+    best = cur
     keep = list(order)
+    pairs = held(order, d0, c0) + held(order, d1, c1)
     for it in range(MOVES):
-        i = int(rng.integers(n))
-        k = order[i]
-        step = int(rng.integers(1, 40))
-        j = i
-        if rng.random() < 0.5:
-            pre = set(red[k])
-            while j > 0 and i - j < step and order[j - 1] not in pre:
-                j -= 1
-            if not any(qi[x] == qi[k] for x in order[j:i]):
-                continue
+        if pairs and rng.random() < 0.5:
+            j, k = pairs[int(rng.integers(len(pairs)))]
+            pj, pk = order.index(j), order.index(k)
+            seg = order[pj + 1:pk + 1]
+            if rng.random() < 0.5:
+                up = [x for x in seg if x == k or reach[k] >> x & 1]
+                new = order[:pj] + up + [j] + [x for x in seg if x != k and not reach[k] >> x & 1] + order[pk + 1:]
+            else:
+                down = [x for x in seg if reach[x] >> j & 1]
+                new = order[:pj] + [x for x in seg if not reach[x] >> j & 1] + [j] + down + order[pk + 1:]
         else:
-            post = set(succ[k])
-            while j < n - 1 and j - i < step and order[j + 1] not in post:
-                j += 1
-            if not any(qi[x] == qi[k] for x in order[i + 1:j + 1]):
-                continue
-        order.insert(j, order.pop(i))
-        s = span(order)
+            i = int(rng.integers(n))
+            k = order[i]
+            step = int(rng.integers(1, 60))
+            j = i
+            if rng.random() < 0.5:
+                while j > 0 and i - j < step and order[j - 1] not in red[k]:
+                    j -= 1
+                if not any(qi[x] == qi[k] for x in order[j:i]):
+                    continue
+            else:
+                while j < n - 1 and j - i < step and order[j + 1] not in succ[k]:
+                    j += 1
+                if not any(qi[x] == qi[k] for x in order[i + 1:j + 1]):
+                    continue
+            new = list(order)
+            new.insert(j, new.pop(i))
+        s, e0, e1 = span(new)
         if s <= cur + TEMP * (1.0 - it / MOVES) * rng.exponential():
-            cur = s
+            order, cur = new, s
+            pairs = held(order, e0, c0) + held(order, e1, c1)
             if s < best:
                 best = s
                 keep = list(order)
-        else:
-            order.insert(i, order.pop(j))
     return keep
 
 
@@ -229,16 +255,21 @@ def rank_program(g, core, T, topo):
             src, dst = cores[r], cores[(r + 1) % N]
             if _relay(src, dst, topo) == core:
                 rid, pid = topo.addr(dst, core)
-                for t in range(3):
-                    g.wait_ge(T.sem["arr%d" % t], NENG)
-                    g.remote_dma(T["in%d" % t][:], T["in%d" % t][:], T.sem["arr%d" % t], T.sem.sent, pid, rid, _mask(core, dst, topo))
-                g.wait_ge(T.sem.sent, 3 * NENG)
+                for t, b, lo, hi in MSGS:
+                    g.wait_ge(T.sem["arr" + t], len(topo.engines(src, core)))
+                    g.remote_dma(T["in" + b][:, lo:hi], T["in" + b][:, lo:hi], T.sem["arr" + t], T.sem.sent, pid, rid,
+                                 topo.mask(core, dst))
+                g.wait_ge(T.sem.sent, len(MSGS) * len(topo.engines(core, dst)))
         return
     nxt = cores[(rank + 1) % N]
     hop = _relay(core, nxt, topo)
     hop = nxt if hop is None else hop
     rid, pid = topo.addr(hop, core)
-    hmask = _mask(core, hop, topo)
+    hmask = topo.mask(core, hop)
+    nout = len(topo.engines(core, hop))
+    prv = cores[(rank - 1) % N]
+    back = _relay(prv, core, topo)
+    nin = len(topo.engines(prv if back is None else back, core))
 
     ops = []
     ndma = [0]
@@ -281,9 +312,9 @@ def rank_program(g, core, T, topo):
         if c is None:
             a = ins[0] if ins else outs[0]
             per = 2.0 if (two and "p" not in (a[4], ins[1][4])) or q == "g" else 1.0
-            c = [{"v": 50.0, "s": 65.0, "g": 130.0}[q] + max(64.0, a[3] * (x if a[4] == "ind" else per)) * 1.04 for x in GC]
+            c = [{"v": 50.0, "s": 65.0, "g": 130.0}[q] + max(64.0, a[3] * (x if a[4] == "ind" else per)) * y for x, y in GC]
         else:
-            c = [c, c]
+            c = [c * y if q == "t" else c for x, y in GC]
         ops.append({"q": q, "f": f, "r": r, "w": w, "b": b, "sem": sem, "n": n, "own": own, "after": list(after), "c": c, "lat": lat,
                     "open": open_})
         return len(ops) - 1
@@ -344,12 +375,14 @@ def rank_program(g, core, T, topo):
         return (t, [], [], 0, "hbm")
 
     def send(t):
-        m = ap("msg%d" % t)
-        sends[t] = rec("g", lambda e: e.remote_dma(T["in%d" % t][:], m[0], T.sem["arr%d" % t], T.sem.sent, pid, rid, hmask), [], [m],
-                       sem="sent", n=NENG * (t + 1), own=True, c=300.0, lat=TRIP)
+        b, lo, hi = [x[1:] for x in MSGS if x[0] == t][0]
+        m = ap("msg" + b, lo, hi)
+        sends[t] = rec("g", lambda e: e.remote_dma(T["in" + b][:, lo:hi], m[0], T.sem["arr" + t], T.sem.sent, pid, rid, hmask), [], [m],
+                       sem="sent", n=nout * (len(sends) + 1), own=True, c=300.0, lat=TRIP + (2500.0 if t == "p" else 0.0))
 
     def arrive(t):
-        rec("x", None, [ap("in%d" % t)], [], sem="arr%d" % t, n=NENG, c=0.0, after=[sends[t]])
+        b, lo, hi = [x[1:] for x in MSGS if x[0] == t][0]
+        rec("x", None, [ap("in" + b, lo, hi)], [], sem="arr" + t, n=nin, c=0.0, after=[sends[t]])
 
     dma("s", ap("acti"), hbm(T.act[:]))
     d_sd = dma("y", ap("sdi"), hbm(T.sd[:]))
@@ -360,21 +393,23 @@ def rank_program(g, core, T, topo):
     iota(ap("c8"), [[0, 8], [1, 8]], 0)
     iota(ap("c4"), [[0, 8], [1, 4]], 0)
     iota(ap("dd"), [[1, 144]], 0, -1)
-    iota(ap("c64"), [[1, 8]], 0)
     iota(ap("s4"), [[1, 8], [0, 4]], 1)
-    iota(ap("cpit", 0, 128, 2), [[-1, 8], [0, 8]], 15)
-    iota(ap("cpit", 1, 128, 2), [[1, 8], [0, 8]], 0)
-    iota(ap("au"), [[1, 8], [2, 8]], 1)
-    iota(ap("az"), [[0, 8], [8, 2], [0, 4]], 0)
-    iota(ap("ct2"), [[-8, 2], [0, 8], [1, 8]], 8)
-    iota(ap("ckey", 0, 64), [[0, 8], [-1, 8]], 7)
-    iota(ap("ckey", 64, 128), [[0, 8], [1, 8]], 0)
+    iota(ap("cpit"), [[-8, 2], [0, 8], [-1, 8]], 15)
+    cp(ap("pp", 0, 8), ap("acti"))
+    ts(ap("pp", 8, 16), ap("acti"), -1.0, A.mult, 15.0, A.add)
+    ts(ap("msg0", 64, 72), ap("acti"), -1.0, A.mult, 15.0, A.add)
+    ts(ap("msg0", 72, 80), ap("acti"), -512.0, A.mult, 7680.0, A.add)
+    send("p")
+    iota(ap("au"), [[64, 8], [512, 2], [2, 4]], 0)
+    iota(ap("ct2"), [[-4096, 2], [0, 8], [512, 8]], 4096)
+    iota(ap("ckey", 0, 64), [[0, 8], [-512, 8]], 3584)
+    iota(ap("ckey", 64, 128), [[0, 8], [512, 8]], 0)
     iota(ap("ones"), [[0, 240]], 1)
     rec("g", lambda e: e.affine_select(T["rst8"][:], T["ones"][:], [[0, 30], [1, 8]], A.is_gt, 0.0, 0, 0), [ap("rst8")], [ap("ones")])
     p = ap("pi", 0, 1)
-    for k, (sh, m) in enumerate([(3, 1), (0, 7), (0, 15), (1, 7), (0, 1), (4, 1)]):
+    for k, (sh, m) in enumerate([(3, 1), (0, 7), (0, 15), (4, 1)]):
         ts(ap("ibits", k, k + 1), p, sh, A.logical_shift_right, m, A.bitwise_and)
-    cp(ap("col", 0, 6), ap("ibits", 0, 6))
+    cp(ap("col", 0, 4), ap("ibits", 0, 4))
     ts(col("il1920"), col("il"), 128.0, A.mult, 1920.0, A.add)
     ts(col("gb128"), col("gb"), 128.0, A.mult)
     ts(col("ngb128"), col("gb"), -128.0, A.mult, 128.0, A.add)
@@ -388,8 +423,8 @@ def rank_program(g, core, T, topo):
     act(lfl("ZB", 4, 8), lfl("BB", 0, 4), bias=8.0)
     act(lfl("YZ", 0, 4), lfl("BB", 0, 4), scale=16.0, bias=col("il"))
     act(lfl("YZ", 4, 8), lfl("BB", 0, 4), scale=16.0, bias=col("il8p"))
-    act(ap("idf"), ap("c64"), scale=16.0, bias=col("i"))
-    act(lfl("SB"), ap("c64"), scale=0.0, bias=col("h"))
+    act(ap("idf"), ap("c8", 0, 8), scale=16.0, bias=col("i"))
+    act(lfl("SBB"), lfl("BB", 0, 8))
     ts(ap("ib16"), ap("dd", 0, 128), 0.0, A.is_equal)
     act(ap("if32"), ap("ib16"))
     ts(ap("ti"), ap("qt"), -128.0, A.mult, col("il1920"), A.add)
@@ -404,8 +439,7 @@ def rank_program(g, core, T, topo):
     act(ap("i3k"), ap("ib16"), scale=float(F))
     act(ap("nf32"), ap("ib16"), scale=-1.0)
     for n, s, sc_, b in [("il128", "il", 128.0, 0.0), ("il904", "il", -128.0, 904.0), ("sw", "ib", -16.0, 8.0), ("i15", "i", -1.0, 15.0),
-                         ("il8", "il", 8.0, 0.0), ("il64", "il", 8.0, 64.0), ("il960", "il", 16.0, 960.0),
-                         ("sgz", "z", -2.0, 1.0), ("z71", "z", 71.0, 0.0)]:
+                         ("il8", "il", 8.0, 0.0), ("il64", "il", 8.0, 64.0), ("ib504", "ib", 504.0, 0.0)]:
         act(col(n), col(s), scale=sc_, bias=b)
     act(lfl("LO"), lfl("BB"), scale=16.0, bias=col("il128"))
     act(lfl("HI"), lfl("BB"), scale=16.0, bias=col("il904"))
@@ -422,93 +456,81 @@ def rank_program(g, core, T, topo):
                 mm(ap("pd", 512 * h, 512 * h + 512), ap("i3k"), ap("one"), False, False)
 
     def clear():
-        for h in range(2):
-            mms([(ap("pd", 512 * h + pos, 512 * h + 512, 8), ap("i3k"), ap("ce0", 64 * h, 64 * h + 64), False, pos == 7)
-                 for pos in range(8)])
+        for h in (1, 0):
+            mms([(ap("pd", 512 * h + 64 * s, 512 * h + 64 * s + 64), ap("i3k"), ap("ce0", 64 * h, 64 * h + 64), False, s == 7)
+                 for s in range(8)])
 
     def refresh(last):
-        act(ap("lo1"), ind(ap("S"), lst("LO")))
+        mm(ap("pl_"), ap("if32"), ap("S", 0, 512), True, False)
         if last:
-            ts(ap("SC"), ap("S"), float(F), A.min)
+            act(ap("SC"), ind(ap("S"), lst("UN")))
         else:
-            tr(ap("TT", 0, 1024), ap("S"))
-        mm(ap("pl_"), ap("if32"), ap("lo1"), True, False)
-        act(ap("hi1"), ind(ap("S"), lst("HI")))
-        if not last:
+            act(ap("S1"), ind(ap("S"), lst("RT")))
+            tr(ap("TT", 0, 1024), ap("S1"))
             for u in range(8):
                 mm(ap("pd", 128 * (7 - u), 128 * (8 - u)), ap("psw"), ap("TT", 128 * u, 128 * u + 128), True, True)
 
-    cp(ap("pp", 0, 8), ap("acti"))
-    ts(ap("pp", 8, 16), ap("acti"), -1.0, A.mult, 15.0, A.add)
-    ms(ap("msg0"), 0)
     tt(ap("uu"), ap("pp", 0, 8), ap("pp", 8, 16), A.min)
     ts(ap("zm"), ind(ap("pp"), lst("ZB")), 8.0, A.is_ge, float(F), A.mult)
     wl_offsets("uu", 0)
-    cp(ap("msg0", 64, 72), ap("pp", 8, 16))
-    tt(ap("ce0"), ind(ap("pp", 8, 16), lst("SB")), ap("cpit"), A.is_equal)
+    tt(ap("ce0"), ind(ap("pp", 8, 16), lst("SBB")), ap("cpit"), A.is_equal)
     cp(ap("oft"), ap("pm_", 0, 8))
-    cp(ap("S"), ind(ap("sdi"), lst("ROT")))
+    ts(ap("tj"), ap("s4"), col("il"), A.add)
+    ts(ap("tj2"), ap("tj"), 7, A.bitwise_and)
+    tt(lfl("LO"), lfl("LO"), ap("tj2"), A.add)
+    tt(lfl("HI"), lfl("HI"), ap("tj2"), A.add)
+    cp(ap("lu", LOFF["LO"], LOFF["RT"]), ap("lf", LOFF["LO"], LOFF["RT"]))
+    cp(ap("S1"), ind(ap("sdi"), lst("ROT")))
+    act(ap("S"), ind(ap("S1"), ap("lu", LOFF["LO"], LOFF["RT"])))
     preload(False)
     clear()
-    tr(ap("TT", 0, 1024), ap("S"))
+    tr(ap("TT", 0, 1024), ap("S1"))
     cp(ap("xg"), ind(ap("TT", 0, 1024), ap("oft")))
-    ts(ap("tj"), ap("s4"), col("il"), A.add)
     tr(ap("yb", 0, 128), ap("xg"))
-    ts(ap("tj2"), ap("tj"), 7, A.bitwise_and)
     tt(ap("ym"), ind(ap("yb", 0, 128), lst("YZ")), ap("zm"), A.max)
-    tt(lfl("LO"), lfl("LO"), ap("tj2"), A.add)
-    tt(ap("r2", 0, 64), ap("ym", 0, 64), ap("ym", 64, 128), A.min)
-    tt(lfl("HI"), lfl("HI"), ap("tj2"), A.add)
-    cp(ap("msg0", 0, 64), ap("r2", 0, 64))
-    send(0)
+    tt(ap("msg0", 0, 64), ap("ym", 0, 64), ap("ym", 64, 128), A.min)
+    send("0")
     iota(ap("cm"), [[0, 8], [1, 8]], 0)
-    iota(ap("c10"), [[0, 64]], 10)
     iota(ap("cr", 0, 64), [[0, 8], [E8, 8]], -2 * E8)
     iota(ap("cr", 64, 128), [[0, 8], [E8, 8]], 2 * E8)
     iota(ap("cr", 71, 128, 8), [[0, 8]], E8)
-    iota(ap("cr", 128, 192), [[0, 64]], -4 * E8)
-    iota(ap("cr", 135, 192, 8), [[0, 8]], 4 * E8)
     iota(ap("yb", 144, 160), [[0, 16]], F)
     iota(ap("pa"), [[0, 240]], 0)
     iota(ap("crn"), [[0, 64]], E8)
     iota(ap("one"), [[0, 512]], 1)
 
     act(lfl("DUP"), lfl("BB"), scale=8.0, bias=col("il"))
+    act(ap("t8"), ap("c8"), scale=8.0, bias=col("ib504"))
     act(lfl("YL", 0, 4), lfl("BB", 0, 4), scale=0.0, bias=144.0)
-    act(lfl("YL", 4, 5), col("il"), bias=136.0)
+    act(col("il32"), col("ib"), scale=32.0, bias=col("il"))
+    act(lfl("YL", 4, 5), col("il32"), bias=136.0)
     act(lfl("YL", 5, 9), lfl("YZ", 4, 8))
-    act(lfl("YL", 9, 10), col("il"), bias=136.0)
+    act(lfl("YL", 9, 10), col("il32"), bias=136.0)
     act(lfl("YL", 10, 14), lfl("YZ", 0, 4))
-    act(lfl("YL", 14, 15), col("il"), bias=128.0)
+    act(lfl("YL", 14, 15), col("il32"), bias=128.0)
     act(lfl("YL", 15, 16), col("il"), bias=128.0)
     act(lfl("CB", 0, 4), lfl("BB", 0, 4), scale=8.0, bias=7.0)
     act(lfl("CB", 4, 5), col("il"), scale=8.0, bias=7.0)
     act(lfl("CB", 5, 6), col("il"), scale=8.0, bias=7.0)
-    act(col("bp"), col("h"), scale=8.0, bias=col("z71"))
+    act(col("bn"), col("il"), scale=8.0, bias=col("ib"))
     act(lfl("NAT", 0, 4), lfl("BB", 0, 4), bias=col("il8"))
     act(lfl("NAT", 4, 8), lfl("BB", 0, 4), bias=col("il64"))
-    act(lfl("PS"), ap("c64"), scale=col("sgz"), bias=col("bp"))
+    act(lfl("UN"), ap("au"), bias=col("bn"))
     act(lfl("NATD"), lfl("BB", 0, 8), bias=col("il8"))
-    act(ap("t8"), ap("c8"), scale=2.0, bias=col("ib"))
-    act(lfl("FB"), ap("c8", 0, 32), scale=16.0, bias=col("i"))
-    act(ap("tf3"), ap("t8"), AF.Abs, scale=128.0, bias=-960.0)
-    for n, v in SCALED[:2]:
-        act(ap(n), ap("ib16"), scale=v)
-    act(ap("tf4"), ap("tf3"), scale=-1.0, bias=col("il960"))
-    for n, v in SCALED[2:]:
+    for n, v in SCALED:
         act(ap(n), ap("ib16"), scale=v)
 
-    cp(ap("lu", LOFF["LO"], LOFF["BB"]), ap("lf", LOFF["LO"], LOFF["BB"]))
-    cp(ap("S"), ap("pd"))
+    ts(ap("tf3"), ap("ti2"), 0.5, A.mult)
+    tt(ap("tf4"), ap("t8"), ap("qt"), A.add)
+    tt(lfl("RT"), ap("tf3"), ap("tf4"), A.add)
+    cp(ap("lu", LOFF["RT"], LOFF["YL"]), ap("lf", LOFF["RT"], LOFF["YL"]))
+    for h in (1, 0):
+        cp(ap("S", 512 * h, 512 * h + 512), ap("pd", 512 * h, 512 * h + 512))
     ts(ap("psw"), ap("dd", 0, 128), col("sw"), A.is_equal)
     refresh(False)
-    ts(ap("ti"), ap("au"), col("ib"), A.add)
-    tt(ap("tf2"), ap("tf4"), ap("az"), A.add)
-    ts(ap("ti2"), ap("ti"), 7, A.bitwise_and)
     ms(ap("xw", F, F + 16), 2.0 ** 61)
-    tt(lfl("UN"), ap("tf2"), ap("ti2"), A.add)
     ts(ap("bm"), ap("dd"), col("i15"), A.is_equal)
-    cp(ap("lu", LOFF["BB"], LTOT), ap("lf", LOFF["BB"], LTOT))
+    cp(ap("lu", LOFF["YL"], LTOT), ap("lf", LOFF["YL"], LTOT))
     ts(ap("bm3"), ap("dd"), col("i15"), A.is_equal, 3.0, A.mult)
 
     xw = ap("xw")
@@ -535,23 +557,25 @@ def rank_program(g, core, T, topo):
 
     def acc(k0, n, stop=False):
         for k in range(k0, k0 + n):
-            mm(ap("pt_", 0, 64), ap("nib"), ap("sig", 64 * k, 64 * k + 64), False, stop)
+            mm(ap("pt_", 0, 64), ap("i8b"), ap("sig", 64 * k, 64 * k + 64), False, stop)
 
     for t in range(3):
         last = t == 2
         m = "in%d" % t
-        arrive(t)
-        act(ap("fa"), ind(xw, ap(m, 0, 64)))
-        cp(ap("mf"), ap(m))
-        tt(ap("t2"), ind(ap("mf", 64, 72), lst("BB", 0, 8)), ap("ct2"), A.add)
-        ts(ap("hl8"), ap("t2"), 8, A.bitwise_and)
-        ts(ap("hlb"), ap("hl8"), 512.0, A.mult)
-        mms([(ap("pl_", 64 * s, 64 * s + 64), ap("ib16"), ap("hlb", 64, 128), False, s == 7) for s in range(8)])
-        tt(ap("fs"), ind(ap("hlb", 0, 64), lst("DUP")), ap("hi1"), A.add)
+        arrive("pqr"[t])
+        arrive(str(t))
+        tt(ap("t2"), ind(ap(m, 72, 80), lst("BB", 0, 8)), ap("ct2"), A.add)
+        ts(ap("offa"), ap(m, 0, 64), float(F), A.min)
+        act(ap("fa"), ind(xw, ap("offa")))
+        ts(ap("hl8"), ap("t2"), 4096, A.bitwise_and)
+        ts(ap("mf"), ap(m, 0, 64), float(F), A.min)
+        cp(ap("hlb"), ap("hl8", 64, 128))
+        mms([(ap("pl_", 64 * s, 64 * s + 64), ap("ib16"), ap("hlb"), False, s == 7) for s in range(8)])
+        tt(ap("fs"), ind(ap("hl8", 0, 64), lst("DUP")), ap("S", 512, 1024), A.add)
         tt(ap("w8"), ap("fs"), ap("pl_"), A.min)
         ts(ap("off"), ap("w8", 0, 448), float(F), A.min)
-        act(ap("nh"), ap("mf", 0, 64), AF.Sign, bias=0.5 - F)
-        lsum = [(ap("if32"), ap("mf", 64, 72))] + [(ap("ih"), ap("nh", k, 64, 8)) for k in range(8)]
+        act(ap("nh"), ap(m, 0, 64), AF.Sign, bias=0.5 - F)
+        lsum = [(ap("if32"), ap(m, 64, 72))] + [(ap("ih"), ap("nh", k, 64, 8)) for k in range(8)]
         group(ap("pc_", 128, 136), lsum)
         if not last:
             act(ap("TT", 1024, 1536), ap("pd", 0, 512))
@@ -566,33 +590,38 @@ def rank_program(g, core, T, topo):
             group(ap("pb_", 320, 384), cnt + [(ap("ib16"), ap("cm"))])
         act(ap("yb", 136, 144), ap("pc_", 136, 144), scale=-1.0, bias=11.0)
         act(ap("yb", 128, 136), ap("pc_", 136, 144), bias=4.0)
+        act(ap("yb", 160, 168), ap("pc_", 136, 144), scale=512.0, bias=2048.0)
         if not last:
+            act(ap("yb", 168, 176), ap("pc_", 136, 144), scale=-512.0, bias=5632.0)
             wl_offsets("yb", 136)
         slot_a(0)
         act(ap("ct"), ap("pb_", 256, 320), bias=-4.0)
+        nat = [(ap("ib16"), ap("crn")), (ap("if32"), ap("mf", 0, 64)), (ap("i8k"), ap("ct"))]
         if not last:
             act(ap("st"), ap("pb_", 320, 384), AF.Sign, bias=-10.5)
-            tail = [(ap("i8k"), ap("ct")), (ap("n32k"), ap("st"))]
-            group(ap("pa_", 256, 320), [(ap("ib16"), ap("cr", 0, 64)), (ap("if32"), ap("mf", 0, 64))] + tail)
+            group(ap("pa_", 256, 320), [(ap("ib16"), ap("cr", 0, 64)), (ap("if32"), ap("mf", 0, 64)), (ap("i8k"), ap("ct")),
+                                        (ap("n32k"), ap("st"))])
             group(ap("pa_", 320, 384), [(ap("ib16"), ap("cr", 64, 128)), (ap("if32"), ap("mf", 0, 64))])
-            group(ap("pa_", 384, 448), [(ap("ib16"), ap("cr", 128, 192))] + tail)
+            group(ap("pa_", 384, 448), nat)
+            act(ap("dc"), ap("pb_", 256, 320), scale=float(E8), bias=-4.0 * E8)
         else:
-            group(ap("pa_", 256, 320), [(ap("ib16"), ap("crn")), (ap("if32"), ap("mf", 0, 64)), (ap("i8k"), ap("ct"))])
+            group(ap("pa_", 256, 320), nat)
         act(ap("cabs"), ap("pb_", 256, 320), AF.Abs, bias=-4.0)
         gath_b(0)
-        group(ap("pt_", 0, 64), [(ap("ib16"), ap("ct")), (ap("i16b"), ap("nh")), (ap("ib16"), ap("c10"))], stop=False)
+        group(ap("pt_", 0, 64), [(ap("n8"), ap("val", 64 * s, 64 * s + 64)) for s in (1, 3, 5)]
+              + [(ap("i64b"), ap("val", 448, 512)), (ap("n128"), ap("nh"))], stop=False)
         diff_b(0, 0)
         diff_b(0, 1)
         tt(ap("key"), ap("hl8"), ap("ckey"), A.add)
         if not last:
             act(ap("code_"), ap("pa_", 256, 448))
             cp(ap("oft"), ap("pm_", 0, 8))
-            tt(ap("om"), ind(ap("yb", 128, 136), lst("BB", 0, 8)), ap("key"), A.is_equal)
+            tt(ap("om"), ind(ap("yb", 160, 168), lst("BB", 0, 8)), ap("key"), A.is_equal)
             act(ap("xg"), ind(ap("TT"), ap("oft")))
         else:
             act(ap("code_", 0, 64), ap("pa_", 256, 320))
-            ts(ap("hn1"), ind(ap("hl8"), lst("NAT")), 0.125, A.mult)
-            tt(ap("om", 0, 64), ind(ap("yb", 128, 136), lst("BB", 0, 4)), ap("key", 0, 64), A.is_equal)
+            ts(ap("hn1"), ind(ap("hl8"), lst("NAT")), 1.0 / 4096, A.mult)
+            tt(ap("om", 0, 64), ind(ap("yb", 160, 168), lst("BB", 0, 4)), ap("key", 0, 64), A.is_equal)
         gath_b(1)
         slot_a(1)
         if last:
@@ -610,13 +639,15 @@ def rank_program(g, core, T, topo):
             scan(ap("cs3"), ap("rst8"), ap("pa"))
         else:
             for s in range(8):
-                act(ap("ins", 128 * s, 128 * s + 128), ap("vq"), AF.Abs, bias=-float(E8 * (s + 1)))
+                act(ap("pm_" if s >= 4 else "pl_", 128 * (s % 4), 128 * (s % 4) + 128), ap("vq"), AF.Abs, bias=-float(E8 * (s + 1)))
         sign_b(1, 0)
         sign_b(1, 1)
         thr(0, 2, ap("pa_", 0, 128))
         slot_a(2)
         if last:
-            tt(ap("S1"), ind(ap("SC"), lst("UN")), ap("ins"), A.min)
+            for h, bank in enumerate(("pl_", "pm_")):
+                tt(ap("S1", 512 * h, 512 * h + 512), ap("SC", 512 * h, 512 * h + 512), ap(bank), A.min)
+                mm(ap(bank), ap("if32"), ap("S1", 512 * h, 512 * h + 512), True, False)
         rows(ap("pb_", 0, 128), 5120, 7168, "bm3")
         acc(0, 2)
         if not last:
@@ -631,7 +662,7 @@ def rank_program(g, core, T, topo):
         rows(ap("pb_", 128, 192), 3072, 4096, "bm")
         thr(3, 1, ap("pb_", 128, 192))
         slot_a(4)
-        rows(ap("pc_", 0, 64), 4096, 5120, "bm")
+        group(ap("pt_", 0, 64), [(ap("bm", 15 - i, 143 - i), ap("cmp", 4096 + i, 5120, 16)) for i in range(16)], False, False)
         acc(3, 1, True)
         if not last:
             tt(ap("app"), ind(ap("yb"), lst("YL", 0, 15)), ap("ea"), A.min)
@@ -642,40 +673,48 @@ def rank_program(g, core, T, topo):
             ts(ap("aq"), ind(ap("mf", 0, 64), lst("NATD")), float(F), A.add)
             ts(ap("hn3"), ap("hn1"), float(F), A.mult)
             tt(ap("w8s", 0, 8), ap("yb", 128, 136), ap("yb", 136, 144), A.subtract)
-        ts(ap("tl"), ap("pc_", 0, 64), 9.5, A.is_ge, 2.0, A.mult)
-        tt(ap("cap"), ap("tl"), ap("pt_", 0, 64), A.is_gt)
+        ts(ap("cap"), ap("pt_", 0, 64), 49.5, A.is_gt)
         if not last:
             tt(ap("prod"), ind(ap("cap"), lst("DUP", 0, 8)), ap("om"), A.mult)
             scan(ap("cs2"), ap("rst8", 0, 128), ap("prod"))
-            tt(ap("r1"), ind(ap("cs2", 64, 128), lst("CB", 0, 5)), ap("ed", 0, 80), A.mult)
-            tt(ap("r2"), ap("r1"), ap("ed", 80, 160), A.add)
-            tt(ap("r3"), ind(ap("cs2", 0, 64), lst("CB", 0, 5)), ap("r2"), A.mult)
-            tt(ap("r4"), ap("r3"), ap("app", 160, 240), A.add)
-            ts(ap("msg%d" % (t + 1)), ap("r4"), float(F), A.min)
-            send(t + 1)
-            tt(ap("vw1"), ap("cap"), ap("code_", 128, 192), A.mult)
-            tt(ap("ncl"), ind(ap("r4", 64, 72), lst("SB")), ap("cpit"), A.not_equal)
-            tt(ap("vw"), ap("code_", 0, 64), ap("vw1"), A.subtract)
+            mo = "msg%d" % (t + 1)
+            tt(ap("r3", 64, 80), ind(ap("cs2", 0, 64), lst("CB", 4, 5)), ap("ed", 144, 160), A.mult)
+            tt(ap("r1", 0, 64), ind(ap("cs2", 64, 128), lst("CB", 0, 4)), ap("ed", 0, 64), A.mult)
+            tt(ap(mo, 64, 80), ap("r3", 64, 80), ap("app", 224, 240), A.add)
+            send("pqr"[t + 1])
+            tt(ap("r2", 0, 64), ap("r1", 0, 64), ap("ed", 80, 144), A.add)
+            tt(ap("r3", 0, 64), ind(ap("cs2", 0, 64), lst("CB", 0, 4)), ap("r2", 0, 64), A.mult)
+            tt(ap(mo, 0, 64), ap("r3", 0, 64), ap("app", 160, 224), A.add)
+            send(str(t + 1))
+            tt(ap("vw1"), ap("cap"), ap("dc"), A.mult)
+            tt(ap("ncl"), ind(ap("msg%d" % (t + 1), 64, 72), lst("BB", 0, 8)), ap("cpit"), A.not_equal)
+            tt(ap("vw"), ap("code_", 128, 192), ap("vw1"), A.subtract)
             tt(ap("kq"), ind(ap("cap"), lst("DUP", 0, 8)), ap("hl8"), A.mult)
             tt(ap("vq"), ind(ap("vw"), lst("DUP", 0, 8)), ap("hl8"), A.mult)
-            tt(ap("vq2"), ind(ap("vq"), lst("PS")), ap("ncl"), A.mult)
-            tt(ap("ce0"), ind(ap("kq"), lst("PS")), ap("ncl"), A.subtract)
-            for pos in range(8):
-                act(ap("ins", pos, 1024, 8), ap("vq2"), AF.Abs, scale=0.125, bias=-float(E8 * (pos + 1)))
+            for h in (1, 0):
+                tt(ap("vq2", 64 * h, 64 * h + 64), ap("vq", 64 * h, 64 * h + 64), ap("ncl", 64 * h, 64 * h + 64), A.mult)
+            tt(ap("ce0"), ap("kq"), ap("ncl"), A.subtract)
+            for h in (1, 0):
+                for s in range(8):
+                    act(ap("ins", 512 * h + 64 * s, 512 * h + 64 * s + 64), ap("vq2", 64 * h, 64 * h + 64), AF.Abs, scale=1.0 / 4096,
+                        bias=-float(E8 * (s + 1)))
             clear()
             if t == 0:
                 tt(ap("sc"), ap("cap"), ap("cabs"), A.mult)
             else:
                 tt(ap("sct"), ap("cap"), ap("cabs"), A.mult)
                 tt(ap("sc"), ap("sc"), ap("sct"), A.add)
-            tt(ap("S"), ap("ins"), ap("pd"), A.min)
+            for h in (1, 0):
+                tt(ap("S", 512 * h, 512 * h + 512), ap("ins", 512 * h, 512 * h + 512), ap("pd", 512 * h, 512 * h + 512), A.min)
             refresh(t == 1)
         else:
             tt(ap("cape"), ind(ap("cap"), lst("NATD")), ap("hn3"), A.mult)
-            tt(ap("yo", 512, 1024), ind(ap("cape"), lst("FB")), ap("S1", 512, 1024), A.max)
+            for bank in ("pm_", "pl_"):
+                mms([(ap(bank, 128 * s, 128 * s + 128), ap("ib16"), ap("cape"), False, s == 3) for s in range(4)])
+            ts(ap("yo", 512, 1024), ap("pm_"), float(F), A.min)
             dma("y", hbm(T.ys[:, 512:1024]), ap("yo", 512, 1024))
             tt(ap("rr"), ap("aq"), ap("cape"), A.subtract)
-            tt(ap("yo", 0, 512), ind(ap("cape"), lst("FB")), ap("S1", 0, 512), A.max)
+            ts(ap("yo", 0, 512), ap("pl_"), float(F), A.min)
             tt(ap("prod", 0, 64), ap("cap"), ap("om", 0, 64), A.mult)
             tt(ap("yo", 0, 128), ap("yo", 0, 128), ap("rr"), A.min)
             dma("s", hbm(T.ys[:, 0:512]), ap("yo", 0, 512))

@@ -1,62 +1,79 @@
+import math
 import numpy as np
 from concourse.mybir import AluOpType, ActivationFunctionType
 
 A = AluOpType
 AF = ActivationFunctionType
-F, E8 = 3072, 8192
-MW = 80
-MSGS = [("p", "0", 64, MW), ("0", "0", 0, 64), ("q", "1", 64, MW), ("1", "1", 0, 64), ("r", "2", 64, MW), ("2", "2", 0, 64)]
-WAKE, TRIP, PE = 110.0, 6000.0, 0.5
-GC = ((1.3, 0.9), (1.85, 1.15))
-MOVES, TEMP, SEED = 130000, 200.0, 4
+F, C0, K2, E16, BIG = 3072, 1536, 4096, 16384, 2 ** 20
+XW = 4096 + F + 16
+MSGS = [("p", "0", 64, 80), ("0a", "0", 0, 32), ("0b", "0", 32, 64), ("1a", "1", 0, 40), ("1b", "1", 48, 88),
+        ("2a", "2", 0, 40), ("2b", "2", 48, 88)]
+WAKE, TRIP, PE = 110.0, 5300.0, 0.545
+FIX, MMFIX, COOL, LAG, WEIGHT = 1.0, 7.0, 150.0, 1, 2.0
+EARLY, ALL, PAIRS, STARTS = 0.05, 1e-4, 0.4, 1
+SQ, ED, JQ, JY = (2, 2, 2), (0, 0), (0, 0), (1, 0)
+GC = ((1.4, 0.84), (1.9, 1.16))
+MOVES, TEMP, SEED, SHAKES, JOLT, MIX = 200000, 60.0, 1, 200, 1500.0, 0.7
 
-LISTS = [("ROT", 64), ("ZB", 8), ("YZ", 8), ("SBB", 8), ("LO", 32), ("HI", 32), ("RT", 64), ("BB", 32), ("DUP", 32),
-         ("YL", 16), ("CB", 6), ("NAT", 8), ("NATD", 8), ("UN", 64)]
+LISTS = [("ROT", 64), ("G0a", 6), ("G0b", 6), ("G1", 8), ("YZ", 4), ("XP", 72), ("DUP", 6), ("OM", 20), ("WV", 2), ("LS", 14),
+         ("CB", 4), ("NAT", 4), ("NATH", 4)]
 LOFF = {}
 _o = 0
 for _n, _k in LISTS:
     LOFF[_n] = _o
     _o += _k
 LTOT = _o
-COLS = ["ib", "il", "i", "gb", "il128", "il904", "il8p", "il8", "il64", "il1920", "sgb", "ib15",
-        "sw", "i15", "ib504", "bn", "il32", "gb128", "ngb128"]
-SCALED = [("nib", -1.0), ("ih", 0.5), ("n75", -7.5), ("n8", -8.0), ("i8b", 8.0), ("i64b", 64.0), ("n128", -128.0),
-          ("i8k", 8192.0), ("n32k", -32768.0)]
+COLS = ["ib", "il", "i", "gb", "i3", "i2", "sgb", "ib15", "il1920", "sw", "i15", "gb64", "ngb64", "xp", "yz", "ls", "cb", "nat"]
+SCALES = [1.0, -1.0, -2.0, -0.5, 2.0, 8.0, -8.0, 16.0, 33.0, -33.0, 80.0, -4096.0, 1536.0, 3072.0, 4096.0, 8192.0, 16384.0, -16384.0,
+          -65536.0, float(BIG), -float(BIG)] + [-2.0 * K2 * s for s in (1, 3, 4, 5, 6, 7)]
+LATE = [80.0, -float(BIG), 2.0, 33.0] + [-2.0 * K2 * s for s in range(1, 8)]
+ON_V = [-1.0, 8192.0, -4096.0, 1536.0, -0.5]
+ON_S = {(0, 0): 2, (0, 1): 2, (1, 0): 3, (1, 1): 2, (2, 0): 2, (2, 1): 2}
 
-f32, bf, i32, u16 = "float32", "bfloat16", "int32", "uint16"
+f32, bf, i32, u16, f16 = "float32", "bfloat16", "int32", "uint16", "float16"
 SB_ = {
-    "xw": (3088, bf), "sdi": (1024, i32), "acti": (8, i32), "S": (1024, f32), "S1": (1024, f32), "SC": (1024, f32), "TT": (2048, f32),
-    "lf": (LTOT, f32), "lu": (LTOT, u16), "pi": (8, i32), "ibits": (8, i32), "col": (32, f32),
-    "c4": (32, f32), "c8": (64, f32), "s8": (64, f32), "s4": (32, f32), "au": (64, f32),
-    "dd": (144, f32), "qt": (64, f32), "t8": (64, f32), "ti": (64, i32), "ti2": (64, i32), "tj": (32, i32), "tj2": (32, i32),
-    "tf": (64, f32), "tf2": (64, f32), "tf3": (64, f32), "tf4": (64, f32), "idf": (8, f32),
-    "idm": (128 * 11, bf), "mwl": (512, f32), "if32": (128, f32), "nf32": (128, f32), "psw": (128, f32), "bm": (144, bf), "bm3": (144, bf),
-    "ct2": (128, f32), "ckey": (128, f32), "cr": (128, bf), "crn": (64, bf), "cm": (64, bf), "cpit": (128, f32),
-    "ones": (240, f32), "one": (512, bf), "rst8": (240, f32),
-    "pp": (16, f32), "uu": (8, f32), "zm": (128, f32), "oft": (8, u16), "xg": (128, f32), "yb": (176, f32), "ym": (128, f32),
-    "mf": (64, f32), "offa": (64, u16), "t2": (128, i32), "hl8": (128, i32), "hlb": (64, bf), "fs": (512, f32), "w8": (512, f32),
-    "off": (448, u16), "fa": (1024, bf), "gb0": (1024, bf), "gb1": (1024, bf),
-    "cmp": (7168, bf), "sig": (384, bf), "val": (512, bf),
-    "nh": (64, bf), "sl": (8, bf), "ct": (64, bf), "cabs": (64, f32), "st": (64, bf), "key": (128, f32),
-    "om": (128, f32), "code_": (192, f32), "pa": (240, f32), "cs3": (240, f32), "ea": (240, f32),
-    "app": (240, f32), "ed": (160, f32), "dc": (64, f32), "cap": (64, f32), "prod": (128, f32), "cs2": (128, f32),
-    "r1": (MW, f32), "r2": (MW, f32), "r3": (MW, f32),
-    "vw1": (64, f32), "vw": (64, f32), "vq": (128, f32), "ncl": (128, f32), "vq2": (128, f32), "kq": (128, f32), "ce0": (128, bf),
-    "cape": (128, bf), "sct": (64, f32), "sc": (64, f32), "scs": (64, f32),
-    "hn1": (128, f32), "hn3": (128, f32), "aq": (128, f32), "ins": (1024, f32), "yo": (1024, f32), "rr": (128, f32),
-    "o8": (16, f32), "w8s": (16, f32),
-    "msg0": (MW, f32), "msg1": (MW, f32), "msg2": (MW, f32), "in0": (MW, f32), "in1": (MW, f32), "in2": (MW, f32),
+    "xw": ([XW], bf), "sdi": ([1024], i32), "acti": ([8], i32), "S1": ([1024], f32), "TT": ([2048], f32),
+    "lf": ([LTOT], f32), "lu": ([LTOT], u16), "pi": ([8], i32), "ibits": ([8], i32), "col": ([32], f32),
+    "su": ([64], f32), "qt": ([64], f32), "ti": ([64], i32), "ti2": ([64], i32), "tf": ([64], f32), "tf2": ([64], f32),
+    "dd": ([144], f32), "idm": ([128 * len(SCALES)], bf), "mwl": ([512], bf), "if32": ([128], f32), "nf32": ([128], f32),
+    "psw": ([128], f32), "bm": ([144], bf), "bm3": ([144], bf),
+    "cG": ([96], f32), "zero": ([128], bf), "cpw": ([160], bf), "kn": ([256], bf), "cL": ([224], bf), "cpos": ([224], f32),
+    "cwl": ([4], bf), "k4": ([512], bf), "cq": ([512], bf), "clp": ([16], bf), "rst8": ([224], bf),
+    "gb0": ([512], bf), "gb1": ([512], bf), "yo": ([128, 8], f32), "o8": ([2, 8], f32),
+    "msg0": ([80], f32), "msg1": ([96], f32), "msg2": ([96], f32), "in0": ([80], f32), "in1": ([96], f32), "in2": ([96], f32),
 }
-ALIAS = {"ib16": ("idm", 0), "i3k": ("idm", 128), "m00": ("mwl", 0), "m01": ("mwl", 128), "m10": ("mwl", 256), "m11": ("mwl", 384)}
-for _k, (_n, _v) in enumerate(SCALED):
-    ALIAS[_n] = ("idm", 128 * (_k + 2))
-PS_ = {"pd": 1024, "pa_": 512, "pb_": 512, "pc_": 512, "pt_": 512, "pl_": 512, "pm_": 512}
+PER = {
+    "X": ([18, 32], f16), "Xf": ([576], f32), "val": ([576], bf), "uu": ([4], bf), "zm": ([64], f32), "y0": ([64], f32), "ym": ([64], f32),
+    "G": ([96], bf), "hv": ([64], bf), "W": ([256], f32), "off": ([224], u16), "offa": ([32], u16), "fa": ([512], bf),
+    "ach0": ([64], f16), "ach1": ([64], f16), "nh": ([64], bf), "sl": ([8], bf), "pb": ([336], bf), "ob0": ([224], bf), "ob1": ([384], bf),
+    "st": ([32], bf), "Rf": ([16, 32], f32), "st0": ([32], bf), "oft": ([4], u16), "xg": ([64], f32), "yb": ([4, 16], f32),
+    "ly": ([224], f32), "cs": ([224], f32), "sb": ([224], f32), "ea": ([224], f32), "cand": ([5, 48], f32),
+    "cmp": ([3584], bf), "sig": ([224], bf), "cap0": ([32], bf), "cap1": ([32], bf), "pr0": ([96], bf), "pr1": ([96], bf),
+    "pr2": ([64], bf), "sc": ([4], bf), "cs2": ([64], f32), "r1": ([48], f32), "r2": ([48], f32),
+    "eq": ([64], bf), "sk": ([128], bf), "ps": ([128], bf), "hmn": ([64], bf), "kmn": ([64], bf), "aq": ([64], f32), "rr": ([64], f32),
+}
+POOL = {}
+ALIAS = {}
+OWN = ("X", "Rf", "yb", "cand", "cmp", "pb", "cs", "cs2", "cap0", "cap1", "hv", "eq", "y0", "off", "offa", "oft", "fa")
+for _c in "ab":
+    for _n, (_s, _d) in PER.items():
+        if _n in OWN:
+            SB_[_n + _c] = (_s, _d)
+        else:
+            _p = "pool" + _d + _c
+            _w = POOL.get(_p, ([0], _d))[0][0]
+            ALIAS[_n + _c] = (_p, _w, _s[0])
+            POOL[_p] = ([_w + (_s[0] + 15) // 16 * 16], _d)
+SB_.update(POOL)
+for _k in range(4):
+    ALIAS["m%d%d" % (_k // 2, _k % 2)] = ("mwl", 128 * _k, 128)
+PS_ = {"pd": [1024], "Ua": [32, 32], "Ub": [32, 32], "Ra": [512], "Rb": [512]}
 SCRATCH = {}
-for _n, (_k, _d) in SB_.items():
-    SCRATCH[_n] = ("sbuf", [128, _k], _d)
-for _n, _k in PS_.items():
-    SCRATCH[_n] = ("psum", [128, _k], "float32")
-SEMAPHORES = ["ev", "es", "et", "eg", "sent", "arrp", "arrq", "arrr", "arr0", "arr1", "arr2"] + ["dm%d" % k for k in range(8)]
+for _n, (_s, _d) in SB_.items():
+    SCRATCH[_n] = ("sbuf", [128] + _s, _d)
+for _n, _s in PS_.items():
+    SCRATCH[_n] = ("psum", [128] + _s, "float32")
+SEMAPHORES = ["ev", "es", "et", "eg", "sent"] + ["arr" + m[0] for m in MSGS] + ["dm%d" % k for k in range(8)]
 _PLAN = {}
 
 
@@ -68,12 +85,28 @@ def _relay(src, dst, topo):
     return (near or ok)[0]
 
 
-def _conflict(ra, rb):
-    for (n, lo, hi, st) in ra:
-        for (n2, lo2, hi2, st2) in rb:
-            if n == n2 and lo < hi2 and lo2 < hi and not (st == st2 and (lo - lo2) % st):
-                return True
-    return False
+def _deps(ops):
+    seen = {}
+    deps = []
+    for k, o in enumerate(ops):
+        d = set(o["after"])
+        for kind, rs in (("r", o["r"]), ("w", o["w"])):
+            for (n, lo, hi, st) in rs:
+                for (j, kind2, lo2, hi2, st2) in seen.get(n, []):
+                    if (kind == "w" or kind2 == "w") and lo < hi2 and lo2 < hi and not (st == st2 and (lo - lo2) % st):
+                        d.add(j)
+        for b in o["b"]:
+            for j in seen.get(b, []):
+                if ops[j]["q"] != o["q"] or ops[j]["open"] or o["open"]:
+                    d.add(j)
+        for kind, rs in (("r", o["r"]), ("w", o["w"])):
+            for (n, lo, hi, st) in rs:
+                seen.setdefault(n, []).append((k, kind, lo, hi, st))
+        for b in set(o["b"]):
+            seen.setdefault(b, []).append(k)
+        d.discard(k)
+        deps.append(sorted(d))
+    return deps
 
 
 def _order(ops, deps):
@@ -83,7 +116,7 @@ def _order(ops, deps):
     for k in range(n):
         m = 0
         keep = []
-        for j in sorted(set(deps[k]), reverse=True):
+        for j in reversed(deps[k]):
             if not m >> j & 1:
                 keep.append(j)
                 m |= reach[j] | 1 << j
@@ -97,28 +130,113 @@ def _order(ops, deps):
     c0 = [o["c"][0] for o in ops]
     c1 = [o["c"][1] for o in ops]
     lat = [o["lat"] + WAKE for o in ops]
+    tail = [0.0] * n
+    for k in range(n - 1, -1, -1):
+        tail[k] = c0[k] + lat[k] + max([tail[j] for j in succ[k]] or [0.0])
+    cm = [MIX * a + (1.0 - MIX) * b for a, b in zip(c0, c1)]
 
-    def span(order):
+    def fit(seq, back):
+        at = [0.0] * n
+        busy = [[] for _ in range(6)]
+        for k in seq:
+            if back:
+                a = max([at[j] + cm[j] for j in succ[k]] or [0.0]) + lat[k]
+            else:
+                a = max([at[j] + cm[j] + lat[j] for j in red[k]] or [0.0])
+            row = busy[qi[k]]
+            x = len(row)
+            while x and row[x - 1][1] > a:
+                x -= 1
+            while x < len(row) and row[x][0] < a + cm[k]:
+                a = max(a, row[x][1])
+                x += 1
+            row.insert(x, (a, a + cm[k]))
+            at[k] = a
+        return at, max(at[k] + cm[k] + (0.0 if back else lat[k]) for k in range(n))
+
+    def pack(seq):
+        at, best = fit(seq, False)
+        while True:
+            bt, _ = fit(sorted(range(n), key=lambda k: (-at[k] - cm[k] - lat[k], -k)), True)
+            ft, s = fit(sorted(range(n), key=lambda k: (-bt[k] - cm[k], k)), False)
+            if s >= best - 1.0:
+                return at, best
+            at, best = ft, s
+
+    rng = np.random.default_rng(SEED)
+    at, best = min(pack(list(range(n))), pack(sorted(range(n), key=lambda k: (-tail[k], k))), key=lambda x: x[1])
+    now, cur = at, best
+    for it in range(SHAKES):
+        mid, wide = rng.random() * cur, (0.05 + 0.3 * rng.random()) * cur
+        jolt = (rng.random(n) * JOLT * (0.2 + rng.random())).tolist()
+        key = [now[k] + (jolt[k] if abs(now[k] - mid) < wide else 0.0) for k in range(n)]
+        for k in range(n):
+            for j in red[k]:
+                key[k] = max(key[k], key[j] + 1e-3)
+        new, s = pack(sorted(range(n), key=lambda k: key[k]))
+        if s <= cur + COOL * (1.0 - it / SHAKES) * rng.exponential():
+            now, cur = new, s
+            if s < best:
+                at, best = new, s
+    order = sorted(range(n), key=lambda k: (at[k], k))
+
+    def dispatch(slack, lag, noise):
+        turn = [o["turn"][0] + lag * o["turn"][1] for o in ops]
+        for k in range(n - 1, -1, -1):
+            turn[k] = min([turn[k]] + [turn[j] for j in succ[k]])
+        key = [(turn[k], -tail[k] - x) for k, x in enumerate((noise * rng.random(n)).tolist())]
+        left = [len(x) for x in red]
+        at = [0.0] * n
+        free = [0.0] * 6
+        ready = [k for k in range(n) if not left[k]]
+        out = []
+        while ready:
+            k = min(ready, key=lambda x: max(at[x], free[qi[x]]))
+            first = max(at[k], free[qi[k]]) + slack
+            k = min((x for x in ready if qi[x] == qi[k] and at[x] <= first), key=lambda x: key[x])
+            ready.remove(k)
+            out.append(k)
+            free[qi[k]] = max(at[k], free[qi[k]]) + cm[k]
+            for j in succ[k]:
+                at[j] = max(at[j], free[qi[k]] + lat[k])
+                left[j] -= 1
+                if not left[j]:
+                    ready.append(j)
+        return out
+
+    sent = [k for k in range(n) if ops[k]["own"]]
+    item = [(qi[k], red[k], c0[k], c1[k], lat[k]) for k in range(n)]
+
+    def span(order, p=0, d=None):
         f0 = [0.0] * 6
         f1 = [0.0] * 6
-        d0 = [0.0] * n
-        d1 = [0.0] * n
-        for k in order:
-            q = qi[k]
+        d0 = list(d[0]) if p else [0.0] * n
+        d1 = list(d[1]) if p else [0.0] * n
+        left = set(range(5))
+        x = p
+        while x and left:
+            x -= 1
+            k = order[x]
+            if qi[k] in left:
+                left.discard(qi[k])
+                f0[qi[k]] = d0[k] - lat[k]
+                f1[qi[k]] = d1[k] - lat[k]
+        for k in order[p:]:
+            q, pre, x, y, z = item[k]
             a = f0[q]
             b = f1[q]
-            for j in red[k]:
+            for j in pre:
                 if d0[j] > a:
                     a = d0[j]
                 if d1[j] > b:
                     b = d1[j]
-            a += c0[k]
-            b += c1[k]
+            a += x
+            b += y
             f0[q] = a
             f1[q] = b
-            d0[k] = a + lat[k]
-            d1[k] = b + lat[k]
-        return max(d0) * 1.3 + max(d1) + 1e-4 * (sum(d0) + sum(d1)), d0, d1
+            d0[k] = a + z
+            d1[k] = b + z
+        return MIX * max(d0) + (1.0 - MIX) * max(d1) + ALL * sum(d0) + EARLY * sum([d0[k] for k in sent]), (d0, d1)
 
     def held(order, d, c):
         before = {}
@@ -140,66 +258,57 @@ def _order(ops, deps):
             else:
                 return out
 
-    rng = np.random.default_rng(SEED)
-    order = list(range(n))
-    cur, d0, d1 = span(order)
-    best = cur
-    keep = list(order)
-    pairs = held(order, d0, c0) + held(order, d1, c1)
-    for it in range(MOVES):
-        if pairs and rng.random() < 0.5:
-            j, k = pairs[int(rng.integers(len(pairs)))]
-            pj, pk = order.index(j), order.index(k)
+    def anneal(order, moves, temp):
+        cur, d = span(order)
+        best, keep, fresh = cur, order, 0
+        pairs = held(order, d[0], c0) + held(order, d[1], c1)
+        draw = rng.random((moves, 4)).tolist()
+        for it, (u, v, w, e) in enumerate(draw):
+            if it % 500 == 0:
+                order = sorted(order, key=lambda k: d[0][k] - lat[k] - c0[k])
+            if pairs and u < PAIRS:
+                j, k = pairs[int(v * len(pairs))]
+                pj, pk = order.index(j), order.index(k)
+                if pj > pk:
+                    continue
+            else:
+                pj = int(v * n)
+                j = order[pj]
+                hop = 1 + int(3.0 * (u * 64.0 % 1.0) ** 2)
+                pk = pj
+                while hop and pk < n - 1:
+                    pk += 1
+                    hop -= qi[order[pk]] == qi[j]
+                k = order[pk]
+                if hop or reach[k] >> j & 1:
+                    continue
             seg = order[pj + 1:pk + 1]
-            if rng.random() < 0.5:
-                up = [x for x in seg if x == k or reach[k] >> x & 1]
-                new = order[:pj] + up + [j] + [x for x in seg if x != k and not reach[k] >> x & 1] + order[pk + 1:]
+            if w < 0.5:
+                m = reach[k] | 1 << k
+                new = order[:pj] + [x for x in seg if m >> x & 1] + [j] + [x for x in seg if not m >> x & 1] + order[pk + 1:]
             else:
-                down = [x for x in seg if reach[x] >> j & 1]
-                new = order[:pj] + [x for x in seg if not reach[x] >> j & 1] + [j] + down + order[pk + 1:]
-        else:
-            i = int(rng.integers(n))
-            k = order[i]
-            step = int(rng.integers(1, 60))
-            j = i
-            if rng.random() < 0.5:
-                while j > 0 and i - j < step and order[j - 1] not in red[k]:
-                    j -= 1
-                if not any(qi[x] == qi[k] for x in order[j:i]):
-                    continue
-            else:
-                while j < n - 1 and j - i < step and order[j + 1] not in succ[k]:
-                    j += 1
-                if not any(qi[x] == qi[k] for x in order[i + 1:j + 1]):
-                    continue
-            new = list(order)
-            new.insert(j, new.pop(i))
-        s, e0, e1 = span(new)
-        if s <= cur + TEMP * (1.0 - it / MOVES) * rng.exponential():
-            order, cur = new, s
-            pairs = held(order, e0, c0) + held(order, e1, c1)
-            if s < best:
-                best = s
-                keep = list(order)
-    return keep
+                new = order[:pj] + [x for x in seg if not reach[x] >> j & 1] + [j] + [x for x in seg if reach[x] >> j & 1] + order[pk + 1:]
+            s, f = span(new, pj, d)
+            if s <= cur - temp * (1.02 - it / moves) * math.log(1.0 - e):
+                order, cur, d = new, s, f
+                if it > fresh:
+                    pairs = held(order, d[0], c0) + held(order, d[1], c1)
+                    fresh = it + 12
+                if s < best:
+                    best, keep = s, order
+        return best, keep
+
+    tries = [anneal(order, MOVES // (2 * STARTS), TEMP) for _ in range(STARTS)]
+    best, order = anneal(min(tries)[1], MOVES // 2, 0.6 * TEMP)
+    _PLAN["span"] = ([x[0] for x in tries], best)
+    return order
 
 
 def _emit(g, T, ops):
     Q = {"v": g.vector, "s": g.scalar, "t": g.tensor, "g": g, "y": g.sync}
     if "deps" not in _PLAN:
-        deps = []
-        for k, o in enumerate(ops):
-            d = list(o["after"])
-            for j in range(k):
-                p = ops[j]
-                c = _conflict(p["w"], o["r"]) or _conflict(p["w"], o["w"]) or _conflict(p["r"], o["w"])
-                if not c and (p["q"] != o["q"] or p["open"] or o["open"]):
-                    c = _conflict(p["b"], o["b"])
-                if c:
-                    d.append(j)
-            deps.append(d)
-        _PLAN["deps"] = deps
-        _PLAN["order"] = _order(ops, deps)
+        _PLAN["deps"] = _deps(ops)
+        _PLAN["order"] = _order(ops, [sorted(set(d + o["soft"])) for d, o in zip(_PLAN["deps"], ops)])
     deps, order = _PLAN["deps"], _PLAN["order"]
     cnt = {"v": 0, "s": 0, "t": 0, "g": 0}
     tok = {}
@@ -222,7 +331,7 @@ def _emit(g, T, ops):
         want = {}
         src = {}
         for j in deps[k]:
-            if q == "t" and ops[j]["q"] == "t":
+            if q == ops[j]["q"] and (q == "t" or (o["own"] and ops[j]["own"])):
                 continue
             s, n = tok[j]
             if n > want.get(s, 0):
@@ -274,33 +383,51 @@ def rank_program(g, core, T, topo):
     ops = []
     ndma = [0]
     sends = {}
+    turn = []
+    now = [9, 0]
+
+    def shape(name):
+        return SB_[name][0] if name in SB_ else PS_[name]
+
+    def pack(name, real, lo, hi, step, n):
+        banks = [(name, b) for b in range(lo // 512, (hi - 1) // 512 + 1)] if name in PS_ else []
+        return (real, [(name, lo, hi, step)], banks, n, "p" if name in PS_ else SB_[name][1])
 
     def ap(name, lo=0, hi=None, step=1):
         if name in ALIAS:
-            name, lo = ALIAS[name]
-            hi = lo + 128
-        w = SB_[name][0] if name in SB_ else PS_[name]
-        hi = w if hi is None else hi
-        real = T[name][:, lo:hi] if step == 1 else T[name][:, lo:hi:step]
-        banks = [(name, b, b + 1, 1) for b in range(lo // 512, (hi - 1) // 512 + 1)] if name in PS_ else []
-        return (real, [(name, lo, hi, step)], banks, len(range(lo, hi, step)), "p" if name in PS_ else SB_[name][1])
+            name, base, w = ALIAS[name]
+            lo, hi = base + lo, base + (w if hi is None else hi)
+        sh = shape(name)
+        hi = int(np.prod(sh)) if hi is None else hi
+        if len(sh) == 1:
+            real = T[name][:, lo:hi:step] if step > 1 else T[name][:, lo:hi]
+        elif lo // sh[1] == (hi - 1) // sh[1]:
+            real = T[name][:, lo // sh[1], lo % sh[1]:(hi - 1) % sh[1] + 1:step]
+        else:
+            real = T[name][:, lo // sh[1]:hi // sh[1], :]
+        return pack(name, real, lo, hi, step, len(range(lo, hi, step)))
+
+    def ap3(name, r0, r1, rs, k0, k1, ks=1):
+        w = shape(name)[1]
+        n = len(range(r0, r1, rs)) * len(range(k0, k1, ks))
+        return pack(name, T[name][:, r0:r1:rs, k0:k1:ks], r0 * w + k0, (r1 - 1) * w + k1, 1, n)
 
     def ind(win, offs):
         return (win[0].indirect(offs[0]), win[1] + offs[1], [], 16 * offs[3], "ind")
 
-    def lst(name, k0=0, k1=None):
+    def lst(name, k0=0, k1=None, buf="lu"):
         k1 = dict(LISTS)[name] if k1 is None else k1
-        return ap("lu", LOFF[name] + k0, LOFF[name] + k1)
-
-    def lfl(name, k0=0, k1=None):
-        k1 = dict(LISTS)[name] if k1 is None else k1
-        return ap("lf", LOFF[name] + k0, LOFF[name] + k1)
+        return ap(buf, LOFF[name] + k0, LOFF[name] + k1)
 
     def col(name):
         k = COLS.index(name)
         return ap("col", k, k + 1)
 
-    def rec(q, f, outs, ins, sem=None, n=0, own=False, after=(), c=None, lat=0.0, two=False, open_=False):
+    def I(v):
+        k = SCALES.index(float(v))
+        return ap("idm", 128 * k, 128 * k + 128)
+
+    def rec(q, f, outs, ins, sem=None, n=0, own=False, after=(), c=None, lat=0.0, two=False, half=False, open_=False):
         r, w, b = [], [], []
         for a in ins:
             if isinstance(a, tuple):
@@ -312,11 +439,14 @@ def rank_program(g, core, T, topo):
         if c is None:
             a = ins[0] if ins else outs[0]
             per = 2.0 if (two and "p" not in (a[4], ins[1][4])) or q == "g" else 1.0
-            c = [{"v": 50.0, "s": 65.0, "g": 130.0}[q] + max(64.0, a[3] * (x if a[4] == "ind" else per)) * y for x, y in GC]
+            if half and a[4] in (bf, f16, u16) and outs[0][4] in (bf, f16, u16):
+                per = 0.5
+            fix = {"v": 50.0, "s": 65.0, "g": 130.0}[q] * (1.0 if a[4] == "ind" or q == "g" else FIX)
+            c = [fix + max(64.0, a[3] * (x if a[4] == "ind" else per)) * y for x, y in GC]
         else:
             c = [c * y if q == "t" else c for x, y in GC]
         ops.append({"q": q, "f": f, "r": r, "w": w, "b": b, "sem": sem, "n": n, "own": own, "after": list(after), "c": c, "lat": lat,
-                    "open": open_})
+                    "open": open_, "soft": [], "turn": tuple(now)})
         return len(ops) - 1
 
     def raw(a):
@@ -327,14 +457,14 @@ def rank_program(g, core, T, topo):
 
     def ts(o, a, s1, op0, s2=None, op1=None):
         if op1 is None:
-            return rec("v", lambda e: e.tensor_scalar(o[0], a[0], raw(s1), None, op0), [o], [a, s1])
-        return rec("v", lambda e: e.tensor_scalar(o[0], a[0], raw(s1), raw(s2), op0, op1), [o], [a, s1, s2])
+            return rec("v", lambda e: e.tensor_scalar(o[0], a[0], raw(s1), None, op0), [o], [a, s1], half=True)
+        return rec("v", lambda e: e.tensor_scalar(o[0], a[0], raw(s1), raw(s2), op0, op1), [o], [a, s1, s2], half=True)
 
     def cp(o, a):
-        return rec("v", lambda e: e.tensor_copy(o[0], a[0]), [o], [a])
+        return rec("v", lambda e: e.tensor_copy(o[0], a[0]), [o], [a], half=True)
 
     def ms(o, c):
-        return rec("v", lambda e: e.memset(o[0], c), [o], [])
+        return rec("v", lambda e: e.memset(o[0], c), [o], [], half=True)
 
     def scan(o, d0, d1):
         return rec("v", lambda e: e.tensor_tensor_scan(o[0], d0[0], d1[0], 0.0, A.mult, A.add), [o], [d0, d1])
@@ -345,23 +475,19 @@ def rank_program(g, core, T, topo):
     def act(o, a, fn=AF.Identity, scale=1.0, bias=0.0):
         return rec("s", lambda e: e.activation(o[0], a[0], fn, bias=raw(bias), scale=raw(scale)), [o], [a, scale, bias])
 
-    def mms(items):
+    def mms(items, start=True, stop=True, each=False):
+        banks = [o[2][0] for o, l, r in items]
+
         def f(e):
-            for (o, l, r, start, stop) in items:
-                ins = e.matmul(o[0], l[0], r[0], start, stop)
+            for k, (o, l, r) in enumerate(items):
+                ins = e.matmul(o[0], l[0], r[0], each or (start and banks[k] not in banks[:k]), each or (stop and banks[k] not in banks[k + 1:]))
             return ins
-        c = sum(max(64, r[3]) * (4 if r[4] == f32 else 1) * PE for (o, l, r, start, stop) in items)
-        return rec("t", f, [x[0] for x in items], [x[1] for x in items] + [x[2] for x in items], c=c,
-                   open_=not (items[0][3] and items[-1][4]))
-
-    def mm(o, l, r, start, stop):
-        return mms([(o, l, r, start, stop)])
-
-    def group(o, terms, start=True, stop=True):
-        return mms([(o, l, r, start and k == 0, stop and k == len(terms) - 1) for k, (l, r) in enumerate(terms)])
+        c = sum((max(64, r[3]) * (4 if r[4] == f32 else 1) + MMFIX) * PE for (o, l, r) in items)
+        return rec("t", f, [x[0] for x in items], [x[1] for x in items] + [x[2] for x in items], c=c, open_=not (start and stop))
 
     def iota(o, pat, base, ch=0):
-        if SB_[o[1][0][0]][1] == i32:
+        name = o[1][0][0]
+        if SB_[name][1] == i32:
             return rec("g", lambda e: e.iota(o[0], pat, base, ch), [o], [])
         return rec("g", lambda e: e.iota(o[0], pat, base, ch, allow_small_or_imprecise_dtypes=True), [o], [])
 
@@ -369,7 +495,7 @@ def rank_program(g, core, T, topo):
         s = "dm%d" % ndma[0]
         ndma[0] += 1
         return rec(q, lambda e: e.dma_start(o[0], a[0]), [o], [a], sem=s, n=16, after=after, c=100.0,
-                   lat=2000.0 + 2.56 * max(o[3], a[3]))
+                   lat=2000.0 + 1.6 * max(o[3], a[3]) * (0.5 if bf in (o[4], a[4]) else 1.0))
 
     def hbm(t):
         return (t, [], [], 0, "hbm")
@@ -378,353 +504,376 @@ def rank_program(g, core, T, topo):
         b, lo, hi = [x[1:] for x in MSGS if x[0] == t][0]
         m = ap("msg" + b, lo, hi)
         sends[t] = rec("g", lambda e: e.remote_dma(T["in" + b][:, lo:hi], m[0], T.sem["arr" + t], T.sem.sent, pid, rid, hmask), [], [m],
-                       sem="sent", n=nout * (len(sends) + 1), own=True, c=300.0, lat=TRIP + (2500.0 if t == "p" else 0.0))
+                       sem="sent", n=nout * (len(sends) + 1), own=True, c=2300.0 if t == "p" else 300.0,
+                       after=list(sends.values())[-1:])
 
     def arrive(t):
         b, lo, hi = [x[1:] for x in MSGS if x[0] == t][0]
-        rec("x", None, [ap("in" + b, lo, hi)], [], sem="arr" + t, n=nin, c=0.0, after=[sends[t]])
+        rec("x", None, [ap("in" + b, lo, hi)], [], sem="arr" + t, n=nin, c=0.0, after=[sends[t]],
+            lat=TRIP + (2000.0 if t == "p" else 0.0))
+
+    def mklist(name, k0, k1, family):
+        ts(lst(name, k0, k1), lst(name, k0, k1, "lf"), col(family), A.add)
 
     dma("s", ap("acti"), hbm(T.act[:]))
     d_sd = dma("y", ap("sdi"), hbm(T.sd[:]))
-    dma("y", ap("xw", 0, F), hbm(T.x[:]), after=[d_sd])
+    d_x = dma("y", ap("xw", 0, F), hbm(T.x[:]), after=[d_sd])
+    ops[dma("y", ap("xw", 4096, 4096 + F), hbm(T.x[:]), after=[d_sd])]["lat"] += ops[d_x]["lat"] - 2000.0
+    ops[-1]["soft"].append(d_sd)
+    cp(ap("msg0", 64, 72), ap("acti"))
+    ts(ap("msg0", 72, 80), ap("acti"), -1.0, A.mult, 15.0, A.add)
+    send("p")
 
     iota(ap("pi", 0, 1), [[0, 1]], 0, 1)
-    iota(ap("s8"), [[1, 8], [0, 8]], 0)
-    iota(ap("c8"), [[0, 8], [1, 8]], 0)
-    iota(ap("c4"), [[0, 8], [1, 4]], 0)
-    iota(ap("dd"), [[1, 144]], 0, -1)
-    iota(ap("s4"), [[1, 8], [0, 4]], 1)
-    iota(ap("cpit"), [[-8, 2], [0, 8], [-1, 8]], 15)
-    cp(ap("pp", 0, 8), ap("acti"))
-    ts(ap("pp", 8, 16), ap("acti"), -1.0, A.mult, 15.0, A.add)
-    ts(ap("msg0", 64, 72), ap("acti"), -1.0, A.mult, 15.0, A.add)
-    ts(ap("msg0", 72, 80), ap("acti"), -512.0, A.mult, 7680.0, A.add)
-    send("p")
-    iota(ap("au"), [[64, 8], [512, 2], [2, 4]], 0)
-    iota(ap("ct2"), [[-4096, 2], [0, 8], [512, 8]], 4096)
-    iota(ap("ckey", 0, 64), [[0, 8], [-512, 8]], 3584)
-    iota(ap("ckey", 64, 128), [[0, 8], [512, 8]], 0)
-    iota(ap("ones"), [[0, 240]], 1)
-    rec("g", lambda e: e.affine_select(T["rst8"][:], T["ones"][:], [[0, 30], [1, 8]], A.is_gt, 0.0, 0, 0), [ap("rst8")], [ap("ones")])
-    p = ap("pi", 0, 1)
-    for k, (sh, m) in enumerate([(3, 1), (0, 7), (0, 15), (4, 1)]):
-        ts(ap("ibits", k, k + 1), p, sh, A.logical_shift_right, m, A.bitwise_and)
+    for k, (sh, m) in enumerate([(3, 1), (0, 7), (0, 15), (4, 1), (0, 3), (2, 3)]):
+        ts(ap("ibits", k, k + 1), ap("pi", 0, 1), sh, A.logical_shift_right, m, A.bitwise_and)
+        cp(ap("col", k, k + 1), ap("ibits", k, k + 1)) if k >= 4 else None
     cp(ap("col", 0, 4), ap("ibits", 0, 4))
-    ts(col("il1920"), col("il"), 128.0, A.mult, 1920.0, A.add)
-    ts(col("gb128"), col("gb"), 128.0, A.mult)
-    ts(col("ngb128"), col("gb"), -128.0, A.mult, 128.0, A.add)
-    act(col("sgb"), col("ib"), scale=-2.0, bias=1.0)
-    act(col("ib15"), col("ib"), scale=15.0)
-    act(col("il8p"), col("il"), bias=8.0)
-    act(ap("qt"), ap("s8"), scale=col("sgb"), bias=col("ib15"))
-    act(lfl("BB"), ap("c4"), scale=2.0, bias=col("ib"))
-    act(ap("tf"), ap("qt"), scale=8.0)
-    act(lfl("ZB", 0, 4), lfl("BB", 0, 4))
-    act(lfl("ZB", 4, 8), lfl("BB", 0, 4), bias=8.0)
-    act(lfl("YZ", 0, 4), lfl("BB", 0, 4), scale=16.0, bias=col("il"))
-    act(lfl("YZ", 4, 8), lfl("BB", 0, 4), scale=16.0, bias=col("il8p"))
-    act(ap("idf"), ap("c8", 0, 8), scale=16.0, bias=col("i"))
-    act(lfl("SBB"), lfl("BB", 0, 8))
-    ts(ap("ib16"), ap("dd", 0, 128), 0.0, A.is_equal)
-    act(ap("if32"), ap("ib16"))
-    ts(ap("ti"), ap("qt"), -128.0, A.mult, col("il1920"), A.add)
-    ts(ap("m00"), ap("dd", 0, 128), 0.0, A.is_equal, col("ngb128"), A.mult)
-    ts(ap("ti2"), ap("ti"), 896, A.bitwise_and)
-    tt(ap("tf2"), ap("tf"), ap("c8"), A.add)
-    ts(ap("m01"), ap("dd", 0, 128), 16.0, A.is_equal, col("ngb128"), A.mult)
-    tt(lfl("ROT"), ap("tf2"), ap("ti2"), A.add)
-    ts(ap("m10"), ap("dd", 0, 128), -16.0, A.is_equal, col("gb128"), A.mult)
-    ts(ap("m11"), ap("dd", 0, 128), 0.0, A.is_equal, col("gb128"), A.mult)
-    cp(ap("lu", 0, LOFF["LO"]), ap("lf", 0, LOFF["LO"]))
-    act(ap("i3k"), ap("ib16"), scale=float(F))
-    act(ap("nf32"), ap("ib16"), scale=-1.0)
-    for n, s, sc_, b in [("il128", "il", 128.0, 0.0), ("il904", "il", -128.0, 904.0), ("sw", "ib", -16.0, 8.0), ("i15", "i", -1.0, 15.0),
-                         ("il8", "il", 8.0, 0.0), ("il64", "il", 8.0, 64.0), ("ib504", "ib", 504.0, 0.0)]:
+    for n, s, sc_, b in [("sgb", "ib", -2.0, 1.0), ("ib15", "ib", 15.0, 0.0), ("il1920", "il", 128.0, 1920.0), ("sw", "ib", -16.0, 8.0),
+                         ("i15", "i", -1.0, 15.0), ("gb64", "gb", 64.0, 0.0), ("ngb64", "gb", -64.0, 64.0), ("xp", "il", 8.0, col("ib")),
+                         ("yz", "ib", 16.0, col("il")), ("ls", "ib", 8.0, 7.0), ("cb", "i3", 8.0, 7.0), ("nat", "i3", 8.0, col("i2"))]:
         act(col(n), col(s), scale=sc_, bias=b)
-    act(lfl("LO"), lfl("BB"), scale=16.0, bias=col("il128"))
-    act(lfl("HI"), lfl("BB"), scale=16.0, bias=col("il904"))
-
-    def wl_offsets(nm, lo):
-        for gp in range(2):
-            group(ap("pm_", gp, 8, 2), [(ap("m%d0" % gp), ap(nm, lo, lo + 8, 2)), (ap("m%d1" % gp), ap(nm, lo + 1, lo + 8, 2)),
-                                        (ap("if32"), ap("idf", gp, 8, 2))])
-
-    def preload(plus):
-        for h in range(2):
-            mm(ap("pd", 512 * h, 512 * h + 512), ap("if32"), ap("S", 512 * h, 512 * h + 512), True, False)
-            if plus:
-                mm(ap("pd", 512 * h, 512 * h + 512), ap("i3k"), ap("one"), False, False)
-
-    def clear():
-        for h in (1, 0):
-            mms([(ap("pd", 512 * h + 64 * s, 512 * h + 64 * s + 64), ap("i3k"), ap("ce0", 64 * h, 64 * h + 64), False, s == 7)
-                 for s in range(8)])
-
-    def refresh(last):
-        mm(ap("pl_"), ap("if32"), ap("S", 0, 512), True, False)
-        if last:
-            act(ap("SC"), ind(ap("S"), lst("UN")))
+    iota(ap("dd"), [[1, 144]], 0, -1)
+    iota(ap("su"), [[0, 2], [1, 8], [0, 4]], 0)
+    iota(ap("tf2"), [[4, 2], [0, 8], [1, 4]], 0)
+    act(ap("qt"), ap("su"), scale=col("sgb"), bias=col("ib15"))
+    ts(ap("ti"), ap("qt"), -128.0, A.mult, col("il1920"), A.add)
+    act(ap("tf"), ap("qt"), scale=8.0)
+    ts(ap("ti2"), ap("ti"), 896, A.bitwise_and)
+    tt(ap("tf"), ap("tf"), ap("tf2"), A.add)
+    tt(lst("ROT", buf="lf"), ap("tf"), ap("ti2"), A.add)
+    cp(lst("ROT"), lst("ROT", buf="lf"))
+    for c in range(2):
+        iota(lst("G0" + "ab"[c], 0, 4, "lf"), [[0, 2], [2, 2]], 4 * c)
+        iota(lst("G0" + "ab"[c], 4, 6, "lf"), [[2, 2]], 8 + 4 * c)
+    iota(lst("G1", 0, 4, "lf"), [[0, 2], [2, 2]], 0)
+    iota(lst("G1", 4, 6, "lf"), [[2, 2]], 4)
+    mklist("G0a", 0, 18, "ib")
+    iota(lst("YZ", buf="lf"), [[8, 2], [32, 2]], 0)
+    mklist("YZ", 0, 4, "yz")
+    ts(I(1), ap("dd", 0, 128), 0.0, A.is_equal)
+    for gp, e, d, cn in [(0, 0, 0.0, "ngb64"), (0, 1, 16.0, "ngb64"), (1, 0, -16.0, "gb64"), (1, 1, 0.0, "gb64")]:
+        ts(ap("m%d%d" % (gp, e)), ap("dd", 0, 128), d, A.is_equal, col(cn), A.mult)
+    iota(ap("cwl"), [[16, 4]], 0)
+    for c in range(2):
+        iota(lst("XP", 36 * c, 36 * c + 8, "lf"), [[0, 2], [64, 2], [2, 2]], 896 + 4 * c)
+        iota(lst("XP", 36 * c + 8, 36 * c + 36, "lf"), [[128, 7], [64, 2], [2, 2]], 4 * c)
+    mklist("XP", 0, 72, "xp")
+    iota(ap("cG", 0, 64), [[8, 2], [0, 4], [1, 8]], 0)
+    iota(ap("cG", 64, 96), [[0, 4], [-1, 8]], 16)
+    ms(ap("k4"), 1.0)
+    iota(ap("zero"), [[0, 128]], 0)
+    for v in SCALES[1:]:
+        if v <= -2.0 * K2 * max(max(SQ), 3) and v > -65536.0:
+            continue
+        if v in LATE:
+            rec("g", lambda e, v=v: e.affine_select(I(v)[0], T["zero"][:], [[-1, 128]], A.not_equal, v, 0, 1), [I(v)], [ap("zero")])
+        elif v in ON_V:
+            ts(I(v), I(1), v, A.mult)
         else:
-            act(ap("S1"), ind(ap("S"), lst("RT")))
-            tr(ap("TT", 0, 1024), ap("S1"))
-            for u in range(8):
-                mm(ap("pd", 128 * (7 - u), 128 * (8 - u)), ap("psw"), ap("TT", 128 * u, 128 * u + 128), True, True)
-
-    tt(ap("uu"), ap("pp", 0, 8), ap("pp", 8, 16), A.min)
-    ts(ap("zm"), ind(ap("pp"), lst("ZB")), 8.0, A.is_ge, float(F), A.mult)
-    wl_offsets("uu", 0)
-    tt(ap("ce0"), ind(ap("pp", 8, 16), lst("SBB")), ap("cpit"), A.is_equal)
-    cp(ap("oft"), ap("pm_", 0, 8))
-    ts(ap("tj"), ap("s4"), col("il"), A.add)
-    ts(ap("tj2"), ap("tj"), 7, A.bitwise_and)
-    tt(lfl("LO"), lfl("LO"), ap("tj2"), A.add)
-    tt(lfl("HI"), lfl("HI"), ap("tj2"), A.add)
-    cp(ap("lu", LOFF["LO"], LOFF["RT"]), ap("lf", LOFF["LO"], LOFF["RT"]))
-    cp(ap("S1"), ind(ap("sdi"), lst("ROT")))
-    act(ap("S"), ind(ap("S1"), ap("lu", LOFF["LO"], LOFF["RT"])))
-    preload(False)
-    clear()
-    tr(ap("TT", 0, 1024), ap("S1"))
-    cp(ap("xg"), ind(ap("TT", 0, 1024), ap("oft")))
-    tr(ap("yb", 0, 128), ap("xg"))
-    tt(ap("ym"), ind(ap("yb", 0, 128), lst("YZ")), ap("zm"), A.max)
-    tt(ap("msg0", 0, 64), ap("ym", 0, 64), ap("ym", 64, 128), A.min)
-    send("0")
-    iota(ap("cm"), [[0, 8], [1, 8]], 0)
-    iota(ap("cr", 0, 64), [[0, 8], [E8, 8]], -2 * E8)
-    iota(ap("cr", 64, 128), [[0, 8], [E8, 8]], 2 * E8)
-    iota(ap("cr", 71, 128, 8), [[0, 8]], E8)
-    iota(ap("yb", 144, 160), [[0, 16]], F)
-    iota(ap("pa"), [[0, 240]], 0)
-    iota(ap("crn"), [[0, 64]], E8)
-    iota(ap("one"), [[0, 512]], 1)
-
-    act(lfl("DUP"), lfl("BB"), scale=8.0, bias=col("il"))
-    act(ap("t8"), ap("c8"), scale=8.0, bias=col("ib504"))
-    act(lfl("YL", 0, 4), lfl("BB", 0, 4), scale=0.0, bias=144.0)
-    act(col("il32"), col("ib"), scale=32.0, bias=col("il"))
-    act(lfl("YL", 4, 5), col("il32"), bias=136.0)
-    act(lfl("YL", 5, 9), lfl("YZ", 4, 8))
-    act(lfl("YL", 9, 10), col("il32"), bias=136.0)
-    act(lfl("YL", 10, 14), lfl("YZ", 0, 4))
-    act(lfl("YL", 14, 15), col("il32"), bias=128.0)
-    act(lfl("YL", 15, 16), col("il"), bias=128.0)
-    act(lfl("CB", 0, 4), lfl("BB", 0, 4), scale=8.0, bias=7.0)
-    act(lfl("CB", 4, 5), col("il"), scale=8.0, bias=7.0)
-    act(lfl("CB", 5, 6), col("il"), scale=8.0, bias=7.0)
-    act(col("bn"), col("il"), scale=8.0, bias=col("ib"))
-    act(lfl("NAT", 0, 4), lfl("BB", 0, 4), bias=col("il8"))
-    act(lfl("NAT", 4, 8), lfl("BB", 0, 4), bias=col("il64"))
-    act(lfl("UN"), ap("au"), bias=col("bn"))
-    act(lfl("NATD"), lfl("BB", 0, 8), bias=col("il8"))
-    for n, v in SCALED:
-        act(ap(n), ap("ib16"), scale=v)
-
-    ts(ap("tf3"), ap("ti2"), 0.5, A.mult)
-    tt(ap("tf4"), ap("t8"), ap("qt"), A.add)
-    tt(lfl("RT"), ap("tf3"), ap("tf4"), A.add)
-    cp(ap("lu", LOFF["RT"], LOFF["YL"]), ap("lf", LOFF["RT"], LOFF["YL"]))
-    for h in (1, 0):
-        cp(ap("S", 512 * h, 512 * h + 512), ap("pd", 512 * h, 512 * h + 512))
+            act(I(v), I(1), scale=v)
+    iota(ap("kn", 0, 192), [[0, 192]], K2)
+    iota(ap("kn", 64, 128), [[0, 64]], K2 + C0)
+    iota(ap("kn", 192, 256), [[0, 64]], C0 + 32)
+    act(ap("if32"), I(1))
+    act(ap("nf32"), I(1), scale=-1.0)
     ts(ap("psw"), ap("dd", 0, 128), col("sw"), A.is_equal)
-    refresh(False)
-    ms(ap("xw", F, F + 16), 2.0 ** 61)
     ts(ap("bm"), ap("dd"), col("i15"), A.is_equal)
-    cp(ap("lu", LOFF["YL"], LTOT), ap("lf", LOFF["YL"], LTOT))
     ts(ap("bm3"), ap("dd"), col("i15"), A.is_equal, 3.0, A.mult)
-
+    ms(ap("xw", F, 4096), 2.0 ** 61)
+    ms(ap("xw", 4096 + F, XW), 2.0 ** 61)
+    iota(lst("DUP", buf="lf"), [[0, 3], [16, 2]], 0)
+    mklist("DUP", 0, 6, "i")
+    iota(lst("OM", buf="lf"), [[0, 10], [2, 2]], 0)
+    iota(lst("OM", 4, 6, "lf"), [[2, 2]], 4)
+    iota(lst("WV", buf="lf"), [[2, 2]], 8)
+    mklist("OM", 0, 22, "ib")
+    cp(lst("G1", 6, 7), col("i3"))
+    iota(lst("LS", buf="lf"), [[16, 14]], 0)
+    mklist("LS", 0, 14, "ls")
+    cp(lst("CB", 0, 2), lst("LS", 0, 2))
+    cp(lst("CB", 2, 3), col("cb"))
+    iota(ap("clp", 0, 8), [[15, 2], [0, 4]], 0)
+    iota(ap("clp", 8, 16), [[-30, 2], [0, 4]], 15)
+    iota(lst("NAT", buf="lf"), [[0, 2], [4, 2]], 0)
+    iota(lst("NATH", buf="lf"), [[-32, 2], [4, 2]], 32)
+    ts(ap("lu", LOFF["NAT"], LTOT), ap("lf", LOFF["NAT"], LTOT), col("nat"), A.add)
+    iota(ap("cpw"), [[0, 20], [1, 8]], 0)
+    iota(ap("cpw", 32, 64), [[0, 4], [-1, 8]], 15)
+    iota(ap("cpw", 128, 160), [[0, 4], [-1, 8]], 15)
+    iota(ap("cL"), [[0, 28], [E16, 8]], -2 * E16)
+    iota(ap("cL", 64, 96), [[0, 4], [E16, 8]], 2 * E16)
+    iota(ap("cL", 71, 96, 8), [[0, 4]], E16)
+    iota(ap("cL", 160, 224), [[0, 64]], -C0)
+    iota(ap("cpos"), [[0, 28], [E16, 8]], E16)
+    iota(ap("cpos", 160, 224), [[0, 64]], 0)
+    rec("g", lambda e: e.affine_select(T["rst8"][:], T["k4"][:, 0:224], [[0, 28], [1, 8]], A.is_gt, 0.0, 0, 0), [ap("rst8")], [ap("k4", 0, 224)])
+    for s in range(max(SQ)):
+        iota(ap("cq", 64 * s, 64 * s + 64), [[0, 64]], s * s)
+    cpit = ap("cG", 0, 64)
+    ones = lambda n: ap("k4", 0, n)
     xw = ap("xw")
 
-    def slot_a(s):
-        tt(ap("cmp", 1024 * s, 1024 * s + 1024), ind(xw, ap("off", 64 * s, 64 * s + 64)), ap("fa"), A.is_lt)
+    def halves(o, lo, l, r):
+        return [(ap(o, lo + 32 * h, lo + 32 * h + 32), l, r) for h in range(2)]
 
-    def gath_b(k):
-        act(ap("gb%d" % k), ind(xw, ap("off", 64 * (5 + k), 64 * (6 + k))))
+    def wl_offsets(c, src, lo):
+        M = "U" + c
+        mms([(ap(M, 600, 604), I(1), ap("cwl"))]
+            + [(ap(M, 600 + gp, 604, 2), ap("m%d%d" % (gp, e)), ap(src, lo + e, lo + 4, 2)) for gp in range(2) for e in range(2)])
+        ts(ap("oft" + c), ap(M, 600, 604), col("i"), A.add)
 
-    def diff_b(k, h):
-        group(ap("pd", 512 * h, 512 * h + 512), [(ap("ib16"), ap("fa", 512 * h, 512 * h + 512)),
-                                                 (ap("nib"), ap("gb%d" % k, 512 * h, 512 * h + 512))])
+    for ci, c in enumerate("ab"):
+        G0 = "G0" + c
+        pown = ap("msg0", 64, 80)
+        act(ap("S1", 512 * ci, 512 * ci + 512), ind(ap("sdi"), lst("ROT", 32 * ci, 32 * ci + 32)))
+        tt(ap("uu" + c), ap("msg0", 64 + 4 * ci, 68 + 4 * ci), ap("msg0", 72 + 4 * ci, 76 + 4 * ci), A.min)
+        ts(ap("zm" + c), ind(pown, lst(G0, 2, 6)), 8.0, A.is_ge, float(F), A.mult)
+        wl_offsets(c, "uu" + c, 0)
+        tr(ap("TT", 1024 * ci, 1024 * ci + 512), ap("S1", 512 * ci, 512 * ci + 512))
+        cp(ap("xg" + c), ind(ap("TT", 1024 * ci, 1024 * ci + 512), ap("oft" + c)))
+        tr(ap("y0" + c), ap("xg" + c))
+        tt(ap("ym" + c), ind(ap("y0" + c), lst("YZ")), ap("zm" + c), A.max)
+        tt(ap("msg0", 32 * ci, 32 * ci + 32), ap("ym" + c, 0, 32), ap("ym" + c, 32, 64), A.min)
+        send("0" + c)
+    for ci, c in enumerate("ab"):
+        X, U, R, G0 = "X" + c, "U" + c, "R" + c, "G0" + c
+        pown = ap("msg0", 64, 80)
+        act(ap("Xf" + c), ind(ap("sdi"), lst("XP", 36 * ci, 36 * ci + 36)), bias=-float(C0))
+        tt(ap("eq" + c), ind(pown, lst(G0, 0, 4)), cpit, A.is_equal)
+        act(ap("sk" + c, 0, 64), ap("eq" + c), scale=2.0, bias=-1.0)
+        mms([(ap(U, 64 * s, 64 * s + 64), I(C0), ap("sk" + c, 0, 64)) for s in range(9)], each=True)
+        tt(ap(X), ap(U, 0, 576), ap("Xf" + c), A.max)
+        ts(ap("val" + c), ap(X), C0 - 0.5, A.is_lt)
+        mms([(ap(R, 0, 64), I(-1), ap("val" + c, 64 * s, 64 * s + 64)) for s in range(9) if s != 1])
+        ts(ap(X, 64, 128), ap(R, 0, 64), float(C0), A.add)
+        mms([(ap("pd", 512 * ci + 64 * (7 - u), 512 * ci + 64 * (8 - u)), ap("psw"), ap("TT", 1024 * ci + 64 * u, 1024 * ci + 64 * u + 64))
+             for u in range(8)], each=True)
+        act(ap("TT", 1024 * ci + 512, 1024 * ci + 1024), ap("pd", 512 * ci, 512 * ci + 512))
+        act(ap("pb" + c, 160, 224), ind(pown, lst(G0, 2, 6)))
+        iota(ap("pb" + c, 288, 304), [[0, 16]], 0)
+        for r in (0, 3, 4):
+            iota(ap("cand" + c, 48 * r + 32, 48 * r + 48), [[0, 16]], 0)
 
-    def sign_b(k, h):
-        lo = 1024 * (5 + k) + 512 * h
-        act(ap("cmp", lo, lo + 512), ap("pd", 512 * h, 512 * h + 512), AF.Sign, bias=-2.0 ** -70)
+    def sow(t, ci):
+        c = "ab"[ci]
+        last = t == 2
+        now[:] = [2 * t + ci, 0]
+        X, U, R, M, pb = "X" + c, "U" + c, "R" + c, "U" + c, "pb" + c
+        m = "in%d" % t
+        s0 = (32 if t == 0 else 48) * ci
+        p0 = 64 + 4 * ci if t == 0 else s0 + 32
+        seeds = ap(m, s0, s0 + 32)
+        ach, ob, cap, pr = "ach%d" % min(t, 1) + c, "ob%d" % (t & 1) + c, "cap%d" % min(t, 1) + c, "pr%d" % t + c
+        hi = ap("hv" + c, 0, 32)
+        cand, cmp_, sig = "cand" + c, "cmp" + c, "sig" + c
+        e8, cnt, cc = ap(ob, 0, 32), ap(ob, 32, 64), ap(pr, 0, 32)
+        om = lambda lo, hi_: ap(ob, 64 + lo, 64 + hi_)
+        mms([(ap(U, 0, 256), I(1), ap3(X, 3, 18, 2, 0, 32)), (ap(U, 0, 256), I(-4096), ones(256))], stop=False)
+        if t == 0 and ci == 0:
+            arrive("p")
+        arrive("%d%s" % (t, c))
+        pw_ = ap(m, 64, 80) if t == 0 else ap(m, p0, p0 + 8)
+        tt(ap("G" + c), ind(pw_, lst("G0" + c if t == 0 else "G1", 0, 6)), ap("cG"), A.is_ge)
+        tt(ap("hv" + c), ap("G" + c, 0, 64), ap("G" + c, 32, 96), A.not_equal)
+        mms([(ap(U, 32 * k, 32 * k + 32), I(8192), hi) for k in range(8)], start=False)
+        ts(ap("offa" + c), seeds, float(F), A.min)
+        act(ap("fa" + c), ind(ap("xw", 0, F + 16), ap("offa" + c)))
+        tt(ap("W" + c), ap(U, 0, 256), ap3(X, 2, 18, 2, 0, 32), A.max)
+        ts(ap("off" + c), ap("W" + c, 32, 256), float(C0), A.add)
+        ts(ap(ach), ind(seeds, lst("DUP", 0, 4)), -float(C0), A.add)
+        act(ap("nh" + c), ind(seeds, lst("DUP", 0, 4)), AF.Sign, bias=0.5 - F)
+        lsum = [(ap("if32"), ap(m, p0, p0 + 4))] + [(I(-0.5), ap("nh" + c, k, 32, 8)) for k in range(8)]
+        mms([(ap(M, 576, 580), l, r) for l, r in lsum])
+        act(ap("sl" + c, 0, 4), ap(M, 576, 580), AF.Sign, bias=-11.5)
+        act(ap("sl" + c, 4, 8), ap(M, 576, 580))
+        mms([(ap(M, 580, 584), I(1), ap("sl" + c, 4, 8)), (ap(M, 580, 584), I(-8), ap("sl" + c, 0, 4))])
+        act(ap(pb, 288, 292), ap(M, 580, 584), bias=-4.0)
+        if not last:
+            wl_offsets(c, pb, 288)
+            mms([(ap(M, 584, 600), I(1), ap("clp"))]
+                + [(ap(M, 584 + 4 * k, 588 + 4 * k), I(v), ap(pb, 288, 292)) for k, v in enumerate((1, -1, -2, 2))])
+            act(ap3(cand, 0, 4, 3, 32, 40), ap(M, 584, 600))
+            act(ap("xg" + c), ind(ap("TT", 1024 * ci, 1024 * ci + 1024), ap("oft" + c)))
+            tr(ap("yb" + c), ap("xg" + c))
+        else:
+            act(ap(pb, 296, 300), ap(M, 580, 584), scale=-2.0, bias=23.0)
+        signs, p0_, c0_ = [((8, 8, -8), 64, 64), ((8, -8), 0, 0), ((8,), 0, 0)][t]
+        npw = 32 * len(signs)
+        mms([(ap(R, 224, 224 + npw), I(1), ap("cpw", c0_, c0_ + npw))]
+            + [(ap(R, 224 + 32 * k, 256 + 32 * k), I(v), hi) for k, v in enumerate(signs)])
+        act(ap(pb, p0_, p0_ + npw), ap(R, 224, 224 + npw))
+        mms([(ap(R, 352, 384), ap("nf32"), ap("W" + c, 0, 32)), (ap(R, 352, 384), I(4096), hi)])
+        act(cnt, ap(R, 352, 384), bias=float(C0))
+        act(e8, ap(R, 352, 384), AF.Relu, bias=float(C0 - 7))
+        if not last:
+            mms([(ap(R, 320, 352), I(1), cnt), (ap(R, 320, 352), I(1), ap("cpw", 0, 32))])
+            act(ap("st" + c), ap(R, 320, 352), AF.Sign, bias=-6.5)
+        lw_ = ap(pb, 288, 304)
+        if t == 0:
+            tt(om(0, 128), ind(lw_, lst("OM", 6, 14)), ap(pb, 96, 224), A.is_equal)
+        elif t == 1:
+            tt(om(0, 288), ind(lw_, lst("OM", 0, 18)), ap(pb, 0, 288), A.is_equal)
+        else:
+            tt(om(32, 64), ind(lw_, lst("OM", 0, 2)), ap(pb, 0, 32), A.is_equal)
 
-    def rows(out, lo, hi, b):
-        group(out, [(ap(b, 15 - i, 143 - i), ap("cmp", lo + i, hi, 16)) for i in range(16)])
+        def v_list(s):
+            k = tt(ap(cmp_, 512 * s, 512 * s + 512), ind(xw, ap("off" + c, 32 * s, 32 * s + 32)), ap("fa" + c), A.is_lt)
+            ops[k]["soft"] += turn[-LAG:][:1]
+            turn.append(k)
 
-    def thr(k0, n, src):
-        act(ap("sig", 64 * k0, 64 * (k0 + n)), src, AF.Sign, bias=-9.5)
+        def s_list(s, k):
+            act(ap("gb%d" % k), ind(xw, ap("off" + c, 32 * s, 32 * s + 32)))
+            mms([(ap("pd", 512 * k, 512 * k + 512), I(1), ap("fa" + c)), (ap("pd", 512 * k, 512 * k + 512), I(-1), ap("gb%d" % k))])
+            act(ap(cmp_, 512 * s, 512 * s + 512), ap("pd", 512 * k, 512 * k + 512), AF.Sign, bias=-2.0 ** -70)
 
-    def acc(k0, n, stop=False):
-        for k in range(k0, k0 + n):
-            mm(ap("pt_", 0, 64), ap("i8b"), ap("sig", 64 * k, 64 * k + 64), False, stop)
+        def rows(lo, s, n, b):
+            mms([(ap(R, lo, lo + 32 * n), ap(b, 15 - i, 143 - i), ap(cmp_, 512 * s + i, 512 * (s + n), 16)) for i in range(16)])
+
+        def place(slots, at):
+            nq = SQ[t]
+            q = []
+            for s in slots:
+                src = "cq" if s < nq else "val" + c
+                if q and q[-1][0] == src and at(s) == at(s - 1) + 64 and at(s) % 512:
+                    q[-1][2] = s + 1
+                else:
+                    q.append([src, s, s + 1])
+            q = [(ap(U, at(a), at(b - 1) + 64), I(K2), ap(src, 64 * a, 64 * b)) for src, a, b in q]
+            for s in slots:
+                o = ap(U, at(s), at(s) + 64)
+                q += [(o, I(1), ap(ach))]
+                if s < nq:
+                    q += [(o, I(K2), ap("ps" + c, 64, 128))] + ([(o, I(-2 * K2 * s), ap("ps" + c, 0, 64))] if s else [])
+            return q
+
+        now[1] = 0 if last else 0.5
+        mms([(ap(R, 416, 480), I(-1), ap(X, 64, 128)), (ap(R, 416, 480), I(16), ap("hv" + c))])
+        act(ap("ps" + c, 0, 64), ap(R, 416, 480), bias=float(C0))
+        if SQ[t]:
+            act(ap("ps" + c, 64, 128), ap(R, 416, 480), AF.Square, bias=float(C0))
+        for s in range(SQ[t], 8):
+            act(ap("val" + c, 64 * s, 64 * s + 64), ap("ps" + c, 0, 64), AF.Abs, bias=-float(s))
+        if not last:
+            N_ = ap(U, 0, 64)
+            mms(place(range(7), lambda s: 64 * s + 64)
+                + [(N_, I(-1), ap("ps" + c, 0, 64)), (N_, I(80), ap("hv" + c)), (N_, I(33), ap("nh" + c)), (N_, I(1), ap("kn", 192, 256))])
+            tt(ap(X, 64, 576), ap(U, 0, 512), ap(X, 64, 576), A.min)
+        now[1] = 0
+
+        if not last:
+            nl = 96 if t == 0 else 224
+            L0 = 608
+            lay = [(ap(M, L0, L0 + nl), I(1), ap("cL", 0, nl)), (ap(M, L0, L0 + 64), I(1), ap(ach)),
+                   (ap(M, L0 + 64, L0 + 96), I(1), ap(ach, 0, 32)), (ap(M, L0, L0 + 64), I(BIG), om(0, 64)),
+                   (ap(M, L0 + 64, L0 + 96), I(BIG), om(32, 64))]
+            lay += halves(M, L0, I(E16), cnt) + halves(M, L0, I(-65536), ap("st" + c))
+            if t == 1:
+                lay += [(ap(M, L0 + 96, L0 + 160), I(1), ap("ach0" + c)), (ap(M, L0 + 96, L0 + 160), I(BIG), om(96, 160)),
+                        (ap(M, L0 + 160, L0 + 224), I(BIG), om(96, 160))]
+                lay += halves(M, L0 + 96, I(E16), ap("ob0" + c, 32, 64)) + halves(M, L0 + 96, I(-E16), ap("pr0" + c, 0, 32))
+                lay += halves(M, L0 + 96, I(-65536), ap("st0" + c)) + halves(M, L0 + 96, I(-BIG), om(64, 96))
+                lay += halves(M, L0 + 160, I(F), ap("cap0" + c))
+            mms(lay)
+            act(ap("ly" + c, 0, nl), ap(M, L0, L0 + nl), AF.Relu, bias=float(C0 - BIG))
+            scan(ap("cs" + c, 0, nl), ap("rst8", 0, nl), ap("ly" + c, 0, nl))
+            tt(ap("sb" + c, 0, nl), ind(ap("cs" + c, 0, nl), lst("LS", 0, nl // 16)), ap("cpos", 0, nl), A.subtract)
+            act(ap("ea" + c, 0, nl), ap("sb" + c, 0, nl), AF.Abs)
+            kill = [(ap(M, L0, L0 + 64), I(F), om(64, 128) if t == 0 else om(160, 224))]
+            if t == 1:
+                kill += [(ap(M, L0, L0 + 64), I(F), om(224, 288)), (ap(M, L0, L0 + 64), ap("if32"), ap("ea" + c, 160, 224))]
+            mms(kill + [(ap(M, L0 + 32 * z, L0 + 32 * z + 32), ap("if32"), ap3("yb" + c, 0, 4, 1, 8 * z, 8 * z + 8)) for z in range(2)]
+                + [(ap(M, L0 + 64, L0 + 96), I(F), ones(32))])
+        else:
+            mms(place(range(8), lambda s: (64 * s + 128) % 576) + [(ap(U, 64, 128), I(1), ones(64))])
+            tt(ap(X), ap(U, 0, 576), ap(X), A.min)
+            nat = [(ap(U, 0, 512), I(C0), ones(512))]
+            nat += [(ap3(U, 0, 14, 1, 4 * k, 4 * k + 4), I(1), ap3(X, 4, 18, 1, k, 32, 8)) for k in range(8)]
+            nat += [(ap3(U, 14, 16, 1, 4 * k, 4 * k + 4), I(1), ap3(X, 0, 2, 1, k, 32, 8)) for k in range(8)]
+            mms(nat, stop=False)
+            act(ap("hmn" + c), ind(ap("hv" + c), lst("NATH")), scale=float(F))
+            act(ap("aq" + c), ind(seeds, lst("NAT")), bias=float(F))
+            tt(om(0, 32), ind(lw_, lst("WV")), om(32, 64), A.mult)
+        ns = ON_S[t, ci]
+        nv = 7 - ns
+        v_list(0)
+        s_list(nv, 0)
+        v_list(1)
+        if not last:
+            tt(ap3(cand, 0, 3, 1, 0, 32), ap(M, L0, L0 + 96), ap("ea" + c, 0, 96), A.min)
+            if t == 1:
+                tt(ap3(cand, 0, 2, 1, 0, 32), ap3(cand, 0, 2, 1, 0, 32), ap("ea" + c, 96, 160), A.min)
+            if ED[t]:
+                mms([(ap(M, 864, 928), ap("if32"), ap3(cand, 1, 3, 1, 0, 32)), (ap(M, 864, 928), ap("nf32"), ap3(cand, 0, 2, 1, 0, 32))])
+                act(ap3(cand, 3, 5, 1, 0, 32), ap(M, 864, 928))
+            else:
+                tt(ap3(cand, 3, 5, 1, 0, 32), ap3(cand, 1, 3, 1, 0, 32), ap3(cand, 0, 2, 1, 0, 32), A.subtract)
+        for k in range(1, ns):
+            s_list(nv + k, k & 1)
+        for s in range(2, nv - 2):
+            v_list(s)
+        rows(0, 0, nv - 2, "bm")
+        rows(32 * (nv - 2), nv, ns, "bm3")
+        act(ap(sig, 0, 160), ap(R, 0, 160), AF.Sign, bias=-9.5)
+        Y = ap(M, 832, 864)
+        mms([(Y, I(-1), cnt), (Y, I(33), e8), (Y, I(-33), ap("nh" + c, 0, 32))]
+            + [(Y, I(1), ap(sig, 32 * k, 32 * k + 32)) for k in range(5)], stop=False)
+        v_list(nv - 2)
+        v_list(nv - 1)
+        rows(160, nv - 2, 2, "bm")
+        act(ap(sig, 160, 224), ap(R, 160, 224), AF.Sign, bias=-9.5)
+        mms([(Y, I(1), ap(sig, 32 * k, 32 * k + 32)) for k in (5, 6)], start=False)
+        ts(ap(cap), Y, 26.5, A.is_gt)
+        if not last:
+            mo = "msg%d" % (t + 1)
+            o0 = 48 * ci
+            tt(ap(pr), ind(ap(cap), lst("DUP")), ap(ob, 32, 128), A.mult)
+            scan(ap("cs2" + c), ap("rst8", 0, 64), ap(pr, 32, 96))
+            tt(ap("r1" + c), ind(ap("cs2" + c, 32, 64), lst("CB", 0, 3)), ap(cand, 192, 240), A.mult)
+            tt(ap("r2" + c), ap("r1" + c), ap(cand, 144, 192), A.add)
+            tt(ap("r1" + c), ind(ap("cs2" + c, 0, 32), lst("CB", 0, 3)), ap("r2" + c), A.mult)
+            tt(ap(mo, o0, o0 + 40), ap("r1" + c, 0, 40), ap(cand, 0, 40), A.add)
+            send("%d%s" % (t + 1, c))
+            now[1] = 1
+            pnew = ap(mo, o0 + 32, o0 + 40)
+            tt(ap("eq" + c), ind(pnew, lst("G1", 0, 4)), cpit, A.is_equal)
+            mms([(ap(R, 352 + 64 * k, 416 + 64 * k), l, r) for k in range(2) for l, r in ((I(-1), ap("hv" + c)), (I(2 - 3 * k), ap("eq" + c)))]
+                + halves(R, 352, I(1), ap(cap)) + halves(R, 416, I(1), ap(cap)))
+            act(ap("sk" + c), ap(R, 352, 480), AF.Sign, bias=-0.5)
+            mms([(ap(U, 64 * s, 64 * s + 64), I(C0), ap("sk" + c, 0, 64)) for s in range(9)], each=True)
+            tt(ap(X), ap(U, 0, 576), ap(X), A.max)
+            sm = ap("sk" + c, 64, 128)
+            mms([(ap(U, 0, 192), I(1), ap("kn", 0, 192))] + place([7], lambda s: 0)
+                + [(ap(U, 0, 64), I(K2), ap("sk" + c, 0, 64)), (ap(U, 64, 128), I(-K2), sm), (ap(U, 128, 192), I(-K2), sm),
+                   (ap(U, 64, 128), I(1), ap("nh" + c)), (ap(U, 128, 192), I(1), ap(ach))])
+            tt(ap(X, 0, 192), ap(U, 0, 192), ap(X, 0, 192), A.min)
+            if t == 0:
+                act(ap(pb, 224, 304), ind(pnew, lst("G1", 2, 7)))
+                mms([(ap(R, 480, 512), I(1), cnt), (ap(R, 480, 512), I(-1), cc), (ap(R, 480, 512), I(1), ap("cpw", 0, 32))])
+                act(ap("st0" + c), ap(R, 480, 512), AF.Sign, bias=-6.5)
+            else:
+                mms([(ap(R, 480, 484), I(1), ap("pr%d" % r + c, k, 32, 8)) for r in range(2) for k in range(8)])
+                act(ap("sc" + c), ap(R, 480, 484))
+        else:
+            tt(ap("kmn" + c), ind(ap(cap), lst("NAT")), ap("hmn" + c), A.mult)
+            mms([(ap(U, 64 * s, 64 * s + 64), I(1), ap("kmn" + c)) for s in range(8)], start=False)
+            if JY[ci]:
+                act(ap("Rf" + c), ap(U, 0, 512), AF.Relu, scale=-1.0, bias=float(F))
+                act(ap3("yo", 0, 128, 1, 4 * ci, 4 * ci + 4), ap("Rf" + c), scale=-1.0, bias=float(F))
+            else:
+                ts(ap3("yo", 0, 128, 1, 4 * ci, 4 * ci + 4), ap(U, 0, 512), float(F), A.min)
+            tt(ap("rr" + c), ap("aq" + c), ap("kmn" + c), A.subtract)
+            tt(ap3("yo", 0, 16, 1, 4 * ci, 4 * ci + 4), ap3("yo", 0, 16, 1, 4 * ci, 4 * ci + 4), ap("rr" + c), A.min)
+            tt(ap(pr), ind(ap(cap), lst("DUP", 0, 4)), ap(ob, 32, 96), A.mult)
+            mms([(ap(R, 256, 264), I(1), ap(pr, k, 64, 8)) for k in range(8)]
+                + [(ap(R, 256, 260), I(1), ap("sc" + c)), (ap(R, 260, 264), I(1), ap(pb, 288, 292))])
+            act(ap3("o8", 0, 2, 1, 4 * ci, 4 * ci + 4), ap(R, 256, 264))
 
     for t in range(3):
-        last = t == 2
-        m = "in%d" % t
-        arrive("pqr"[t])
-        arrive(str(t))
-        tt(ap("t2"), ind(ap(m, 72, 80), lst("BB", 0, 8)), ap("ct2"), A.add)
-        ts(ap("offa"), ap(m, 0, 64), float(F), A.min)
-        act(ap("fa"), ind(xw, ap("offa")))
-        ts(ap("hl8"), ap("t2"), 4096, A.bitwise_and)
-        ts(ap("mf"), ap(m, 0, 64), float(F), A.min)
-        cp(ap("hlb"), ap("hl8", 64, 128))
-        mms([(ap("pl_", 64 * s, 64 * s + 64), ap("ib16"), ap("hlb"), False, s == 7) for s in range(8)])
-        tt(ap("fs"), ind(ap("hl8", 0, 64), lst("DUP")), ap("S", 512, 1024), A.add)
-        tt(ap("w8"), ap("fs"), ap("pl_"), A.min)
-        ts(ap("off"), ap("w8", 0, 448), float(F), A.min)
-        act(ap("nh"), ap(m, 0, 64), AF.Sign, bias=0.5 - F)
-        lsum = [(ap("if32"), ap(m, 64, 72))] + [(ap("ih"), ap("nh", k, 64, 8)) for k in range(8)]
-        group(ap("pc_", 128, 136), lsum)
-        if not last:
-            act(ap("TT", 1024, 1536), ap("pd", 0, 512))
-        act(ap("sl"), ap("pc_", 128, 136), AF.Sign, bias=-3.5)
-        group(ap("pc_", 136, 144), lsum + [(ap("n8"), ap("sl"))])
-        if not last:
-            act(ap("TT", 1536, 2048), ap("pd", 512, 1024))
-        act(ap("val"), ap("w8"), AF.Sign, scale=-1.0, bias=F - 0.5)
-        cnt = [(ap("ih" if s < 7 else "n75"), ap("val", 64 * s, 64 * s + 64)) for s in range(8)]
-        group(ap("pb_", 256, 320), cnt)
-        if not last:
-            group(ap("pb_", 320, 384), cnt + [(ap("ib16"), ap("cm"))])
-        act(ap("yb", 136, 144), ap("pc_", 136, 144), scale=-1.0, bias=11.0)
-        act(ap("yb", 128, 136), ap("pc_", 136, 144), bias=4.0)
-        act(ap("yb", 160, 168), ap("pc_", 136, 144), scale=512.0, bias=2048.0)
-        if not last:
-            act(ap("yb", 168, 176), ap("pc_", 136, 144), scale=-512.0, bias=5632.0)
-            wl_offsets("yb", 136)
-        slot_a(0)
-        act(ap("ct"), ap("pb_", 256, 320), bias=-4.0)
-        nat = [(ap("ib16"), ap("crn")), (ap("if32"), ap("mf", 0, 64)), (ap("i8k"), ap("ct"))]
-        if not last:
-            act(ap("st"), ap("pb_", 320, 384), AF.Sign, bias=-10.5)
-            group(ap("pa_", 256, 320), [(ap("ib16"), ap("cr", 0, 64)), (ap("if32"), ap("mf", 0, 64)), (ap("i8k"), ap("ct")),
-                                        (ap("n32k"), ap("st"))])
-            group(ap("pa_", 320, 384), [(ap("ib16"), ap("cr", 64, 128)), (ap("if32"), ap("mf", 0, 64))])
-            group(ap("pa_", 384, 448), nat)
-            act(ap("dc"), ap("pb_", 256, 320), scale=float(E8), bias=-4.0 * E8)
-        else:
-            group(ap("pa_", 256, 320), nat)
-        act(ap("cabs"), ap("pb_", 256, 320), AF.Abs, bias=-4.0)
-        gath_b(0)
-        group(ap("pt_", 0, 64), [(ap("n8"), ap("val", 64 * s, 64 * s + 64)) for s in (1, 3, 5)]
-              + [(ap("i64b"), ap("val", 448, 512)), (ap("n128"), ap("nh"))], stop=False)
-        diff_b(0, 0)
-        diff_b(0, 1)
-        tt(ap("key"), ap("hl8"), ap("ckey"), A.add)
-        if not last:
-            act(ap("code_"), ap("pa_", 256, 448))
-            cp(ap("oft"), ap("pm_", 0, 8))
-            tt(ap("om"), ind(ap("yb", 160, 168), lst("BB", 0, 8)), ap("key"), A.is_equal)
-            act(ap("xg"), ind(ap("TT"), ap("oft")))
-        else:
-            act(ap("code_", 0, 64), ap("pa_", 256, 320))
-            ts(ap("hn1"), ind(ap("hl8"), lst("NAT")), 1.0 / 4096, A.mult)
-            tt(ap("om", 0, 64), ind(ap("yb", 160, 168), lst("BB", 0, 4)), ap("key", 0, 64), A.is_equal)
-        gath_b(1)
-        slot_a(1)
-        if last:
-            tt(ap("vq"), ind(ap("code_", 0, 64), lst("NATD")), ap("hn1"), A.mult)
-        sign_b(0, 0)
-        sign_b(0, 1)
-        diff_b(1, 0)
-        diff_b(1, 1)
-        rows(ap("pa_", 0, 128), 0, 2048, "bm")
-        if not last:
-            tt(ap("pa", 0, 64), ap("code_", 64, 128), ap("om", 64, 128), A.mult)
-            tt(ap("pa", 80, 144), ap("code_", 0, 64), ap("om", 64, 128), A.mult)
-            tt(ap("pa", 160, 224), ap("code_", 0, 64), ap("om", 0, 64), A.mult)
-            tr(ap("yb", 0, 128), ap("xg"))
-            scan(ap("cs3"), ap("rst8"), ap("pa"))
-        else:
-            for s in range(8):
-                act(ap("pm_" if s >= 4 else "pl_", 128 * (s % 4), 128 * (s % 4) + 128), ap("vq"), AF.Abs, bias=-float(E8 * (s + 1)))
-        sign_b(1, 0)
-        sign_b(1, 1)
-        thr(0, 2, ap("pa_", 0, 128))
-        slot_a(2)
-        if last:
-            for h, bank in enumerate(("pl_", "pm_")):
-                tt(ap("S1", 512 * h, 512 * h + 512), ap("SC", 512 * h, 512 * h + 512), ap(bank), A.min)
-                mm(ap(bank), ap("if32"), ap("S1", 512 * h, 512 * h + 512), True, False)
-        rows(ap("pb_", 0, 128), 5120, 7168, "bm3")
-        acc(0, 2)
-        if not last:
-            for pos in range(8):
-                act(ap("ea", pos, 240, 8), ap("cs3", 7, 240, 8), AF.Abs, bias=-float(E8 * (pos + 1)))
-        rows(ap("pa_", 128, 192), 2048, 3072, "bm")
-        thr(4, 2, ap("pb_", 0, 128))
-        thr(2, 1, ap("pa_", 128, 192))
-        slot_a(3)
-        acc(4, 2)
-        acc(2, 1)
-        rows(ap("pb_", 128, 192), 3072, 4096, "bm")
-        thr(3, 1, ap("pb_", 128, 192))
-        slot_a(4)
-        group(ap("pt_", 0, 64), [(ap("bm", 15 - i, 143 - i), ap("cmp", 4096 + i, 5120, 16)) for i in range(16)], False, False)
-        acc(3, 1, True)
-        if not last:
-            tt(ap("app"), ind(ap("yb"), lst("YL", 0, 15)), ap("ea"), A.min)
-            group(ap("pm_", 256, 416), [(ap("if32"), ap("app", 0, 160)), (ap("nf32"), ap("app", 80, 240))])
-            act(ap("ed"), ap("pm_", 256, 416))
-            preload(True)
-        else:
-            ts(ap("aq"), ind(ap("mf", 0, 64), lst("NATD")), float(F), A.add)
-            ts(ap("hn3"), ap("hn1"), float(F), A.mult)
-            tt(ap("w8s", 0, 8), ap("yb", 128, 136), ap("yb", 136, 144), A.subtract)
-        ts(ap("cap"), ap("pt_", 0, 64), 49.5, A.is_gt)
-        if not last:
-            tt(ap("prod"), ind(ap("cap"), lst("DUP", 0, 8)), ap("om"), A.mult)
-            scan(ap("cs2"), ap("rst8", 0, 128), ap("prod"))
-            mo = "msg%d" % (t + 1)
-            tt(ap("r3", 64, 80), ind(ap("cs2", 0, 64), lst("CB", 4, 5)), ap("ed", 144, 160), A.mult)
-            tt(ap("r1", 0, 64), ind(ap("cs2", 64, 128), lst("CB", 0, 4)), ap("ed", 0, 64), A.mult)
-            tt(ap(mo, 64, 80), ap("r3", 64, 80), ap("app", 224, 240), A.add)
-            send("pqr"[t + 1])
-            tt(ap("r2", 0, 64), ap("r1", 0, 64), ap("ed", 80, 144), A.add)
-            tt(ap("r3", 0, 64), ind(ap("cs2", 0, 64), lst("CB", 0, 4)), ap("r2", 0, 64), A.mult)
-            tt(ap(mo, 0, 64), ap("r3", 0, 64), ap("app", 160, 224), A.add)
-            send(str(t + 1))
-            tt(ap("vw1"), ap("cap"), ap("dc"), A.mult)
-            tt(ap("ncl"), ind(ap("msg%d" % (t + 1), 64, 72), lst("BB", 0, 8)), ap("cpit"), A.not_equal)
-            tt(ap("vw"), ap("code_", 128, 192), ap("vw1"), A.subtract)
-            tt(ap("kq"), ind(ap("cap"), lst("DUP", 0, 8)), ap("hl8"), A.mult)
-            tt(ap("vq"), ind(ap("vw"), lst("DUP", 0, 8)), ap("hl8"), A.mult)
-            for h in (1, 0):
-                tt(ap("vq2", 64 * h, 64 * h + 64), ap("vq", 64 * h, 64 * h + 64), ap("ncl", 64 * h, 64 * h + 64), A.mult)
-            tt(ap("ce0"), ap("kq"), ap("ncl"), A.subtract)
-            for h in (1, 0):
-                for s in range(8):
-                    act(ap("ins", 512 * h + 64 * s, 512 * h + 64 * s + 64), ap("vq2", 64 * h, 64 * h + 64), AF.Abs, scale=1.0 / 4096,
-                        bias=-float(E8 * (s + 1)))
-            clear()
-            if t == 0:
-                tt(ap("sc"), ap("cap"), ap("cabs"), A.mult)
-            else:
-                tt(ap("sct"), ap("cap"), ap("cabs"), A.mult)
-                tt(ap("sc"), ap("sc"), ap("sct"), A.add)
-            for h in (1, 0):
-                tt(ap("S", 512 * h, 512 * h + 512), ap("ins", 512 * h, 512 * h + 512), ap("pd", 512 * h, 512 * h + 512), A.min)
-            refresh(t == 1)
-        else:
-            tt(ap("cape"), ind(ap("cap"), lst("NATD")), ap("hn3"), A.mult)
-            for bank in ("pm_", "pl_"):
-                mms([(ap(bank, 128 * s, 128 * s + 128), ap("ib16"), ap("cape"), False, s == 3) for s in range(4)])
-            ts(ap("yo", 512, 1024), ap("pm_"), float(F), A.min)
-            dma("y", hbm(T.ys[:, 512:1024]), ap("yo", 512, 1024))
-            tt(ap("rr"), ap("aq"), ap("cape"), A.subtract)
-            ts(ap("yo", 0, 512), ap("pl_"), float(F), A.min)
-            tt(ap("prod", 0, 64), ap("cap"), ap("om", 0, 64), A.mult)
-            tt(ap("yo", 0, 128), ap("yo", 0, 128), ap("rr"), A.min)
-            dma("s", hbm(T.ys[:, 0:512]), ap("yo", 0, 512))
-            tt(ap("sct"), ap("cap"), ap("cabs"), A.mult)
-            scan(ap("cs2", 0, 64), ap("rst8", 0, 64), ap("prod", 0, 64))
-            tt(ap("sc"), ap("sc"), ap("sct"), A.add)
-            tt(ap("w8s", 8, 16), ap("w8s", 0, 8), ap("cs2", 7, 64, 8), A.mult)
-            scan(ap("scs"), ap("rst8", 0, 64), ap("sc"))
-            tt(ap("o8", 0, 8), ap("w8s", 8, 16), ap("yb", 136, 144), A.add)
-            dma("s", hbm(T.yp[:]), ap("o8", 0, 8))
-            cp(ap("o8", 8, 16), ap("scs", 7, 64, 8))
-            dma("y", hbm(T.yc[:]), ap("o8", 8, 16))
+        for ci in range(2):
+            sow(t, ci)
+    dma("y", hbm(T.ys[:, 512:1024]), ap("yo", 512, 1024))
+    dma("s", hbm(T.ys[:, 0:512]), ap("yo", 0, 512))
+    dma("s", hbm(T.yp[:]), ap("o8", 8, 16))
+    dma("y", hbm(T.yc[:]), ap("o8", 0, 8))
     _emit(g, T, ops)

import math
import numpy as np
from concourse.mybir import AluOpType, ActivationFunctionType

A = AluOpType
AF = ActivationFunctionType
F, C0, K2, E16, BIG = 3072, 1536, 4096, 16384, 2 ** 20
XW = 4096 + F + 16
MSGS = [("p", "0", 64, 80), ("0a", "0", 0, 32), ("0b", "0", 32, 64), ("1a", "1", 0, 40), ("1b", "1", 48, 88),
        ("2a", "2", 0, 40), ("2b", "2", 48, 88)]
WAKE, TRIP, PE = 110.0, 5300.0, 0.545
FIX, MMFIX, COOL, LAG, WEIGHT = 1.0, 7.0, 150.0, 1, 2.0
EARLY, ALL, PAIRS, STARTS = 0.05, 1e-4, 0.4, 1
SQ, ED, JQ, JY = (2, 2, 2), (0, 0), (0, 0), (1, 0)
GC = ((1.4, 0.84), (1.9, 1.16))
MOVES, TEMP, SEED, SHAKES, JOLT, MIX = 200000, 60.0, 1, 200, 1500.0, 0.7

LISTS = [("ROT", 64), ("G0a", 6), ("G0b", 6), ("G1", 8), ("YZ", 4), ("XP", 72), ("DUP", 6), ("OM", 20), ("WV", 2), ("LS", 14),
         ("CB", 4), ("NAT", 4), ("NATH", 4)]
LOFF = {}
_o = 0
for _n, _k in LISTS:
    LOFF[_n] = _o
    _o += _k
LTOT = _o
COLS = ["ib", "il", "i", "gb", "i3", "i2", "sgb", "ib15", "il1920", "sw", "i15", "gb64", "ngb64", "xp", "yz", "ls", "cb", "nat"]
SCALES = [1.0, -1.0, -2.0, -0.5, 2.0, 8.0, -8.0, 16.0, 33.0, -33.0, 80.0, -4096.0, 1536.0, 3072.0, 4096.0, 8192.0, 16384.0, -16384.0,
          -65536.0, float(BIG), -float(BIG)] + [-2.0 * K2 * s for s in (1, 3, 4, 5, 6, 7)]
LATE = [80.0, -float(BIG), 2.0, 33.0] + [-2.0 * K2 * s for s in range(1, 8)]
ON_V = [-1.0, 8192.0, -4096.0, 1536.0, -0.5]
ON_S = {(0, 0): 2, (0, 1): 2, (1, 0): 3, (1, 1): 2, (2, 0): 2, (2, 1): 2}

f32, bf, i32, u16, f16 = "float32", "bfloat16", "int32", "uint16", "float16"
SB_ = {
    "xw": ([XW], bf), "sdi": ([1024], i32), "acti": ([8], i32), "S1": ([1024], f32), "TT": ([2048], f32),
    "lf": ([LTOT], f32), "lu": ([LTOT], u16), "pi": ([8], i32), "ibits": ([8], i32), "col": ([32], f32),
    "su": ([64], f32), "qt": ([64], f32), "ti": ([64], i32), "ti2": ([64], i32), "tf": ([64], f32), "tf2": ([64], f32),
    "dd": ([144], f32), "idm": ([128 * len(SCALES)], bf), "mwl": ([512], bf), "if32": ([128], f32), "nf32": ([128], f32),
    "psw": ([128], f32), "bm": ([144], bf), "bm3": ([144], bf),
    "cG": ([96], f32), "zero": ([128], bf), "cpw": ([160], bf), "kn": ([256], bf), "cL": ([224], bf), "cpos": ([224], f32),
    "cwl": ([4], bf), "k4": ([512], bf), "cq": ([512], bf), "clp": ([16], bf), "rst8": ([224], bf),
    "gb0": ([512], bf), "gb1": ([512], bf), "yo": ([128, 8], f32), "o8": ([2, 8], f32),
    "msg0": ([80], f32), "msg1": ([96], f32), "msg2": ([96], f32), "in0": ([80], f32), "in1": ([96], f32), "in2": ([96], f32),
}
PER = {
    "X": ([18, 32], f16), "Xf": ([576], f32), "val": ([576], bf), "uu": ([4], bf), "zm": ([64], f32), "y0": ([64], f32), "ym": ([64], f32),
    "G": ([96], bf), "hv": ([64], bf), "W": ([256], f32), "off": ([224], u16), "offa": ([32], u16), "fa": ([512], bf),
    "ach0": ([64], f16), "ach1": ([64], f16), "nh": ([64], bf), "sl": ([8], bf), "pb": ([336], bf), "ob0": ([224], bf), "ob1": ([384], bf),
    "st": ([32], bf), "Rf": ([16, 32], f32), "st0": ([32], bf), "oft": ([4], u16), "xg": ([64], f32), "yb": ([4, 16], f32),
    "ly": ([224], f32), "cs": ([224], f32), "sb": ([224], f32), "ea": ([224], f32), "cand": ([5, 48], f32),
    "cmp": ([3584], bf), "sig": ([224], bf), "cap0": ([32], bf), "cap1": ([32], bf), "pr0": ([96], bf), "pr1": ([96], bf),
    "pr2": ([64], bf), "sc": ([4], bf), "cs2": ([64], f32), "r1": ([48], f32), "r2": ([48], f32),
    "eq": ([64], bf), "sk": ([128], bf), "ps": ([128], bf), "hmn": ([64], bf), "kmn": ([64], bf), "aq": ([64], f32), "rr": ([64], f32),
}
POOL = {}
ALIAS = {}
OWN = ("X", "Rf", "yb", "cand", "cmp", "pb", "cs", "cs2", "cap0", "cap1", "hv", "eq", "y0", "off", "offa", "oft", "fa")
for _c in "ab":
    for _n, (_s, _d) in PER.items():
        if _n in OWN:
            SB_[_n + _c] = (_s, _d)
        else:
            _p = "pool" + _d + _c
            _w = POOL.get(_p, ([0], _d))[0][0]
            ALIAS[_n + _c] = (_p, _w, _s[0])
            POOL[_p] = ([_w + (_s[0] + 15) // 16 * 16], _d)
SB_.update(POOL)
for _k in range(4):
    ALIAS["m%d%d" % (_k // 2, _k % 2)] = ("mwl", 128 * _k, 128)
PS_ = {"pd": [1024], "Ua": [32, 32], "Ub": [32, 32], "Ra": [512], "Rb": [512]}
SCRATCH = {}
for _n, (_s, _d) in SB_.items():
    SCRATCH[_n] = ("sbuf", [128] + _s, _d)
for _n, _s in PS_.items():
    SCRATCH[_n] = ("psum", [128] + _s, "float32")
SEMAPHORES = ["ev", "es", "et", "eg", "sent"] + ["arr" + m[0] for m in MSGS] + ["dm%d" % k for k in range(8)]
_PLAN = {}


def _relay(src, dst, topo):
    if topo.may_write(src, dst):
        return None
    ok = [c for c in topo.cores_of(src) if c != src and topo.may_write(c, dst)]
    near = [c for c in ok if topo.die(c) == topo.die(src)]
    return (near or ok)[0]


def _deps(ops):
    seen = {}
    deps = []
    for k, o in enumerate(ops):
        d = set(o["after"])
        for kind, rs in (("r", o["r"]), ("w", o["w"])):
            for (n, lo, hi, st) in rs:
                for (j, kind2, lo2, hi2, st2) in seen.get(n, []):
                    if (kind == "w" or kind2 == "w") and lo < hi2 and lo2 < hi and not (st == st2 and (lo - lo2) % st):
                        d.add(j)
        for b in o["b"]:
            for j in seen.get(b, []):
                if ops[j]["q"] != o["q"] or ops[j]["open"] or o["open"]:
                    d.add(j)
        for kind, rs in (("r", o["r"]), ("w", o["w"])):
            for (n, lo, hi, st) in rs:
                seen.setdefault(n, []).append((k, kind, lo, hi, st))
        for b in set(o["b"]):
            seen.setdefault(b, []).append(k)
        d.discard(k)
        deps.append(sorted(d))
    return deps


def _order(ops, deps):
    n = len(ops)
    reach = []
    red = []
    for k in range(n):
        m = 0
        keep = []
        for j in reversed(deps[k]):
            if not m >> j & 1:
                keep.append(j)
                m |= reach[j] | 1 << j
        reach.append(m)
        red.append(keep)
    succ = [[] for _ in range(n)]
    for k in range(n):
        for j in red[k]:
            succ[j].append(k)
    qi = ["vstgyx".index(o["q"]) for o in ops]
    c0 = [o["c"][0] for o in ops]
    c1 = [o["c"][1] for o in ops]
    lat = [o["lat"] + WAKE for o in ops]
    tail = [0.0] * n
    for k in range(n - 1, -1, -1):
        tail[k] = c0[k] + lat[k] + max([tail[j] for j in succ[k]] or [0.0])
    cm = [MIX * a + (1.0 - MIX) * b for a, b in zip(c0, c1)]

    def fit(seq, back):
        at = [0.0] * n
        busy = [[] for _ in range(6)]
        for k in seq:
            if back:
                a = max([at[j] + cm[j] for j in succ[k]] or [0.0]) + lat[k]
            else:
                a = max([at[j] + cm[j] + lat[j] for j in red[k]] or [0.0])
            row = busy[qi[k]]
            x = len(row)
            while x and row[x - 1][1] > a:
                x -= 1
            while x < len(row) and row[x][0] < a + cm[k]:
                a = max(a, row[x][1])
                x += 1
            row.insert(x, (a, a + cm[k]))
            at[k] = a
        return at, max(at[k] + cm[k] + (0.0 if back else lat[k]) for k in range(n))

    def pack(seq):
        at, best = fit(seq, False)
        while True:
            bt, _ = fit(sorted(range(n), key=lambda k: (-at[k] - cm[k] - lat[k], -k)), True)
            ft, s = fit(sorted(range(n), key=lambda k: (-bt[k] - cm[k], k)), False)
            if s >= best - 1.0:
                return at, best
            at, best = ft, s

    rng = np.random.default_rng(SEED)
    at, best = min(pack(list(range(n))), pack(sorted(range(n), key=lambda k: (-tail[k], k))), key=lambda x: x[1])
    now, cur = at, best
    for it in range(SHAKES):
        mid, wide = rng.random() * cur, (0.05 + 0.3 * rng.random()) * cur
        jolt = (rng.random(n) * JOLT * (0.2 + rng.random())).tolist()
        key = [now[k] + (jolt[k] if abs(now[k] - mid) < wide else 0.0) for k in range(n)]
        for k in range(n):
            for j in red[k]:
                key[k] = max(key[k], key[j] + 1e-3)
        new, s = pack(sorted(range(n), key=lambda k: key[k]))
        if s <= cur + COOL * (1.0 - it / SHAKES) * rng.exponential():
            now, cur = new, s
            if s < best:
                at, best = new, s
    order = sorted(range(n), key=lambda k: (at[k], k))

    def dispatch(slack, lag, noise):
        turn = [o["turn"][0] + lag * o["turn"][1] for o in ops]
        for k in range(n - 1, -1, -1):
            turn[k] = min([turn[k]] + [turn[j] for j in succ[k]])
        key = [(turn[k], -tail[k] - x) for k, x in enumerate((noise * rng.random(n)).tolist())]
        left = [len(x) for x in red]
        at = [0.0] * n
        free = [0.0] * 6
        ready = [k for k in range(n) if not left[k]]
        out = []
        while ready:
            k = min(ready, key=lambda x: max(at[x], free[qi[x]]))
            first = max(at[k], free[qi[k]]) + slack
            k = min((x for x in ready if qi[x] == qi[k] and at[x] <= first), key=lambda x: key[x])
            ready.remove(k)
            out.append(k)
            free[qi[k]] = max(at[k], free[qi[k]]) + cm[k]
            for j in succ[k]:
                at[j] = max(at[j], free[qi[k]] + lat[k])
                left[j] -= 1
                if not left[j]:
                    ready.append(j)
        return out

    sent = [k for k in range(n) if ops[k]["own"]]
    item = [(qi[k], red[k], c0[k], c1[k], lat[k]) for k in range(n)]

    def span(order, p=0, d=None):
        f0 = [0.0] * 6
        f1 = [0.0] * 6
        d0 = list(d[0]) if p else [0.0] * n
        d1 = list(d[1]) if p else [0.0] * n
        left = set(range(5))
        x = p
        while x and left:
            x -= 1
            k = order[x]
            if qi[k] in left:
                left.discard(qi[k])
                f0[qi[k]] = d0[k] - lat[k]
                f1[qi[k]] = d1[k] - lat[k]
        for k in order[p:]:
            q, pre, x, y, z = item[k]
            a = f0[q]
            b = f1[q]
            for j in pre:
                if d0[j] > a:
                    a = d0[j]
                if d1[j] > b:
                    b = d1[j]
            a += x
            b += y
            f0[q] = a
            f1[q] = b
            d0[k] = a + z
            d1[k] = b + z
        return MIX * max(d0) + (1.0 - MIX) * max(d1) + ALL * sum(d0) + EARLY * sum([d0[k] for k in sent]), (d0, d1)

    def held(order, d, c):
        before = {}
        prev = [-1] * n
        for k in order:
            prev[k] = before.get(qi[k], -1)
            before[qi[k]] = k
        k = max(range(n), key=lambda x: d[x])
        out = []
        while True:
            start = d[k] - lat[k] - c[k]
            j = max(red[k], key=lambda x: d[x]) if red[k] else -1
            if j >= 0 and d[j] >= start - 1e-6:
                k = j
            elif prev[k] >= 0:
                if not reach[k] >> prev[k] & 1:
                    out.append((prev[k], k))
                k = prev[k]
            else:
                return out

    def anneal(order, moves, temp):
        cur, d = span(order)
        best, keep, fresh = cur, order, 0
        pairs = held(order, d[0], c0) + held(order, d[1], c1)
        draw = rng.random((moves, 4)).tolist()
        for it, (u, v, w, e) in enumerate(draw):
            if it % 500 == 0:
                order = sorted(order, key=lambda k: d[0][k] - lat[k] - c0[k])
            if pairs and u < PAIRS:
                j, k = pairs[int(v * len(pairs))]
                pj, pk = order.index(j), order.index(k)
                if pj > pk:
                    continue
            else:
                pj = int(v * n)
                j = order[pj]
                hop = 1 + int(3.0 * (u * 64.0 % 1.0) ** 2)
                pk = pj
                while hop and pk < n - 1:
                    pk += 1
                    hop -= qi[order[pk]] == qi[j]
                k = order[pk]
                if hop or reach[k] >> j & 1:
                    continue
            seg = order[pj + 1:pk + 1]
            if w < 0.5:
                m = reach[k] | 1 << k
                new = order[:pj] + [x for x in seg if m >> x & 1] + [j] + [x for x in seg if not m >> x & 1] + order[pk + 1:]
            else:
                new = order[:pj] + [x for x in seg if not reach[x] >> j & 1] + [j] + [x for x in seg if reach[x] >> j & 1] + order[pk + 1:]
            s, f = span(new, pj, d)
            if s <= cur - temp * (1.02 - it / moves) * math.log(1.0 - e):
                order, cur, d = new, s, f
                if it > fresh:
                    pairs = held(order, d[0], c0) + held(order, d[1], c1)
                    fresh = it + 12
                if s < best:
                    best, keep = s, order
        return best, keep

    tries = [anneal(order, MOVES // (2 * STARTS), TEMP) for _ in range(STARTS)]
    best, order = anneal(min(tries)[1], MOVES // 2, 0.6 * TEMP)
    _PLAN["span"] = ([x[0] for x in tries], best)
    return order


def _emit(g, T, ops):
    Q = {"v": g.vector, "s": g.scalar, "t": g.tensor, "g": g, "y": g.sync}
    if "deps" not in _PLAN:
        _PLAN["deps"] = _deps(ops)
        _PLAN["order"] = _order(ops, [sorted(set(d + o["soft"])) for d, o in zip(_PLAN["deps"], ops)])
    deps, order = _PLAN["deps"], _PLAN["order"]
    cnt = {"v": 0, "s": 0, "t": 0, "g": 0}
    tok = {}
    for k in order:
        o = ops[k]
        if o["sem"] is not None:
            tok[k] = (o["sem"], o["n"])
        else:
            cnt[o["q"]] += 1
            tok[k] = ("e" + o["q"], cnt[o["q"]])
    known = {q: {} for q in Q}
    clock = {}
    last = {}
    for k in order:
        o = ops[k]
        q = o["q"]
        if q == "x":
            clock[k] = {tok[k][0]: tok[k][1]}
            continue
        want = {}
        src = {}
        for j in deps[k]:
            if q == ops[j]["q"] and (q == "t" or (o["own"] and ops[j]["own"])):
                continue
            s, n = tok[j]
            if n > want.get(s, 0):
                want[s] = n
                src[s] = j
        for s in sorted(want, key=lambda s: -len(clock[src[s]])):
            if known[q].get(s, 0) < want[s]:
                Q[q].wait_ge(T.sem[s], want[s])
                for s2, n2 in clock[src[s]].items():
                    if known[q].get(s2, 0) < n2:
                        known[q][s2] = n2
        ins = o["f"](Q[q])
        c = dict(known[q])
        if not o["own"]:
            ins.then_inc(T.sem[tok[k][0]], 16 if o["sem"] is not None else 1)
        c[tok[k][0]] = tok[k][1]
        last[tok[k][0]] = max(last.get(tok[k][0], 0), tok[k][1])
        clock[k] = c
    for s, n in last.items():
        if max(known[q].get(s, 0) for q in Q) < n:
            g.wait_ge(T.sem[s], n)


def rank_program(g, core, T, topo):
    cores = list(T.cores)
    N = len(cores)
    rank = T.rank_of(core)
    if rank is None:
        for r in range(N):
            src, dst = cores[r], cores[(r + 1) % N]
            if _relay(src, dst, topo) == core:
                rid, pid = topo.addr(dst, core)
                for t, b, lo, hi in MSGS:
                    g.wait_ge(T.sem["arr" + t], len(topo.engines(src, core)))
                    g.remote_dma(T["in" + b][:, lo:hi], T["in" + b][:, lo:hi], T.sem["arr" + t], T.sem.sent, pid, rid,
                                 topo.mask(core, dst))
                g.wait_ge(T.sem.sent, len(MSGS) * len(topo.engines(core, dst)))
        return
    nxt = cores[(rank + 1) % N]
    hop = _relay(core, nxt, topo)
    hop = nxt if hop is None else hop
    rid, pid = topo.addr(hop, core)
    hmask = topo.mask(core, hop)
    nout = len(topo.engines(core, hop))
    prv = cores[(rank - 1) % N]
    back = _relay(prv, core, topo)
    nin = len(topo.engines(prv if back is None else back, core))

    ops = []
    ndma = [0]
    sends = {}
    turn = []
    now = [9, 0]

    def shape(name):
        return SB_[name][0] if name in SB_ else PS_[name]

    def pack(name, real, lo, hi, step, n):
        banks = [(name, b) for b in range(lo // 512, (hi - 1) // 512 + 1)] if name in PS_ else []
        return (real, [(name, lo, hi, step)], banks, n, "p" if name in PS_ else SB_[name][1])

    def ap(name, lo=0, hi=None, step=1):
        if name in ALIAS:
            name, base, w = ALIAS[name]
            lo, hi = base + lo, base + (w if hi is None else hi)
        sh = shape(name)
        hi = int(np.prod(sh)) if hi is None else hi
        if len(sh) == 1:
            real = T[name][:, lo:hi:step] if step > 1 else T[name][:, lo:hi]
        elif lo // sh[1] == (hi - 1) // sh[1]:
            real = T[name][:, lo // sh[1], lo % sh[1]:(hi - 1) % sh[1] + 1:step]
        else:
            real = T[name][:, lo // sh[1]:hi // sh[1], :]
        return pack(name, real, lo, hi, step, len(range(lo, hi, step)))

    def ap3(name, r0, r1, rs, k0, k1, ks=1):
        w = shape(name)[1]
        n = len(range(r0, r1, rs)) * len(range(k0, k1, ks))
        return pack(name, T[name][:, r0:r1:rs, k0:k1:ks], r0 * w + k0, (r1 - 1) * w + k1, 1, n)

    def ind(win, offs):
        return (win[0].indirect(offs[0]), win[1] + offs[1], [], 16 * offs[3], "ind")

    def lst(name, k0=0, k1=None, buf="lu"):
        k1 = dict(LISTS)[name] if k1 is None else k1
        return ap(buf, LOFF[name] + k0, LOFF[name] + k1)

    def col(name):
        k = COLS.index(name)
        return ap("col", k, k + 1)

    def I(v):
        k = SCALES.index(float(v))
        return ap("idm", 128 * k, 128 * k + 128)

    def rec(q, f, outs, ins, sem=None, n=0, own=False, after=(), c=None, lat=0.0, two=False, half=False, open_=False):
        r, w, b = [], [], []
        for a in ins:
            if isinstance(a, tuple):
                r += a[1]
                b += a[2]
        for a in outs:
            w += a[1]
            b += a[2]
        if c is None:
            a = ins[0] if ins else outs[0]
            per = 2.0 if (two and "p" not in (a[4], ins[1][4])) or q == "g" else 1.0
            if half and a[4] in (bf, f16, u16) and outs[0][4] in (bf, f16, u16):
                per = 0.5
            fix = {"v": 50.0, "s": 65.0, "g": 130.0}[q] * (1.0 if a[4] == "ind" or q == "g" else FIX)
            c = [fix + max(64.0, a[3] * (x if a[4] == "ind" else per)) * y for x, y in GC]
        else:
            c = [c * y if q == "t" else c for x, y in GC]
        ops.append({"q": q, "f": f, "r": r, "w": w, "b": b, "sem": sem, "n": n, "own": own, "after": list(after), "c": c, "lat": lat,
                    "open": open_, "soft": [], "turn": tuple(now)})
        return len(ops) - 1

    def raw(a):
        return a[0] if isinstance(a, tuple) else a

    def tt(o, a, b, op):
        return rec("v", lambda e: e.tensor_tensor(o[0], a[0], b[0], op), [o], [a, b], two=True)

    def ts(o, a, s1, op0, s2=None, op1=None):
        if op1 is None:
            return rec("v", lambda e: e.tensor_scalar(o[0], a[0], raw(s1), None, op0), [o], [a, s1], half=True)
        return rec("v", lambda e: e.tensor_scalar(o[0], a[0], raw(s1), raw(s2), op0, op1), [o], [a, s1, s2], half=True)

    def cp(o, a):
        return rec("v", lambda e: e.tensor_copy(o[0], a[0]), [o], [a], half=True)

    def ms(o, c):
        return rec("v", lambda e: e.memset(o[0], c), [o], [], half=True)

    def scan(o, d0, d1):
        return rec("v", lambda e: e.tensor_tensor_scan(o[0], d0[0], d1[0], 0.0, A.mult, A.add), [o], [d0, d1])

    def tr(o, a):
        return rec("v", lambda e: e.transpose(o[0], a[0]), [o], [a])

    def act(o, a, fn=AF.Identity, scale=1.0, bias=0.0):
        return rec("s", lambda e: e.activation(o[0], a[0], fn, bias=raw(bias), scale=raw(scale)), [o], [a, scale, bias])

    def mms(items, start=True, stop=True, each=False):
        banks = [o[2][0] for o, l, r in items]

        def f(e):
            for k, (o, l, r) in enumerate(items):
                ins = e.matmul(o[0], l[0], r[0], each or (start and banks[k] not in banks[:k]), each or (stop and banks[k] not in banks[k + 1:]))
            return ins
        c = sum((max(64, r[3]) * (4 if r[4] == f32 else 1) + MMFIX) * PE for (o, l, r) in items)
        return rec("t", f, [x[0] for x in items], [x[1] for x in items] + [x[2] for x in items], c=c, open_=not (start and stop))

    def iota(o, pat, base, ch=0):
        name = o[1][0][0]
        if SB_[name][1] == i32:
            return rec("g", lambda e: e.iota(o[0], pat, base, ch), [o], [])
        return rec("g", lambda e: e.iota(o[0], pat, base, ch, allow_small_or_imprecise_dtypes=True), [o], [])

    def dma(q, o, a, after=()):
        s = "dm%d" % ndma[0]
        ndma[0] += 1
        return rec(q, lambda e: e.dma_start(o[0], a[0]), [o], [a], sem=s, n=16, after=after, c=100.0,
                   lat=2000.0 + 1.6 * max(o[3], a[3]) * (0.5 if bf in (o[4], a[4]) else 1.0))

    def hbm(t):
        return (t, [], [], 0, "hbm")

    def send(t):
        b, lo, hi = [x[1:] for x in MSGS if x[0] == t][0]
        m = ap("msg" + b, lo, hi)
        sends[t] = rec("g", lambda e: e.remote_dma(T["in" + b][:, lo:hi], m[0], T.sem["arr" + t], T.sem.sent, pid, rid, hmask), [], [m],
                       sem="sent", n=nout * (len(sends) + 1), own=True, c=2300.0 if t == "p" else 300.0,
                       after=list(sends.values())[-1:])

    def arrive(t):
        b, lo, hi = [x[1:] for x in MSGS if x[0] == t][0]
        rec("x", None, [ap("in" + b, lo, hi)], [], sem="arr" + t, n=nin, c=0.0, after=[sends[t]],
            lat=TRIP + (2000.0 if t == "p" else 0.0))

    def mklist(name, k0, k1, family):
        ts(lst(name, k0, k1), lst(name, k0, k1, "lf"), col(family), A.add)

    dma("s", ap("acti"), hbm(T.act[:]))
    d_sd = dma("y", ap("sdi"), hbm(T.sd[:]))
    d_x = dma("y", ap("xw", 0, F), hbm(T.x[:]), after=[d_sd])
    ops[dma("y", ap("xw", 4096, 4096 + F), hbm(T.x[:]), after=[d_sd])]["lat"] += ops[d_x]["lat"] - 2000.0
    ops[-1]["soft"].append(d_sd)
    cp(ap("msg0", 64, 72), ap("acti"))
    ts(ap("msg0", 72, 80), ap("acti"), -1.0, A.mult, 15.0, A.add)
    send("p")

    iota(ap("pi", 0, 1), [[0, 1]], 0, 1)
    for k, (sh, m) in enumerate([(3, 1), (0, 7), (0, 15), (4, 1), (0, 3), (2, 3)]):
        ts(ap("ibits", k, k + 1), ap("pi", 0, 1), sh, A.logical_shift_right, m, A.bitwise_and)
        cp(ap("col", k, k + 1), ap("ibits", k, k + 1)) if k >= 4 else None
    cp(ap("col", 0, 4), ap("ibits", 0, 4))
    for n, s, sc_, b in [("sgb", "ib", -2.0, 1.0), ("ib15", "ib", 15.0, 0.0), ("il1920", "il", 128.0, 1920.0), ("sw", "ib", -16.0, 8.0),
                         ("i15", "i", -1.0, 15.0), ("gb64", "gb", 64.0, 0.0), ("ngb64", "gb", -64.0, 64.0), ("xp", "il", 8.0, col("ib")),
                         ("yz", "ib", 16.0, col("il")), ("ls", "ib", 8.0, 7.0), ("cb", "i3", 8.0, 7.0), ("nat", "i3", 8.0, col("i2"))]:
        act(col(n), col(s), scale=sc_, bias=b)
    iota(ap("dd"), [[1, 144]], 0, -1)
    iota(ap("su"), [[0, 2], [1, 8], [0, 4]], 0)
    iota(ap("tf2"), [[4, 2], [0, 8], [1, 4]], 0)
    act(ap("qt"), ap("su"), scale=col("sgb"), bias=col("ib15"))
    ts(ap("ti"), ap("qt"), -128.0, A.mult, col("il1920"), A.add)
    act(ap("tf"), ap("qt"), scale=8.0)
    ts(ap("ti2"), ap("ti"), 896, A.bitwise_and)
    tt(ap("tf"), ap("tf"), ap("tf2"), A.add)
    tt(lst("ROT", buf="lf"), ap("tf"), ap("ti2"), A.add)
    cp(lst("ROT"), lst("ROT", buf="lf"))
    for c in range(2):
        iota(lst("G0" + "ab"[c], 0, 4, "lf"), [[0, 2], [2, 2]], 4 * c)
        iota(lst("G0" + "ab"[c], 4, 6, "lf"), [[2, 2]], 8 + 4 * c)
    iota(lst("G1", 0, 4, "lf"), [[0, 2], [2, 2]], 0)
    iota(lst("G1", 4, 6, "lf"), [[2, 2]], 4)
    mklist("G0a", 0, 18, "ib")
    iota(lst("YZ", buf="lf"), [[8, 2], [32, 2]], 0)
    mklist("YZ", 0, 4, "yz")
    ts(I(1), ap("dd", 0, 128), 0.0, A.is_equal)
    for gp, e, d, cn in [(0, 0, 0.0, "ngb64"), (0, 1, 16.0, "ngb64"), (1, 0, -16.0, "gb64"), (1, 1, 0.0, "gb64")]:
        ts(ap("m%d%d" % (gp, e)), ap("dd", 0, 128), d, A.is_equal, col(cn), A.mult)
    iota(ap("cwl"), [[16, 4]], 0)
    for c in range(2):
        iota(lst("XP", 36 * c, 36 * c + 8, "lf"), [[0, 2], [64, 2], [2, 2]], 896 + 4 * c)
        iota(lst("XP", 36 * c + 8, 36 * c + 36, "lf"), [[128, 7], [64, 2], [2, 2]], 4 * c)
    mklist("XP", 0, 72, "xp")
    iota(ap("cG", 0, 64), [[8, 2], [0, 4], [1, 8]], 0)
    iota(ap("cG", 64, 96), [[0, 4], [-1, 8]], 16)
    ms(ap("k4"), 1.0)
    iota(ap("zero"), [[0, 128]], 0)
    for v in SCALES[1:]:
        if v <= -2.0 * K2 * max(max(SQ), 3) and v > -65536.0:
            continue
        if v in LATE:
            rec("g", lambda e, v=v: e.affine_select(I(v)[0], T["zero"][:], [[-1, 128]], A.not_equal, v, 0, 1), [I(v)], [ap("zero")])
        elif v in ON_V:
            ts(I(v), I(1), v, A.mult)
        else:
            act(I(v), I(1), scale=v)
    iota(ap("kn", 0, 192), [[0, 192]], K2)
    iota(ap("kn", 64, 128), [[0, 64]], K2 + C0)
    iota(ap("kn", 192, 256), [[0, 64]], C0 + 32)
    act(ap("if32"), I(1))
    act(ap("nf32"), I(1), scale=-1.0)
    ts(ap("psw"), ap("dd", 0, 128), col("sw"), A.is_equal)
    ts(ap("bm"), ap("dd"), col("i15"), A.is_equal)
    ts(ap("bm3"), ap("dd"), col("i15"), A.is_equal, 3.0, A.mult)
    ms(ap("xw", F, 4096), 2.0 ** 61)
    ms(ap("xw", 4096 + F, XW), 2.0 ** 61)
    iota(lst("DUP", buf="lf"), [[0, 3], [16, 2]], 0)
    mklist("DUP", 0, 6, "i")
    iota(lst("OM", buf="lf"), [[0, 10], [2, 2]], 0)
    iota(lst("OM", 4, 6, "lf"), [[2, 2]], 4)
    iota(lst("WV", buf="lf"), [[2, 2]], 8)
    mklist("OM", 0, 22, "ib")
    cp(lst("G1", 6, 7), col("i3"))
    iota(lst("LS", buf="lf"), [[16, 14]], 0)
    mklist("LS", 0, 14, "ls")
    cp(lst("CB", 0, 2), lst("LS", 0, 2))
    cp(lst("CB", 2, 3), col("cb"))
    iota(ap("clp", 0, 8), [[15, 2], [0, 4]], 0)
    iota(ap("clp", 8, 16), [[-30, 2], [0, 4]], 15)
    iota(lst("NAT", buf="lf"), [[0, 2], [4, 2]], 0)
    iota(lst("NATH", buf="lf"), [[-32, 2], [4, 2]], 32)
    ts(ap("lu", LOFF["NAT"], LTOT), ap("lf", LOFF["NAT"], LTOT), col("nat"), A.add)
    iota(ap("cpw"), [[0, 20], [1, 8]], 0)
    iota(ap("cpw", 32, 64), [[0, 4], [-1, 8]], 15)
    iota(ap("cpw", 128, 160), [[0, 4], [-1, 8]], 15)
    iota(ap("cL"), [[0, 28], [E16, 8]], -2 * E16)
    iota(ap("cL", 64, 96), [[0, 4], [E16, 8]], 2 * E16)
    iota(ap("cL", 71, 96, 8), [[0, 4]], E16)
    iota(ap("cL", 160, 224), [[0, 64]], -C0)
    iota(ap("cpos"), [[0, 28], [E16, 8]], E16)
    iota(ap("cpos", 160, 224), [[0, 64]], 0)
    rec("g", lambda e: e.affine_select(T["rst8"][:], T["k4"][:, 0:224], [[0, 28], [1, 8]], A.is_gt, 0.0, 0, 0), [ap("rst8")], [ap("k4", 0, 224)])
    for s in range(max(SQ)):
        iota(ap("cq", 64 * s, 64 * s + 64), [[0, 64]], s * s)
    cpit = ap("cG", 0, 64)
    ones = lambda n: ap("k4", 0, n)
    xw = ap("xw")

    def halves(o, lo, l, r):
        return [(ap(o, lo + 32 * h, lo + 32 * h + 32), l, r) for h in range(2)]

    def wl_offsets(c, src, lo):
        M = "U" + c
        mms([(ap(M, 600, 604), I(1), ap("cwl"))]
            + [(ap(M, 600 + gp, 604, 2), ap("m%d%d" % (gp, e)), ap(src, lo + e, lo + 4, 2)) for gp in range(2) for e in range(2)])
        ts(ap("oft" + c), ap(M, 600, 604), col("i"), A.add)

    for ci, c in enumerate("ab"):
        G0 = "G0" + c
        pown = ap("msg0", 64, 80)
        act(ap("S1", 512 * ci, 512 * ci + 512), ind(ap("sdi"), lst("ROT", 32 * ci, 32 * ci + 32)))
        tt(ap("uu" + c), ap("msg0", 64 + 4 * ci, 68 + 4 * ci), ap("msg0", 72 + 4 * ci, 76 + 4 * ci), A.min)
        ts(ap("zm" + c), ind(pown, lst(G0, 2, 6)), 8.0, A.is_ge, float(F), A.mult)
        wl_offsets(c, "uu" + c, 0)
        tr(ap("TT", 1024 * ci, 1024 * ci + 512), ap("S1", 512 * ci, 512 * ci + 512))
        cp(ap("xg" + c), ind(ap("TT", 1024 * ci, 1024 * ci + 512), ap("oft" + c)))
        tr(ap("y0" + c), ap("xg" + c))
        tt(ap("ym" + c), ind(ap("y0" + c), lst("YZ")), ap("zm" + c), A.max)
        tt(ap("msg0", 32 * ci, 32 * ci + 32), ap("ym" + c, 0, 32), ap("ym" + c, 32, 64), A.min)
        send("0" + c)
    for ci, c in enumerate("ab"):
        X, U, R, G0 = "X" + c, "U" + c, "R" + c, "G0" + c
        pown = ap("msg0", 64, 80)
        act(ap("Xf" + c), ind(ap("sdi"), lst("XP", 36 * ci, 36 * ci + 36)), bias=-float(C0))
        tt(ap("eq" + c), ind(pown, lst(G0, 0, 4)), cpit, A.is_equal)
        act(ap("sk" + c, 0, 64), ap("eq" + c), scale=2.0, bias=-1.0)
        mms([(ap(U, 64 * s, 64 * s + 64), I(C0), ap("sk" + c, 0, 64)) for s in range(9)], each=True)
        tt(ap(X), ap(U, 0, 576), ap("Xf" + c), A.max)
        ts(ap("val" + c), ap(X), C0 - 0.5, A.is_lt)
        mms([(ap(R, 0, 64), I(-1), ap("val" + c, 64 * s, 64 * s + 64)) for s in range(9) if s != 1])
        ts(ap(X, 64, 128), ap(R, 0, 64), float(C0), A.add)
        mms([(ap("pd", 512 * ci + 64 * (7 - u), 512 * ci + 64 * (8 - u)), ap("psw"), ap("TT", 1024 * ci + 64 * u, 1024 * ci + 64 * u + 64))
             for u in range(8)], each=True)
        act(ap("TT", 1024 * ci + 512, 1024 * ci + 1024), ap("pd", 512 * ci, 512 * ci + 512))
        act(ap("pb" + c, 160, 224), ind(pown, lst(G0, 2, 6)))
        iota(ap("pb" + c, 288, 304), [[0, 16]], 0)
        for r in (0, 3, 4):
            iota(ap("cand" + c, 48 * r + 32, 48 * r + 48), [[0, 16]], 0)

    def sow(t, ci):
        c = "ab"[ci]
        last = t == 2
        now[:] = [2 * t + ci, 0]
        X, U, R, M, pb = "X" + c, "U" + c, "R" + c, "U" + c, "pb" + c
        m = "in%d" % t
        s0 = (32 if t == 0 else 48) * ci
        p0 = 64 + 4 * ci if t == 0 else s0 + 32
        seeds = ap(m, s0, s0 + 32)
        ach, ob, cap, pr = "ach%d" % min(t, 1) + c, "ob%d" % (t & 1) + c, "cap%d" % min(t, 1) + c, "pr%d" % t + c
        hi = ap("hv" + c, 0, 32)
        cand, cmp_, sig = "cand" + c, "cmp" + c, "sig" + c
        e8, cnt, cc = ap(ob, 0, 32), ap(ob, 32, 64), ap(pr, 0, 32)
        om = lambda lo, hi_: ap(ob, 64 + lo, 64 + hi_)
        mms([(ap(U, 0, 256), I(1), ap3(X, 3, 18, 2, 0, 32)), (ap(U, 0, 256), I(-4096), ones(256))], stop=False)
        if t == 0 and ci == 0:
            arrive("p")
        arrive("%d%s" % (t, c))
        pw_ = ap(m, 64, 80) if t == 0 else ap(m, p0, p0 + 8)
        tt(ap("G" + c), ind(pw_, lst("G0" + c if t == 0 else "G1", 0, 6)), ap("cG"), A.is_ge)
        tt(ap("hv" + c), ap("G" + c, 0, 64), ap("G" + c, 32, 96), A.not_equal)
        mms([(ap(U, 32 * k, 32 * k + 32), I(8192), hi) for k in range(8)], start=False)
        ts(ap("offa" + c), seeds, float(F), A.min)
        act(ap("fa" + c), ind(ap("xw", 0, F + 16), ap("offa" + c)))
        tt(ap("W" + c), ap(U, 0, 256), ap3(X, 2, 18, 2, 0, 32), A.max)
        ts(ap("off" + c), ap("W" + c, 32, 256), float(C0), A.add)
        ts(ap(ach), ind(seeds, lst("DUP", 0, 4)), -float(C0), A.add)
        act(ap("nh" + c), ind(seeds, lst("DUP", 0, 4)), AF.Sign, bias=0.5 - F)
        lsum = [(ap("if32"), ap(m, p0, p0 + 4))] + [(I(-0.5), ap("nh" + c, k, 32, 8)) for k in range(8)]
        mms([(ap(M, 576, 580), l, r) for l, r in lsum])
        act(ap("sl" + c, 0, 4), ap(M, 576, 580), AF.Sign, bias=-11.5)
        act(ap("sl" + c, 4, 8), ap(M, 576, 580))
        mms([(ap(M, 580, 584), I(1), ap("sl" + c, 4, 8)), (ap(M, 580, 584), I(-8), ap("sl" + c, 0, 4))])
        act(ap(pb, 288, 292), ap(M, 580, 584), bias=-4.0)
        if not last:
            wl_offsets(c, pb, 288)
            mms([(ap(M, 584, 600), I(1), ap("clp"))]
                + [(ap(M, 584 + 4 * k, 588 + 4 * k), I(v), ap(pb, 288, 292)) for k, v in enumerate((1, -1, -2, 2))])
            act(ap3(cand, 0, 4, 3, 32, 40), ap(M, 584, 600))
            act(ap("xg" + c), ind(ap("TT", 1024 * ci, 1024 * ci + 1024), ap("oft" + c)))
            tr(ap("yb" + c), ap("xg" + c))
        else:
            act(ap(pb, 296, 300), ap(M, 580, 584), scale=-2.0, bias=23.0)
        signs, p0_, c0_ = [((8, 8, -8), 64, 64), ((8, -8), 0, 0), ((8,), 0, 0)][t]
        npw = 32 * len(signs)
        mms([(ap(R, 224, 224 + npw), I(1), ap("cpw", c0_, c0_ + npw))]
            + [(ap(R, 224 + 32 * k, 256 + 32 * k), I(v), hi) for k, v in enumerate(signs)])
        act(ap(pb, p0_, p0_ + npw), ap(R, 224, 224 + npw))
        mms([(ap(R, 352, 384), ap("nf32"), ap("W" + c, 0, 32)), (ap(R, 352, 384), I(4096), hi)])
        act(cnt, ap(R, 352, 384), bias=float(C0))
        act(e8, ap(R, 352, 384), AF.Relu, bias=float(C0 - 7))
        if not last:
            mms([(ap(R, 320, 352), I(1), cnt), (ap(R, 320, 352), I(1), ap("cpw", 0, 32))])
            act(ap("st" + c), ap(R, 320, 352), AF.Sign, bias=-6.5)
        lw_ = ap(pb, 288, 304)
        if t == 0:
            tt(om(0, 128), ind(lw_, lst("OM", 6, 14)), ap(pb, 96, 224), A.is_equal)
        elif t == 1:
            tt(om(0, 288), ind(lw_, lst("OM", 0, 18)), ap(pb, 0, 288), A.is_equal)
        else:
            tt(om(32, 64), ind(lw_, lst("OM", 0, 2)), ap(pb, 0, 32), A.is_equal)

        def v_list(s):
            k = tt(ap(cmp_, 512 * s, 512 * s + 512), ind(xw, ap("off" + c, 32 * s, 32 * s + 32)), ap("fa" + c), A.is_lt)
            ops[k]["soft"] += turn[-LAG:][:1]
            turn.append(k)

        def s_list(s, k):
            act(ap("gb%d" % k), ind(xw, ap("off" + c, 32 * s, 32 * s + 32)))
            mms([(ap("pd", 512 * k, 512 * k + 512), I(1), ap("fa" + c)), (ap("pd", 512 * k, 512 * k + 512), I(-1), ap("gb%d" % k))])
            act(ap(cmp_, 512 * s, 512 * s + 512), ap("pd", 512 * k, 512 * k + 512), AF.Sign, bias=-2.0 ** -70)

        def rows(lo, s, n, b):
            mms([(ap(R, lo, lo + 32 * n), ap(b, 15 - i, 143 - i), ap(cmp_, 512 * s + i, 512 * (s + n), 16)) for i in range(16)])

        def place(slots, at):
            nq = SQ[t]
            q = []
            for s in slots:
                src = "cq" if s < nq else "val" + c
                if q and q[-1][0] == src and at(s) == at(s - 1) + 64 and at(s) % 512:
                    q[-1][2] = s + 1
                else:
                    q.append([src, s, s + 1])
            q = [(ap(U, at(a), at(b - 1) + 64), I(K2), ap(src, 64 * a, 64 * b)) for src, a, b in q]
            for s in slots:
                o = ap(U, at(s), at(s) + 64)
                q += [(o, I(1), ap(ach))]
                if s < nq:
                    q += [(o, I(K2), ap("ps" + c, 64, 128))] + ([(o, I(-2 * K2 * s), ap("ps" + c, 0, 64))] if s else [])
            return q

        now[1] = 0 if last else 0.5
        mms([(ap(R, 416, 480), I(-1), ap(X, 64, 128)), (ap(R, 416, 480), I(16), ap("hv" + c))])
        act(ap("ps" + c, 0, 64), ap(R, 416, 480), bias=float(C0))
        if SQ[t]:
            act(ap("ps" + c, 64, 128), ap(R, 416, 480), AF.Square, bias=float(C0))
        for s in range(SQ[t], 8):
            act(ap("val" + c, 64 * s, 64 * s + 64), ap("ps" + c, 0, 64), AF.Abs, bias=-float(s))
        if not last:
            N_ = ap(U, 0, 64)
            mms(place(range(7), lambda s: 64 * s + 64)
                + [(N_, I(-1), ap("ps" + c, 0, 64)), (N_, I(80), ap("hv" + c)), (N_, I(33), ap("nh" + c)), (N_, I(1), ap("kn", 192, 256))])
            tt(ap(X, 64, 576), ap(U, 0, 512), ap(X, 64, 576), A.min)
        now[1] = 0

        if not last:
            nl = 96 if t == 0 else 224
            L0 = 608
            lay = [(ap(M, L0, L0 + nl), I(1), ap("cL", 0, nl)), (ap(M, L0, L0 + 64), I(1), ap(ach)),
                   (ap(M, L0 + 64, L0 + 96), I(1), ap(ach, 0, 32)), (ap(M, L0, L0 + 64), I(BIG), om(0, 64)),
                   (ap(M, L0 + 64, L0 + 96), I(BIG), om(32, 64))]
            lay += halves(M, L0, I(E16), cnt) + halves(M, L0, I(-65536), ap("st" + c))
            if t == 1:
                lay += [(ap(M, L0 + 96, L0 + 160), I(1), ap("ach0" + c)), (ap(M, L0 + 96, L0 + 160), I(BIG), om(96, 160)),
                        (ap(M, L0 + 160, L0 + 224), I(BIG), om(96, 160))]
                lay += halves(M, L0 + 96, I(E16), ap("ob0" + c, 32, 64)) + halves(M, L0 + 96, I(-E16), ap("pr0" + c, 0, 32))
                lay += halves(M, L0 + 96, I(-65536), ap("st0" + c)) + halves(M, L0 + 96, I(-BIG), om(64, 96))
                lay += halves(M, L0 + 160, I(F), ap("cap0" + c))
            mms(lay)
            act(ap("ly" + c, 0, nl), ap(M, L0, L0 + nl), AF.Relu, bias=float(C0 - BIG))
            scan(ap("cs" + c, 0, nl), ap("rst8", 0, nl), ap("ly" + c, 0, nl))
            tt(ap("sb" + c, 0, nl), ind(ap("cs" + c, 0, nl), lst("LS", 0, nl // 16)), ap("cpos", 0, nl), A.subtract)
            act(ap("ea" + c, 0, nl), ap("sb" + c, 0, nl), AF.Abs)
            kill = [(ap(M, L0, L0 + 64), I(F), om(64, 128) if t == 0 else om(160, 224))]
            if t == 1:
                kill += [(ap(M, L0, L0 + 64), I(F), om(224, 288)), (ap(M, L0, L0 + 64), ap("if32"), ap("ea" + c, 160, 224))]
            mms(kill + [(ap(M, L0 + 32 * z, L0 + 32 * z + 32), ap("if32"), ap3("yb" + c, 0, 4, 1, 8 * z, 8 * z + 8)) for z in range(2)]
                + [(ap(M, L0 + 64, L0 + 96), I(F), ones(32))])
        else:
            mms(place(range(8), lambda s: (64 * s + 128) % 576) + [(ap(U, 64, 128), I(1), ones(64))])
            tt(ap(X), ap(U, 0, 576), ap(X), A.min)
            nat = [(ap(U, 0, 512), I(C0), ones(512))]
            nat += [(ap3(U, 0, 14, 1, 4 * k, 4 * k + 4), I(1), ap3(X, 4, 18, 1, k, 32, 8)) for k in range(8)]
            nat += [(ap3(U, 14, 16, 1, 4 * k, 4 * k + 4), I(1), ap3(X, 0, 2, 1, k, 32, 8)) for k in range(8)]
            mms(nat, stop=False)
            act(ap("hmn" + c), ind(ap("hv" + c), lst("NATH")), scale=float(F))
            act(ap("aq" + c), ind(seeds, lst("NAT")), bias=float(F))
            tt(om(0, 32), ind(lw_, lst("WV")), om(32, 64), A.mult)
        ns = ON_S[t, ci]
        nv = 7 - ns
        v_list(0)
        s_list(nv, 0)
        v_list(1)
        if not last:
            tt(ap3(cand, 0, 3, 1, 0, 32), ap(M, L0, L0 + 96), ap("ea" + c, 0, 96), A.min)
            if t == 1:
                tt(ap3(cand, 0, 2, 1, 0, 32), ap3(cand, 0, 2, 1, 0, 32), ap("ea" + c, 96, 160), A.min)
            if ED[t]:
                mms([(ap(M, 864, 928), ap("if32"), ap3(cand, 1, 3, 1, 0, 32)), (ap(M, 864, 928), ap("nf32"), ap3(cand, 0, 2, 1, 0, 32))])
                act(ap3(cand, 3, 5, 1, 0, 32), ap(M, 864, 928))
            else:
                tt(ap3(cand, 3, 5, 1, 0, 32), ap3(cand, 1, 3, 1, 0, 32), ap3(cand, 0, 2, 1, 0, 32), A.subtract)
        for k in range(1, ns):
            s_list(nv + k, k & 1)
        for s in range(2, nv - 2):
            v_list(s)
        rows(0, 0, nv - 2, "bm")
        rows(32 * (nv - 2), nv, ns, "bm3")
        act(ap(sig, 0, 160), ap(R, 0, 160), AF.Sign, bias=-9.5)
        Y = ap(M, 832, 864)
        mms([(Y, I(-1), cnt), (Y, I(33), e8), (Y, I(-33), ap("nh" + c, 0, 32))]
            + [(Y, I(1), ap(sig, 32 * k, 32 * k + 32)) for k in range(5)], stop=False)
        v_list(nv - 2)
        v_list(nv - 1)
        rows(160, nv - 2, 2, "bm")
        act(ap(sig, 160, 224), ap(R, 160, 224), AF.Sign, bias=-9.5)
        mms([(Y, I(1), ap(sig, 32 * k, 32 * k + 32)) for k in (5, 6)], start=False)
        ts(ap(cap), Y, 26.5, A.is_gt)
        if not last:
            mo = "msg%d" % (t + 1)
            o0 = 48 * ci
            tt(ap(pr), ind(ap(cap), lst("DUP")), ap(ob, 32, 128), A.mult)
            scan(ap("cs2" + c), ap("rst8", 0, 64), ap(pr, 32, 96))
            tt(ap("r1" + c), ind(ap("cs2" + c, 32, 64), lst("CB", 0, 3)), ap(cand, 192, 240), A.mult)
            tt(ap("r2" + c), ap("r1" + c), ap(cand, 144, 192), A.add)
            tt(ap("r1" + c), ind(ap("cs2" + c, 0, 32), lst("CB", 0, 3)), ap("r2" + c), A.mult)
            tt(ap(mo, o0, o0 + 40), ap("r1" + c, 0, 40), ap(cand, 0, 40), A.add)
            send("%d%s" % (t + 1, c))
            now[1] = 1
            pnew = ap(mo, o0 + 32, o0 + 40)
            tt(ap("eq" + c), ind(pnew, lst("G1", 0, 4)), cpit, A.is_equal)
            mms([(ap(R, 352 + 64 * k, 416 + 64 * k), l, r) for k in range(2) for l, r in ((I(-1), ap("hv" + c)), (I(2 - 3 * k), ap("eq" + c)))]
                + halves(R, 352, I(1), ap(cap)) + halves(R, 416, I(1), ap(cap)))
            act(ap("sk" + c), ap(R, 352, 480), AF.Sign, bias=-0.5)
            mms([(ap(U, 64 * s, 64 * s + 64), I(C0), ap("sk" + c, 0, 64)) for s in range(9)], each=True)
            tt(ap(X), ap(U, 0, 576), ap(X), A.max)
            sm = ap("sk" + c, 64, 128)
            mms([(ap(U, 0, 192), I(1), ap("kn", 0, 192))] + place([7], lambda s: 0)
                + [(ap(U, 0, 64), I(K2), ap("sk" + c, 0, 64)), (ap(U, 64, 128), I(-K2), sm), (ap(U, 128, 192), I(-K2), sm),
                   (ap(U, 64, 128), I(1), ap("nh" + c)), (ap(U, 128, 192), I(1), ap(ach))])
            tt(ap(X, 0, 192), ap(U, 0, 192), ap(X, 0, 192), A.min)
            if t == 0:
                act(ap(pb, 224, 304), ind(pnew, lst("G1", 2, 7)))
                mms([(ap(R, 480, 512), I(1), cnt), (ap(R, 480, 512), I(-1), cc), (ap(R, 480, 512), I(1), ap("cpw", 0, 32))])
                act(ap("st0" + c), ap(R, 480, 512), AF.Sign, bias=-6.5)
            else:
                mms([(ap(R, 480, 484), I(1), ap("pr%d" % r + c, k, 32, 8)) for r in range(2) for k in range(8)])
                act(ap("sc" + c), ap(R, 480, 484))
        else:
            tt(ap("kmn" + c), ind(ap(cap), lst("NAT")), ap("hmn" + c), A.mult)
            mms([(ap(U, 64 * s, 64 * s + 64), I(1), ap("kmn" + c)) for s in range(8)], start=False)
            if JY[ci]:
                act(ap("Rf" + c), ap(U, 0, 512), AF.Relu, scale=-1.0, bias=float(F))
                act(ap3("yo", 0, 128, 1, 4 * ci, 4 * ci + 4), ap("Rf" + c), scale=-1.0, bias=float(F))
            else:
                ts(ap3("yo", 0, 128, 1, 4 * ci, 4 * ci + 4), ap(U, 0, 512), float(F), A.min)
            tt(ap("rr" + c), ap("aq" + c), ap("kmn" + c), A.subtract)
            tt(ap3("yo", 0, 16, 1, 4 * ci, 4 * ci + 4), ap3("yo", 0, 16, 1, 4 * ci, 4 * ci + 4), ap("rr" + c), A.min)
            tt(ap(pr), ind(ap(cap), lst("DUP", 0, 4)), ap(ob, 32, 96), A.mult)
            mms([(ap(R, 256, 264), I(1), ap(pr, k, 64, 8)) for k in range(8)]
                + [(ap(R, 256, 260), I(1), ap("sc" + c)), (ap(R, 260, 264), I(1), ap(pb, 288, 292))])
            act(ap3("o8", 0, 2, 1, 4 * ci, 4 * ci + 4), ap(R, 256, 264))

    for t in range(3):
        for ci in range(2):
            sow(t, ci)
    dma("y", hbm(T.ys[:, 512:1024]), ap("yo", 512, 1024))
    dma("s", hbm(T.ys[:, 0:512]), ap("yo", 0, 512))
    dma("s", hbm(T.yp[:]), ap("o8", 8, 16))
    dma("y", hbm(T.yc[:]), ap("o8", 0, 8))
    _emit(g, T, ops)
